import numpy as np
import ml_dtypes


def mxq(x, axis, fmt="e4m3"):
    dtype, down = {"e4m3": (ml_dtypes.float8_e4m3fn, 7), "e5m2": (ml_dtypes.float8_e5m2, 14)}[fmt]
    v = np.moveaxis(np.asarray(x, np.float32).astype(ml_dtypes.bfloat16).astype(np.float64), axis, -1)
    blocks = v.reshape(v.shape[:-1] + (-1, 32))
    amax = np.abs(blocks).max(-1, keepdims=True)
    byte = np.maximum(np.where(amax > 0, np.frexp(amax)[1] - 1 + 127, 0) - down, 1)
    scale = np.exp2(byte - 127.0)
    codes = (blocks / scale).astype(np.float32).astype(dtype).astype(np.float64)
    return np.moveaxis((codes * scale).reshape(v.shape), -1, axis)


WIDE = False


def mx_kscale(k):
    if not WIDE:
        return np.ones(k)
    levels = np.array([10, -10, 5, -5, 0])
    if k % 512:
        return np.exp2(np.random.permutation(np.resize(levels, k // 32))).repeat(32)
    a = np.empty((k // 512, 16))
    for p in range(k // 512):
        a[p, :8] = np.random.permutation(np.resize(levels, 8))
        for g in range(8):
            far = levels[np.abs(levels - a[p, g]) >= 10]
            a[p, g + 8] = far[np.random.randint(len(far))]
    return np.exp2(a.ravel()).repeat(32)


BF16 = ml_dtypes.bfloat16


def bf(x):
    return np.asarray(x, np.float32).astype(BF16)


def f64(x):
    return np.asarray(x).astype(np.float64)


E2M1 = np.array([0.0, 0.5, 1.0, 1.5, 2.0, 3.0, 4.0, 6.0, -0.0, -0.5, -1.0, -1.5, -2.0, -3.0, -4.0, -6.0])


def pack_weight(w, fmt):
    k, n = w.shape
    w = f64(bf(w)).reshape(k // 32, 32, n)
    amax = np.abs(w).max(1)
    if fmt == "e4m3":
        byte = np.frexp(amax)[1] - 1 + 127 - 7
    else:
        mant, ex = np.frexp(amax / 6.0)
        byte = np.where(mant > 0.5, ex, ex - 1) + 127
    byte = np.clip(np.where(amax > 0, byte, 1), 1, 254)
    scaled = (w * np.exp2(127.0 - byte)[:, None, :]).reshape(k, n).astype(np.float32)
    by_word = np.ascontiguousarray(scaled.reshape(k // 512, 128, 4, n).transpose(0, 1, 3, 2))
    if fmt == "e4m3":
        words = by_word.astype(ml_dtypes.float8_e4m3fn).view(np.uint8)
    else:
        c = by_word.astype(ml_dtypes.float4_e2m1fn).view(np.uint8) & 0xF
        words = c[..., 0::2] | (c[..., 1::2] << 4)
    return np.ascontiguousarray(words), np.ascontiguousarray(byte.astype(np.uint8).reshape(k // 512, 16, n))


def unpack_weight(words, scales, fmt):
    g, p, n, _ = words.shape
    if fmt == "e4m3":
        vals = np.ascontiguousarray(words).view(ml_dtypes.float8_e4m3fn).astype(np.float64)
    else:
        nib = np.empty((g, p, n, 4), np.uint8)
        nib[..., 0::2] = words & 0xF
        nib[..., 1::2] = words >> 4
        vals = E2M1[nib]
    vals = vals * np.repeat(np.exp2(scales.astype(np.float64) - 127.0), 8, axis=1)[..., None]
    return vals.transpose(0, 1, 3, 2).reshape(g * 512, n)
def pack4(w):
    words, scales = pack_weight(w, "e2m1")
    return words.reshape(words.shape[0], 128, -1), scales


def unpack4(words, scales):
    return unpack_weight(words.reshape(words.shape[0], 128, -1, 2), scales, "e2m1")


M, N, D, R = 1536, 1024, 2048, 512

SPREAD = 0.6
COEF = 1.0


def draw0():
    s = mx_kscale(D)
    t = mx_kscale(M)
    gen = bf(np.random.standard_normal((M, D)) * SPREAD / D ** 0.25 * s)
    real = bf(np.random.standard_normal((N, D)) * SPREAD / D ** 0.25 / s)
    imp = bf((1 + 0.1 * np.random.standard_normal(M)) * t)
    mult_words, mult_scales = pack4(np.random.standard_normal((M, R)) / np.sqrt(M) / t[:, None])
    return {"gen": gen, "real": real, "imp": imp,
            "mult_words": mult_words, "mult_scales": mult_scales}


def core(gen, real, imp, mult_words, mult_scales):
    dots = mxq(f64(gen), 1, "e4m3") @ mxq(f64(real), 1, "e4m3").T
    v = dots + COEF
    ker = v * v * v * f64(imp)[:, None]
    mult = unpack4(mult_words, mult_scales)
    return mult.T @ mxq(ker, 0, "e4m3")


def e4m3fn_bytes(y):
    return np.clip(np.asarray(y, np.float64), -448.0, 448.0).astype(np.float32).astype(ml_dtypes.float8_e4m3fn).view(np.uint8)


def e4m3fn_values(b):
    return np.asarray(b, np.uint8).view(ml_dtypes.float8_e4m3fn).astype(np.float64)


def setup_inputs():
    d = draw0()
    x0 = np.asarray(d['gen']).astype(np.float64)
    s = (np.max(np.abs(x0), axis=(0,), keepdims=True) / 448.0).astype(np.float32)
    out = {}
    for k, v in d.items():
        if k == 'gen':
            out['gen_bytes'] = e4m3fn_bytes(x0 / s.astype(np.float64))
            out['gen_scale'] = s
        else:
            out[k] = v
    return out


def reference(gen_bytes, gen_scale, real, imp, mult_words, mult_scales):
    return core(e4m3fn_values(gen_bytes) * gen_scale.astype(np.float64), real, imp, mult_words, mult_scales)

@@ -1,0 +1,261 @@
+from contextlib import ExitStack
+
+import concourse.mybir as mybir
+from concourse.masks import make_identity
+
+M, N, D, R = 1536, 1024, 2048, 512
+FLOPS = 2 * M * N * D + 2 * M * R * N
+
+F32 = mybir.dt.float32
+BF16 = mybir.dt.bfloat16
+I32 = mybir.dt.int32
+U32 = mybir.dt.uint32
+U8 = mybir.dt.uint8
+FP8 = mybir.dt.float8_e4m3fn
+FP8X4 = mybir.dt.float8_e4m3fn_x4
+FP4X4 = mybir.dt.float4_e2m1fn_x4
+MULT = mybir.AluOpType.mult
+SQUARE = mybir.ActivationFunctionType.Square
+IDENTITY = mybir.ActivationFunctionType.Identity
+
+P = 128
+PACK = 4
+G = D // (P * PACK)
+C = M // (P * PACK)
+H = 2
+HN = N // H
+JT = HN // P
+KT = C * PACK
+B = R // P
+WARM = 12
+LATE = 5
+
+
+def tile_kid_bootstrap_witness_s13_kernel(tc, gen_bytes, gen_scale, real, imp, mult_words, mult_scales, out):
+    nc = tc.nc
+    with ExitStack() as ctx:
+        keep = ctx.enter_context(tc.tile_pool(name="keep", bufs=1))
+        work = ctx.enter_context(tc.tile_pool(name="work", bufs=1))
+        psum = ctx.enter_context(tc.psum_pool(name="psum", bufs=8))
+        ctx.enter_context(tc.manual_schedule())
+
+        ident = keep.tile([P, P], F32, name="ident")
+        make_identity(nc, ident[:])
+        scale_row = keep.tile([P, D], F32, name="scale_row")
+        scale_cols = keep.tile([P, G, PACK], F32, name="scale_cols")
+        warm = keep.tile([P, 512], BF16, name="warm")
+        nc.vector.memset(warm[:], 0.0)
+        wwords = keep.tile([P, C, 2 * R], U8, name="wwords", align_bytes=64)
+        wscales = keep.tile([P, C, R], U8, name="wscales", align_bytes=64)
+        imp_raw = keep.tile([P, C, PACK], BF16, name="imp_raw")
+        imp32 = keep.tile([P, KT], F32, name="imp32")
+        rcodes = keep.tile([P, H, G, HN], U32, name="rcodes", align_bytes=64)
+        rscales = keep.tile([P, H, G, HN], U8, name="rscales", align_bytes=64)
+
+        nc.gpsimd.memset(wscales[:].rearrange("p c n -> p (c n)").bitcast(I32), 0)
+        nc.gpsimd.dma_start(out=imp_raw[:], in_=imp.rearrange("(c p t) -> p c t", p=P, t=PACK))
+        nc.gpsimd.tensor_copy(out=imp32[:], in_=imp_raw[:].rearrange("p c t -> p (c t)"))
+
+        gen_rows = gen_bytes.rearrange("(c p t) k -> c p t k", p=P, t=PACK)
+        scale_vec = gen_scale.rearrange("o k -> (o k)")
+        gen_tiles = {}
+        real_tiles = {}
+
+        nc.scalar.dma_start(out=scale_cols[:], in_=scale_vec.rearrange("(g p t) -> p g t", p=P, t=PACK))
+
+        def load_scale():
+            nc.sync.dma_start(out=scale_row[:], in_=scale_vec.partition_broadcast(P))
+
+        def load_gen(k, n=2):
+            tile = work.tile([P, n, D], U8, name="codes_in%d" % n, bufs=4 if n == 2 else 2)
+            for q in range(2 if k == 0 else 1):
+                cols = slice(q * D // 2, (q + 1) * D // 2) if k == 0 else slice(0, D)
+                nc.sync.dma_start(out=tile[:, :, cols], in_=gen_rows[k // PACK][:, k % PACK : k % PACK + n, cols])
+            for i in range(n):
+                gen_tiles[k + i] = tile[:, i, :]
+
+        def load_real(j):
+            tile = work.tile([P, D], BF16, name="real_in", bufs=8)
+            nc.sync.dma_start(out=tile[:], in_=real[j * P : (j + 1) * P, :])
+            real_tiles[j] = tile
+
+        def load_mult():
+            nc.sync.dma_start(out=wwords[:].rearrange("p c n -> p (c n)").bitcast(I32).rearrange("p (c n) -> p c n", c=C),
+                              in_=mult_words.rearrange("c p n -> p c n").bitcast(I32))
+            for q in range(4):
+                nc.sync.dma_start(out=wscales[32 * q : 32 * q + 4].bitcast(I32),
+                                  in_=mult_scales[:, 4 * q : 4 * q + 4, :].rearrange("c q n -> q c n").bitcast(I32))
+
+        wide = {}
+
+        def widen(k):
+            tile = work.tile([P, D], BF16, name="wide", bufs=6)
+            if k >= LATE:
+                nc.vector.tensor_tensor(out=tile[:], in0=gen_tiles[k].bitcast(FP8), in1=scale_row[:], op=MULT)
+            half = D // 2
+            for q in range(2 if k < LATE else 0):
+                cols = slice(q * half, (q + 1) * half)
+                codes = gen_tiles[k][:, cols].bitcast(FP8)
+                if k < 1:
+                    nc.vector.tensor_copy(out=tile[:, cols], in_=codes)
+                else:
+                    nc.scalar.copy(out=tile[:, cols], in_=codes)
+            wide[k] = tile
+
+        def turn(src, x):
+            words = src[:].bitcast(F32)
+            bank = psum.tile([P, 512], F32, name="bank")
+            for i in range(2):
+                for u in range(2):
+                    first = 256 * (2 * x + i) + u
+                    col = (2 * u + i) * P
+                    nc.tensor.transpose(bank[:, col : col + P], words[:, first : first + 255 : 2], ident[:])
+            return bank
+
+        def untangle(bank):
+            return bank[:].rearrange("p (u g r) -> p g r u", g=2, u=2)
+
+        turned = {}
+        gen_grouped = {}
+        real_grouped = {}
+
+        def turn_gen(k):
+            turned[k] = [turn(wide[k], x) for x in range(2)]
+
+        def copy_gen(k):
+            tile = work.tile([P, G, P, PACK], BF16, name="gen_grouped", bufs=3, align_bytes=64)
+            w32 = tile[:].rearrange("p g r t -> p (g r t)").bitcast(F32).rearrange("p (g r u) -> p g r u", g=G, u=2)
+            for x in range(2):
+                if k >= LATE:
+                    nc.scalar.copy(out=w32[:, 2 * x : 2 * x + 2], in_=untangle(turned[k][x]))
+                    continue
+                pair = slice(2 * x, 2 * x + 2)
+                values = turned[k][x][:].bitcast(BF16).rearrange("p (u g r e) -> p g r u e", g=2, u=2, e=2)
+                by_k = scale_cols[:, pair].rearrange("p g (u e) -> p g u e", u=2).unsqueeze(2).to_broadcast([P, 2, P, 2, 2])
+                nc.vector.tensor_tensor(out=tile[:, pair].rearrange("p g r (u e) -> p g r u e", u=2), in0=values, in1=by_k, op=MULT)
+            gen_grouped[k] = tile
+
+        def real_tile_steps(j):
+            h = j // JT
+            if h not in real_grouped:
+                grouped = work.tile([P, G, HN, PACK], BF16, name="real_grouped", tag="stage", bufs=4, align_bytes=64)
+                real_grouped[h] = grouped
+            tile = real_grouped[h]
+            w32 = tile[:].rearrange("p g r t -> p (g r t)").bitcast(F32).rearrange("p (g r u) -> p g r u", g=G, u=2)
+            r0 = (j % JT) * P
+            for x in range(2):
+                bank = turn(real_tiles[j], x)
+                nc.scalar.copy(out=w32[:, 2 * x : 2 * x + 2, r0 : r0 + P], in_=untangle(bank))
+
+        gcodes = {}
+
+        def quant_gen(k):
+            codes = work.tile([P, G * P], U32, name="gcodes", bufs=6, align_bytes=64)
+            scales = work.tile([P, G * P], U8, name="gscales", bufs=6, align_bytes=64)
+            nc.vector.quantize_mx(out=codes[:].bitcast(FP8X4), scales=scales[:], in_=gen_grouped[k][:].rearrange("p g r t -> p (g r t)"))
+            gcodes[k] = (codes, scales)
+
+        def quant_reals(h):
+            for x in range(2):
+                pair = slice(2 * x, 2 * x + 2)
+                nc.vector.quantize_mx(out=rcodes[:, h, pair].rearrange("p g n -> p (g n)").bitcast(FP8X4),
+                                      scales=rscales[:, h, pair].rearrange("p g n -> p (g n)"),
+                                      in_=real_grouped[h][:, pair].rearrange("p g r t -> p (g r t)"))
+
+        factors = {}
+
+        def dots(k, h):
+            codes, scales = gcodes[k]
+            bank = psum.tile([P, 512], F32, name="bank")
+            for g in range(G):
+                m = slice(g * P, (g + 1) * P)
+                nc.tensor.matmul_mx(out=bank[:], lhsT=codes[:, m].bitcast(FP8X4), lhsT_scale=scales[:, m],
+                                    rhs=rcodes[:, h, g].bitcast(FP8X4), rhs_scale=rscales[:, h, g],
+                                    start=(g == 0), stop=(g == G - 1))
+            c, t = k // PACK, k % PACK
+            if t == 0:
+                pair = work.tile([P, 2, PACK, HN], F32, name="factors", tag="stage", bufs=4, align_bytes=64)
+                factors[c, h] = pair
+            pair = factors[c, h]
+            nc.scalar.activation(out=pair[:, 0, t], in_=bank[:], func=SQUARE, bias=1.0)
+            nc.scalar.activation(out=pair[:, 1, t], in_=bank[:], func=IDENTITY, scale=imp32[:, k : k + 1], bias=imp32[:, k : k + 1])
+
+        ker = {}
+        kcodes = {}
+
+        def product(c, h):
+            pair = factors[c, h]
+            tile = work.tile([P, HN, PACK], BF16, name="ker", bufs=2, align_bytes=64)
+            nc.vector.tensor_tensor(out=tile[:].rearrange("p (n i) t -> p n t i", i=4),
+                                    in0=pair[:, 0].rearrange("p t (n i) -> p n t i", i=4),
+                                    in1=pair[:, 1].rearrange("p t (n i) -> p n t i", i=4), op=MULT)
+            ker[c, h] = tile
+
+        def quant_ker(c, h):
+            codes = work.tile([P, HN], U32, name="kcodes", bufs=6, align_bytes=64)
+            scales = work.tile([P, HN], U8, name="kscales", bufs=6, align_bytes=64)
+            nc.vector.quantize_mx(out=codes[:].bitcast(FP8X4), scales=scales[:], in_=ker[c, h][:].rearrange("p n t -> p (n t)"))
+            kcodes[c, h] = (codes, scales)
+
+        sums = {}
+
+        def witness(h, b, chunks):
+            if (h, b) not in sums:
+                bank = psum.tile([P, 512], F32, name="bank")
+                sums[h, b] = bank
+            for c in chunks:
+                codes, scales = kcodes[c, h]
+                nc.tensor.matmul_mx(out=sums[h, b][:], lhsT=wwords[:, c, 2 * P * b : 2 * P * (b + 1)].bitcast(FP4X4),
+                                    lhsT_scale=wscales[:, c, P * b : P * (b + 1)],
+                                    rhs=codes[:].bitcast(FP8X4), rhs_scale=scales[:],
+                                    start=(c == 0), stop=(c == C - 1))
+
+        def emit(h, b, on_vector, parts=1):
+            tile = work.tile([P, HN], F32, name="result", bufs=4)
+            w = HN // parts
+            for i in range(parts):
+                cols = slice(i * w, (i + 1) * w)
+                if on_vector:
+                    nc.vector.tensor_copy(out=tile[:, cols], in_=sums[h, b][:, cols])
+                else:
+                    nc.scalar.copy(out=tile[:, cols], in_=sums[h, b][:, cols])
+                nc.sync.dma_start(out=out[b * P : (b + 1) * P, h * HN + i * w : h * HN + (i + 1) * w], in_=tile[:, cols])
+
+        load_gen(0, 1)
+        load_gen(1, 1)
+        load_gen(2)
+        for j in range(H * JT):
+            load_real(j)
+        load_gen(4)
+        load_scale()
+        load_gen(6)
+
+        bank = psum.tile([P, 512], F32, name="bank")
+        for i in range(WARM):
+            nc.tensor.matmul(bank[:], lhsT=warm[:, :P], rhs=warm[:], start=True, stop=True)
+
+        steps = {"W": widen, "T": turn_gen, "C": copy_gen, "R": real_tile_steps, "Q": quant_gen, "H": quant_reals, "L": load_gen}
+        pairs = {"D": dots, "P": product, "K": quant_ker}
+        text = """W0 T0 W1 T1 W2 C0 R0 W3 C1 Q0 T2 R1 C2 Q1 R2 Q2 T3 R3 C3 R4 H0 W4 R5 Q3 R6 T4 C4 R7 D00 D10 W5 H1 D20 Q4 D30 T5 C5
+            W6 D01 Q5 D11 L8 W7 T6 C6 D21 W8 D31 T7 C7 L10 W9 Q6 T8 C8 M W10 D40 D41 Q7 T9 C9 W11 D50 D51 Q8 T10 C10
+            P00 Q9 T11 C11 D60 D61 K00 Q10 P01 Q11 D70 D71 K01 P10 D80 D90 D100 D110 K10 P11 D81 K11 D91 P20 D101 K20 D111 P21"""
+        for step in text.split():
+            if step == "M":
+                load_mult()
+            elif step[0] in steps:
+                steps[step[0]](int(step[1:]))
+            else:
+                pairs[step[0]](int(step[1:-1]), int(step[-1]))
+
+        for b in range(B):
+            witness(0, b, [0, 1])
+        for b in range(B):
+            witness(0, b, [2])
+        for b in range(B):
+            emit(0, b, False)
+        for b in range(B):
+            witness(1, b, [0, 1])
+        quant_ker(2, 1)
+        for b in range(B):
+            witness(1, b, [2])
+            emit(1, b, b % 2 == 1, 1 if b < 2 else 2)

@@ -27,8 +27,7 @@ HN = N // H
 JT = HN // P
 KT = C * PACK
 B = R // P
-WARM = 12
-LATE = 5
+BANK = 512
 
 
 def tile_kid_bootstrap_witness_s13_kernel(tc, gen_bytes, gen_scale, real, imp, mult_words, mult_scales, out):
@@ -41,10 +40,8 @@ def tile_kid_bootstrap_witness_s13_kernel(tc, gen_bytes, gen_scale, real, imp, m
 
         ident = keep.tile([P, P], F32, name="ident")
         make_identity(nc, ident[:])
-        scale_row = keep.tile([P, D], F32, name="scale_row")
         scale_cols = keep.tile([P, G, PACK], F32, name="scale_cols")
-        warm = keep.tile([P, 512], BF16, name="warm")
-        nc.vector.memset(warm[:], 0.0)
+        scale_row = keep.tile([P, D], F32, name="scale_row")
         wwords = keep.tile([P, C, 2 * R], U8, name="wwords", align_bytes=64)
         wscales = keep.tile([P, C, R], U8, name="wscales", align_bytes=64)
         imp_raw = keep.tile([P, C, PACK], BF16, name="imp_raw")
@@ -53,29 +50,20 @@ def tile_kid_bootstrap_witness_s13_kernel(tc, gen_bytes, gen_scale, real, imp, m
         rscales = keep.tile([P, H, G, HN], U8, name="rscales", align_bytes=64)
 
         nc.gpsimd.memset(wscales[:].rearrange("p c n -> p (c n)").bitcast(I32), 0)
-        nc.gpsimd.dma_start(out=imp_raw[:], in_=imp.rearrange("(c p t) -> p c t", p=P, t=PACK))
-        nc.gpsimd.tensor_copy(out=imp32[:], in_=imp_raw[:].rearrange("p c t -> p (c t)"))
+        nc.scalar.dma_start(out=scale_cols[:], in_=gen_scale.rearrange("o (g p t) -> p (o g) t", p=P, t=PACK))
+        nc.scalar.dma_start(out=imp_raw[:], in_=imp.rearrange("(c p t) -> p c t", p=P, t=PACK))
 
         gen_rows = gen_bytes.rearrange("(c p t) k -> c p t k", p=P, t=PACK)
-        scale_vec = gen_scale.rearrange("o k -> (o k)")
         gen_tiles = {}
         real_tiles = {}
 
-        nc.scalar.dma_start(out=scale_cols[:], in_=scale_vec.rearrange("(g p t) -> p g t", p=P, t=PACK))
-
-        def load_scale():
-            nc.sync.dma_start(out=scale_row[:], in_=scale_vec.partition_broadcast(P))
-
-        def load_gen(k, n=2):
-            tile = work.tile([P, n, D], U8, name="codes_in%d" % n, bufs=4 if n == 2 else 2)
-            for q in range(2 if k == 0 else 1):
-                cols = slice(q * D // 2, (q + 1) * D // 2) if k == 0 else slice(0, D)
-                nc.sync.dma_start(out=tile[:, :, cols], in_=gen_rows[k // PACK][:, k % PACK : k % PACK + n, cols])
-            for i in range(n):
-                gen_tiles[k + i] = tile[:, i, :]
+        def load_gen(k):
+            tile = work.tile([P, D], U8, name="gen_in", bufs=8)
+            nc.sync.dma_start(out=tile[:], in_=gen_rows[k // PACK][:, k % PACK])
+            gen_tiles[k] = tile
 
         def load_real(j):
-            tile = work.tile([P, D], BF16, name="real_in", bufs=8)
+            tile = work.tile([P, D], BF16, name="real_in", tag="rows", bufs=8)
             nc.sync.dma_start(out=tile[:], in_=real[j * P : (j + 1) * P, :])
             real_tiles[j] = tile
 
@@ -86,96 +74,89 @@ def tile_kid_bootstrap_witness_s13_kernel(tc, gen_bytes, gen_scale, real, imp, m
                 nc.sync.dma_start(out=wscales[32 * q : 32 * q + 4].bitcast(I32),
                                   in_=mult_scales[:, 4 * q : 4 * q + 4, :].rearrange("c q n -> q c n").bitcast(I32))
 
+        def spread_scales():
+            for g in range(G):
+                bank = psum.tile([P, BANK], F32, name="bank")
+                for t in range(PACK):
+                    nc.tensor.transpose(bank[:, t * P : (t + 1) * P], scale_cols[:, g, t : t + 1].to_broadcast([P, P]), ident[:])
+                nc.scalar.copy(out=scale_row[:, g * BANK : (g + 1) * BANK].rearrange("p (q t) -> p q t", t=PACK),
+                               in_=bank[:].rearrange("p (t q) -> p q t", t=PACK))
+
         wide = {}
 
-        def widen(k):
-            tile = work.tile([P, D], BF16, name="wide", bufs=6)
-            if k >= LATE:
-                nc.vector.tensor_tensor(out=tile[:], in0=gen_tiles[k].bitcast(FP8), in1=scale_row[:], op=MULT)
-            half = D // 2
-            for q in range(2 if k < LATE else 0):
-                cols = slice(q * half, (q + 1) * half)
-                codes = gen_tiles[k][:, cols].bitcast(FP8)
-                if k < 1:
-                    nc.vector.tensor_copy(out=tile[:, cols], in_=codes)
-                else:
-                    nc.scalar.copy(out=tile[:, cols], in_=codes)
+        def widen(k, parts=1):
+            tile = work.tile([P, D], BF16, name="wide", bufs=3)
+            for i in range(parts):
+                cols = slice(i * D // parts, (i + 1) * D // parts)
+                nc.vector.tensor_tensor(out=tile[:, cols], in0=gen_tiles[k][:, cols].bitcast(FP8), in1=scale_row[:, cols], op=MULT)
             wide[k] = tile
 
-        def turn(src, x):
-            words = src[:].bitcast(F32)
-            bank = psum.tile([P, 512], F32, name="bank")
+        def turn(words, x, window):
+            bank = psum.tile([P, BANK], F32, name="bank")
             for i in range(2):
                 for u in range(2):
-                    first = 256 * (2 * x + i) + u
                     col = (2 * u + i) * P
-                    nc.tensor.transpose(bank[:, col : col + P], words[:, first : first + 255 : 2], ident[:])
+                    nc.tensor.transpose(bank[:, col : col + P], words[:, window(2 * x + i, u)], ident[:])
             return bank
+
+        def every_second(g, u):
+            return slice(256 * g + u, 256 * g + u + 255, 2)
+
+        def in_a_run(g, u):
+            return slice(512 * u + P * g, 512 * u + P * (g + 1))
 
         def untangle(bank):
             return bank[:].rearrange("p (u g r) -> p g r u", g=2, u=2)
 
-        turned = {}
+        def as_words(tile):
+            return tile[:].rearrange("p g r t -> p (g r t)").bitcast(F32).rearrange("p (g r u) -> p g r u", g=G, u=2)
+
         gen_grouped = {}
         real_grouped = {}
 
         def turn_gen(k):
-            turned[k] = [turn(wide[k], x) for x in range(2)]
-
-        def copy_gen(k):
             tile = work.tile([P, G, P, PACK], BF16, name="gen_grouped", bufs=3, align_bytes=64)
-            w32 = tile[:].rearrange("p g r t -> p (g r t)").bitcast(F32).rearrange("p (g r u) -> p g r u", g=G, u=2)
             for x in range(2):
-                if k >= LATE:
-                    nc.scalar.copy(out=w32[:, 2 * x : 2 * x + 2], in_=untangle(turned[k][x]))
-                    continue
-                pair = slice(2 * x, 2 * x + 2)
-                values = turned[k][x][:].bitcast(BF16).rearrange("p (u g r e) -> p g r u e", g=2, u=2, e=2)
-                by_k = scale_cols[:, pair].rearrange("p g (u e) -> p g u e", u=2).unsqueeze(2).to_broadcast([P, 2, P, 2, 2])
-                nc.vector.tensor_tensor(out=tile[:, pair].rearrange("p g r (u e) -> p g r u e", u=2), in0=values, in1=by_k, op=MULT)
+                bank = turn(wide[k][:].bitcast(F32), x, every_second)
+                nc.scalar.copy(out=as_words(tile)[:, 2 * x : 2 * x + 2], in_=untangle(bank))
             gen_grouped[k] = tile
 
-        def real_tile_steps(j):
+        def turn_real(j):
             h = j // JT
             if h not in real_grouped:
-                grouped = work.tile([P, G, HN, PACK], BF16, name="real_grouped", tag="stage", bufs=4, align_bytes=64)
-                real_grouped[h] = grouped
-            tile = real_grouped[h]
-            w32 = tile[:].rearrange("p g r t -> p (g r t)").bitcast(F32).rearrange("p (g r u) -> p g r u", g=G, u=2)
+                real_grouped[h] = work.tile([P, G, HN, PACK], BF16, name="real_grouped", tag="stage", bufs=5, align_bytes=64)
             r0 = (j % JT) * P
             for x in range(2):
-                bank = turn(real_tiles[j], x)
-                nc.scalar.copy(out=w32[:, 2 * x : 2 * x + 2, r0 : r0 + P], in_=untangle(bank))
+                bank = turn(real_tiles[j][:].bitcast(F32), x, every_second)
+                nc.scalar.copy(out=as_words(real_grouped[h])[:, 2 * x : 2 * x + 2, r0 : r0 + P], in_=untangle(bank))
 
         gcodes = {}
 
         def quant_gen(k):
-            codes = work.tile([P, G * P], U32, name="gcodes", bufs=6, align_bytes=64)
-            scales = work.tile([P, G * P], U8, name="gscales", bufs=6, align_bytes=64)
+            codes = work.tile([P, G * P], U32, name="gcodes", bufs=KT, align_bytes=64)
+            scales = work.tile([P, G * P], U8, name="gscales", bufs=KT, align_bytes=64)
             nc.vector.quantize_mx(out=codes[:].bitcast(FP8X4), scales=scales[:], in_=gen_grouped[k][:].rearrange("p g r t -> p (g r t)"))
             gcodes[k] = (codes, scales)
 
-        def quant_reals(h):
-            for x in range(2):
-                pair = slice(2 * x, 2 * x + 2)
-                nc.vector.quantize_mx(out=rcodes[:, h, pair].rearrange("p g n -> p (g n)").bitcast(FP8X4),
-                                      scales=rscales[:, h, pair].rearrange("p g n -> p (g n)"),
-                                      in_=real_grouped[h][:, pair].rearrange("p g r t -> p (g r t)"))
+        def quant_real(pair):
+            h, rows = pair // 2, slice(pair % 2 * 2 * P, (pair % 2 + 1) * 2 * P)
+            for g in range(G):
+                nc.vector.quantize_mx(out=rcodes[:, h, g, rows].bitcast(FP8X4), scales=rscales[:, h, g, rows],
+                                      in_=real_grouped[h][:, g, rows].rearrange("p r t -> p (r t)"))
 
         factors = {}
 
         def dots(k, h):
             codes, scales = gcodes[k]
-            bank = psum.tile([P, 512], F32, name="bank")
+            bank = psum.tile([P, BANK], F32, name="bank")
             for g in range(G):
                 m = slice(g * P, (g + 1) * P)
                 nc.tensor.matmul_mx(out=bank[:], lhsT=codes[:, m].bitcast(FP8X4), lhsT_scale=scales[:, m],
                                     rhs=rcodes[:, h, g].bitcast(FP8X4), rhs_scale=rscales[:, h, g],
                                     start=(g == 0), stop=(g == G - 1))
             c, t = k // PACK, k % PACK
-            if t == 0:
-                pair = work.tile([P, 2, PACK, HN], F32, name="factors", tag="stage", bufs=4, align_bytes=64)
-                factors[c, h] = pair
+            if (c, h) not in factors:
+                factors[c, h] = work.tile([P, 2, PACK, HN], F32, name="factors", tag="stage", bufs=5, align_bytes=64)
             pair = factors[c, h]
             nc.scalar.activation(out=pair[:, 0, t], in_=bank[:], func=SQUARE, bias=1.0)
             nc.scalar.activation(out=pair[:, 1, t], in_=bank[:], func=IDENTITY, scale=imp32[:, k : k + 1], bias=imp32[:, k : k + 1])
@@ -192,8 +173,8 @@ def tile_kid_bootstrap_witness_s13_kernel(tc, gen_bytes, gen_scale, real, imp, m
             ker[c, h] = tile
 
         def quant_ker(c, h):
-            codes = work.tile([P, HN], U32, name="kcodes", bufs=6, align_bytes=64)
-            scales = work.tile([P, HN], U8, name="kscales", bufs=6, align_bytes=64)
+            codes = work.tile([P, HN], U32, name="kcodes", bufs=C * H, align_bytes=64)
+            scales = work.tile([P, HN], U8, name="kscales", bufs=C * H, align_bytes=64)
             nc.vector.quantize_mx(out=codes[:].bitcast(FP8X4), scales=scales[:], in_=ker[c, h][:].rearrange("p n t -> p (n t)"))
             kcodes[c, h] = (codes, scales)
 
@@ -201,8 +182,7 @@ def tile_kid_bootstrap_witness_s13_kernel(tc, gen_bytes, gen_scale, real, imp, m
 
         def witness(h, b, chunks):
             if (h, b) not in sums:
-                bank = psum.tile([P, 512], F32, name="bank")
-                sums[h, b] = bank
+                sums[h, b] = psum.tile([P, BANK], F32, name="bank")
             for c in chunks:
                 codes, scales = kcodes[c, h]
                 nc.tensor.matmul_mx(out=sums[h, b][:], lhsT=wwords[:, c, 2 * P * b : 2 * P * (b + 1)].bitcast(FP4X4),
@@ -210,52 +190,74 @@ def tile_kid_bootstrap_witness_s13_kernel(tc, gen_bytes, gen_scale, real, imp, m
                                     rhs=codes[:].bitcast(FP8X4), rhs_scale=scales[:],
                                     start=(c == 0), stop=(c == C - 1))
 
-        def emit(h, b, on_vector, parts=1):
-            tile = work.tile([P, HN], F32, name="result", bufs=4)
-            w = HN // parts
-            for i in range(parts):
-                cols = slice(i * w, (i + 1) * w)
-                if on_vector:
-                    nc.vector.tensor_copy(out=tile[:, cols], in_=sums[h, b][:, cols])
-                else:
-                    nc.scalar.copy(out=tile[:, cols], in_=sums[h, b][:, cols])
-                nc.sync.dma_start(out=out[b * P : (b + 1) * P, h * HN + i * w : h * HN + (i + 1) * w], in_=tile[:, cols])
-
-        load_gen(0, 1)
-        load_gen(1, 1)
-        load_gen(2)
-        for j in range(H * JT):
-            load_real(j)
-        load_gen(4)
-        load_scale()
-        load_gen(6)
-
-        bank = psum.tile([P, 512], F32, name="bank")
-        for i in range(WARM):
-            nc.tensor.matmul(bank[:], lhsT=warm[:, :P], rhs=warm[:], start=True, stop=True)
-
-        steps = {"W": widen, "T": turn_gen, "C": copy_gen, "R": real_tile_steps, "Q": quant_gen, "H": quant_reals, "L": load_gen}
-        pairs = {"D": dots, "P": product, "K": quant_ker}
-        text = """W0 T0 W1 T1 W2 C0 R0 W3 C1 Q0 T2 R1 C2 Q1 R2 Q2 T3 R3 C3 R4 H0 W4 R5 Q3 R6 T4 C4 R7 D00 D10 W5 H1 D20 Q4 D30 T5 C5
-            W6 D01 Q5 D11 L8 W7 T6 C6 D21 W8 D31 T7 C7 L10 W9 Q6 T8 C8 M W10 D40 D41 Q7 T9 C9 W11 D50 D51 Q8 T10 C10
-            P00 Q9 T11 C11 D60 D61 K00 Q10 P01 Q11 D70 D71 K01 P10 D80 D90 D100 D110 K10 P11 D81 K11 D91 P20 D101 K20 D111 P21"""
-        for step in text.split():
-            if step == "M":
-                load_mult()
-            elif step[0] in steps:
-                steps[step[0]](int(step[1:]))
+        def emit(h, b, on_vector):
+            tile = work.tile([P, HN], F32, name="result", tag="rows", bufs=8)
+            if on_vector:
+                nc.vector.tensor_copy(out=tile[:], in_=sums[h, b][:])
             else:
-                pairs[step[0]](int(step[1:-1]), int(step[-1]))
+                nc.scalar.copy(out=tile[:], in_=sums[h, b][:])
+            nc.sync.dma_start(out=out[b * P : (b + 1) * P, h * HN : (h + 1) * HN], in_=tile[:])
 
+        load_gen(0)
+        for pair in range(H * JT // 2):
+            load_real(2 * pair)
+            load_real(2 * pair + 1)
+            load_gen(pair + 1)
+        for k in range(5, 8):
+            load_gen(k)
+        nc.scalar.activation(out=imp32[:], in_=imp_raw[:].rearrange("p c t -> p (c t)"), func=IDENTITY)
+        spread_scales()
+
+        products = {7: (0, 0), 10: (0, 1), 12: (1, 0)}
+        for step in range(KT + 1):
+            if 2 <= step < KT - 6:
+                load_gen(step + 6)
+            if step == 6:
+                load_mult()
+            if step < KT:
+                widen(step, 4 if step == 0 else 1)
+            if step >= 1:
+                turn_gen(step - 1)
+            if step < H * JT // 2:
+                turn_real(2 * step)
+                turn_real(2 * step + 1)
+            if step - 1 in products:
+                quant_ker(*products[step - 1])
+            if 1 <= step <= H * JT // 2:
+                quant_real(step - 1)
+            if step == 4:
+                dots(0, 0)
+            if step >= 4:
+                dots(step - 3, 0)
+            if step >= 5:
+                dots(step - 5, 1) if step < KT else dots(KT - 2, 0)
+            if step >= 2 and step < KT:
+                quant_gen(step - 2)
+            if step == KT - 1:
+                quant_gen(step - 1)
+            if step in products:
+                product(*products[step])
+
+        quant_gen(KT - 1)
+        quant_ker(*products[KT])
+        dots(KT - 5, 1)
+        dots(KT - 1, 0)
+        for k in range(KT - PACK, KT):
+            dots(k, 1)
+        product(1, 1)
+        product(2, 0)
+        quant_ker(1, 1)
+        quant_ker(2, 0)
         for b in range(B):
-            witness(0, b, [0, 1])
+            witness(0, b, range(C - 1))
         for b in range(B):
-            witness(0, b, [2])
+            witness(0, b, [C - 1])
+        product(2, 1)
         for b in range(B):
             emit(0, b, False)
         for b in range(B):
-            witness(1, b, [0, 1])
+            witness(1, b, range(C - 1))
         quant_ker(2, 1)
         for b in range(B):
-            witness(1, b, [2])
-            emit(1, b, b % 2 == 1, 1 if b < 2 else 2)
+            witness(1, b, [C - 1])
+            emit(1, b, b % 2 == 1)

@@ -167,9 +167,9 @@ def tile_kid_bootstrap_witness_s13_kernel(tc, gen_bytes, gen_scale, real, imp, m
         def product(c, h):
             pair = factors[c, h]
             tile = work.tile([P, HN, PACK], BF16, name="ker", bufs=2, align_bytes=64)
-            nc.vector.tensor_tensor(out=tile[:].rearrange("p (n i) t -> p n t i", i=4),
-                                    in0=pair[:, 0].rearrange("p t (n i) -> p n t i", i=4),
-                                    in1=pair[:, 1].rearrange("p t (n i) -> p n t i", i=4), op=MULT)
+            nc.vector.tensor_tensor(out=tile[:].rearrange("p (n i) t -> p n t i", i=2),
+                                    in0=pair[:, 0].rearrange("p t (n i) -> p n t i", i=2),
+                                    in1=pair[:, 1].rearrange("p t (n i) -> p n t i", i=2), op=MULT)
             ker[c, h] = tile
 
         def quant_ker(c, h):

@@ -40,7 +40,7 @@ def tile_kid_bootstrap_witness_s13_kernel(tc, gen_bytes, gen_scale, real, imp, m
 
         ident = keep.tile([P, P], F32, name="ident")
         make_identity(nc, ident[:])
-        scale_cols = keep.tile([P, G, PACK], F32, name="scale_cols")
+        scale_cols = keep.tile([P, G, 8], F32, name="scale_cols")
         scale_row = keep.tile([P, D], F32, name="scale_row")
         wwords = keep.tile([P, C, 2 * R], U8, name="wwords", align_bytes=64)
         wscales = keep.tile([P, C, R], U8, name="wscales", align_bytes=64)
@@ -50,8 +50,9 @@ def tile_kid_bootstrap_witness_s13_kernel(tc, gen_bytes, gen_scale, real, imp, m
         rscales = keep.tile([P, H, G, HN], U8, name="rscales", align_bytes=64)
 
         nc.gpsimd.memset(wscales[:].rearrange("p c n -> p (c n)").bitcast(I32), 0)
-        nc.scalar.dma_start(out=scale_cols[:], in_=gen_scale.rearrange("o (g p t) -> p (o g) t", p=P, t=PACK))
-        nc.scalar.dma_start(out=imp_raw[:], in_=imp.rearrange("(c p t) -> p c t", p=P, t=PACK))
+        scale_by_k = gen_scale.rearrange("o (g p t) -> p (o g) t", p=P, t=PACK)
+        nc.sync.dma_start(out=scale_cols[:, :1, :PACK], in_=scale_by_k[:, :1])
+        nc.scalar.dma_start(out=scale_cols[:, 1:, :PACK], in_=scale_by_k[:, 1:])
 
         gen_rows = gen_bytes.rearrange("(c p t) k -> c p t k", p=P, t=PACK)
         gen_tiles = {}
@@ -79,13 +80,13 @@ def tile_kid_bootstrap_witness_s13_kernel(tc, gen_bytes, gen_scale, real, imp, m
                 bank = psum.tile([P, BANK], F32, name="bank")
                 for t in range(PACK):
                     nc.tensor.transpose(bank[:, t * P : (t + 1) * P], scale_cols[:, g, t : t + 1].to_broadcast([P, P]), ident[:])
-                nc.scalar.copy(out=scale_row[:, g * BANK : (g + 1) * BANK].rearrange("p (q t) -> p q t", t=PACK),
-                               in_=bank[:].rearrange("p (t q) -> p q t", t=PACK))
+                nc.scalar.activation(out=scale_row[:, g * BANK : (g + 1) * BANK].rearrange("p (q t) -> p q t", t=PACK),
+                                     in_=bank[:].rearrange("p (t q) -> p q t", t=PACK), func=IDENTITY)
 
         wide = {}
 
         def widen(k, parts=1):
-            tile = work.tile([P, D], BF16, name="wide", bufs=3)
+            tile = work.tile([P, D], BF16, name="wide", bufs=4)
             for i in range(parts):
                 cols = slice(i * D // parts, (i + 1) * D // parts)
                 nc.vector.tensor_tensor(out=tile[:, cols], in0=gen_tiles[k][:, cols].bitcast(FP8), in1=scale_row[:, cols], op=MULT)
@@ -102,47 +103,50 @@ def tile_kid_bootstrap_witness_s13_kernel(tc, gen_bytes, gen_scale, real, imp, m
         def every_second(g, u):
             return slice(256 * g + u, 256 * g + u + 255, 2)
 
-        def in_a_run(g, u):
-            return slice(512 * u + P * g, 512 * u + P * (g + 1))
-
         def untangle(bank):
             return bank[:].rearrange("p (u g r) -> p g r u", g=2, u=2)
 
-        def as_words(tile):
-            return tile[:].rearrange("p g r t -> p (g r t)").bitcast(F32).rearrange("p (g r u) -> p g r u", g=G, u=2)
+        def as_words(tile, groups=G):
+            return tile[:].rearrange("p g r t -> p (g r t)").bitcast(F32).rearrange("p (g r u) -> p g r u", g=groups, u=2)
 
         gen_grouped = {}
         real_grouped = {}
 
-        def turn_gen(k):
-            tile = work.tile([P, G, P, PACK], BF16, name="gen_grouped", bufs=3, align_bytes=64)
-            for x in range(2):
-                bank = turn(wide[k][:].bitcast(F32), x, every_second)
-                nc.scalar.copy(out=as_words(tile)[:, 2 * x : 2 * x + 2], in_=untangle(bank))
-            gen_grouped[k] = tile
+        def turn_gen(k, on_vector=0):
+            if k % 2 == 0:
+                gen_grouped[k // 2] = work.tile([P, 2 * G, P, PACK], BF16, name="gen_grouped", bufs=2, align_bytes=64)
+            words = as_words(gen_grouped[k // 2], 2 * G)
+            banks = [turn(wide[k][:].bitcast(F32), x, every_second) for x in range(2)]
+            for x in (1, 0):
+                first = G * (k % 2) + 2 * x
+                copy = nc.vector.tensor_copy if x < on_vector else nc.scalar.copy
+                copy(out=words[:, first : first + 2], in_=untangle(banks[x]))
 
         def turn_real(j):
             h = j // JT
             if h not in real_grouped:
                 real_grouped[h] = work.tile([P, G, HN, PACK], BF16, name="real_grouped", tag="stage", bufs=5, align_bytes=64)
             r0 = (j % JT) * P
-            for x in range(2):
-                bank = turn(real_tiles[j][:].bitcast(F32), x, every_second)
-                nc.scalar.copy(out=as_words(real_grouped[h])[:, 2 * x : 2 * x + 2, r0 : r0 + P], in_=untangle(bank))
+            banks = [turn(real_tiles[j][:].bitcast(F32), x, every_second) for x in range(2)]
+            for x in (1, 0):
+                nc.scalar.copy(out=as_words(real_grouped[h])[:, 2 * x : 2 * x + 2, r0 : r0 + P], in_=untangle(banks[x]))
 
         gcodes = {}
 
-        def quant_gen(k):
-            codes = work.tile([P, G * P], U32, name="gcodes", bufs=KT, align_bytes=64)
-            scales = work.tile([P, G * P], U8, name="gscales", bufs=KT, align_bytes=64)
-            nc.vector.quantize_mx(out=codes[:].bitcast(FP8X4), scales=scales[:], in_=gen_grouped[k][:].rearrange("p g r t -> p (g r t)"))
-            gcodes[k] = (codes, scales)
+        def quant_gen(pair):
+            codes = work.tile([P, 2, G * P], U32, name="gcodes", bufs=4, align_bytes=64)
+            scales = work.tile([P, 2, G * P], U8, name="gscales", bufs=4, align_bytes=64)
+            nc.vector.quantize_mx(out=codes[:].rearrange("p i n -> p (i n)").bitcast(FP8X4), scales=scales[:].rearrange("p i n -> p (i n)"),
+                                  in_=gen_grouped[pair][:].rearrange("p g r t -> p (g r t)"))
+            for i in range(2):
+                gcodes[2 * pair + i] = (codes[:, i], scales[:, i])
 
-        def quant_real(pair):
-            h, rows = pair // 2, slice(pair % 2 * 2 * P, (pair % 2 + 1) * 2 * P)
-            for g in range(G):
-                nc.vector.quantize_mx(out=rcodes[:, h, g, rows].bitcast(FP8X4), scales=rscales[:, h, g, rows],
-                                      in_=real_grouped[h][:, g, rows].rearrange("p r t -> p (r t)"))
+        def quant_real(h):
+            for x in range(2):
+                pair = slice(2 * x, 2 * x + 2)
+                nc.vector.quantize_mx(out=rcodes[:, h, pair].rearrange("p g n -> p (g n)").bitcast(FP8X4),
+                                      scales=rscales[:, h, pair].rearrange("p g n -> p (g n)"),
+                                      in_=real_grouped[h][:, pair].rearrange("p g r t -> p (g r t)"))
 
         factors = {}
 
@@ -199,57 +203,71 @@ def tile_kid_bootstrap_witness_s13_kernel(tc, gen_bytes, gen_scale, real, imp, m
             nc.sync.dma_start(out=out[b * P : (b + 1) * P, h * HN : (h + 1) * HN], in_=tile[:])
 
         load_gen(0)
-        for pair in range(H * JT // 2):
+        load_real(0)
+        load_gen(1)
+        load_real(1)
+        for pair in range(1, H * JT // 2):
+            load_gen(pair + 1)
             load_real(2 * pair)
             load_real(2 * pair + 1)
-            load_gen(pair + 1)
+        nc.sync.dma_start(out=imp_raw[:], in_=imp.rearrange("(c p t) -> p c t", p=P, t=PACK))
         for k in range(5, 8):
             load_gen(k)
-        nc.scalar.activation(out=imp32[:], in_=imp_raw[:].rearrange("p c t -> p (c t)"), func=IDENTITY)
         spread_scales()
 
-        products = {7: (0, 0), 10: (0, 1), 12: (1, 0)}
-        for step in range(KT + 1):
-            if 2 <= step < KT - 6:
-                load_gen(step + 6)
-            if step == 6:
-                load_mult()
-            if step < KT:
-                widen(step, 4 if step == 0 else 1)
-            if step >= 1:
-                turn_gen(step - 1)
-            if step < H * JT // 2:
-                turn_real(2 * step)
-                turn_real(2 * step + 1)
-            if step - 1 in products:
-                quant_ker(*products[step - 1])
-            if 1 <= step <= H * JT // 2:
-                quant_real(step - 1)
-            if step == 4:
-                dots(0, 0)
-            if step >= 4:
-                dots(step - 3, 0)
-            if step >= 5:
-                dots(step - 5, 1) if step < KT else dots(KT - 2, 0)
-            if step >= 2 and step < KT:
-                quant_gen(step - 2)
-            if step == KT - 1:
-                quant_gen(step - 1)
-            if step in products:
-                product(*products[step])
-
-        quant_gen(KT - 1)
-        quant_ker(*products[KT])
-        dots(KT - 5, 1)
-        dots(KT - 1, 0)
+        widen(0, G)
+        widen(1)
+        for k in range(PACK):
+            if k + 2 < PACK:
+                widen(k + 2)
+            turn_real(2 * k)
+            turn_real(2 * k + 1)
+            turn_gen(k)
+            load_gen(k + 8)
+            if k == 1:
+                quant_gen(0)
+                quant_real(0)
+        load_mult()
+        nc.scalar.activation(out=imp32[:], in_=imp_raw[:].rearrange("p c t -> p (c t)"), func=IDENTITY)
+        widen(4)
+        widen(5)
+        dots(0, 0)
+        dots(1, 0)
+        quant_gen(1)
+        quant_real(1)
+        turn_gen(4)
+        turn_gen(5)
+        for pair in range(3, KT // 2):
+            last = pair == KT // 2 - 1
+            widen(2 * pair)
+            if pair == 5:
+                quant_ker(0, 0)
+            widen(2 * pair + 1)
+            for k, h in ((2 * pair - 4, 0), (2 * pair - 3, 0), (2 * pair - 6, 1), (2 * pair - 5, 1)):
+                dots(k, h)
+            quant_gen(pair - 1)
+            if pair >= 4:
+                product(0, pair - 4)
+            turn_gen(2 * pair, 0 if last else 0)
+            turn_gen(2 * pair + 1, 0 if last else 0)
+        quant_ker(0, 1)
+        dots(8, 0)
+        dots(9, 0)
+        quant_gen(5)
+        product(1, 0)
+        dots(6, 1)
+        dots(7, 1)
+        dots(10, 0)
+        dots(11, 0)
         for k in range(KT - PACK, KT):
             dots(k, 1)
         product(1, 1)
-        product(2, 0)
+        quant_ker(1, 0)
         quant_ker(1, 1)
-        quant_ker(2, 0)
+        product(2, 0)
         for b in range(B):
             witness(0, b, range(C - 1))
+        quant_ker(2, 0)
         for b in range(B):
             witness(0, b, [C - 1])
         product(2, 1)

@@ -28,6 +28,7 @@ JT = HN // P
 KT = C * PACK
 B = R // P
 BANK = 512
+ON_VECTOR = 2
 
 
 def tile_kid_bootstrap_witness_s13_kernel(tc, gen_bytes, gen_scale, real, imp, mult_words, mult_scales, out):
@@ -40,8 +41,7 @@ def tile_kid_bootstrap_witness_s13_kernel(tc, gen_bytes, gen_scale, real, imp, m
 
         ident = keep.tile([P, P], F32, name="ident")
         make_identity(nc, ident[:])
-        scale_cols = keep.tile([P, G, 8], F32, name="scale_cols")
-        scale_row = keep.tile([P, D], F32, name="scale_row")
+        scale_cols = keep.tile([P, G, PACK], F32, name="scale_cols")
         wwords = keep.tile([P, C, 2 * R], U8, name="wwords", align_bytes=64)
         wscales = keep.tile([P, C, R], U8, name="wscales", align_bytes=64)
         imp_raw = keep.tile([P, C, PACK], BF16, name="imp_raw")
@@ -50,9 +50,7 @@ def tile_kid_bootstrap_witness_s13_kernel(tc, gen_bytes, gen_scale, real, imp, m
         rscales = keep.tile([P, H, G, HN], U8, name="rscales", align_bytes=64)
 
         nc.gpsimd.memset(wscales[:].rearrange("p c n -> p (c n)").bitcast(I32), 0)
-        scale_by_k = gen_scale.rearrange("o (g p t) -> p (o g) t", p=P, t=PACK)
-        nc.sync.dma_start(out=scale_cols[:, :1, :PACK], in_=scale_by_k[:, :1])
-        nc.scalar.dma_start(out=scale_cols[:, 1:, :PACK], in_=scale_by_k[:, 1:])
+        nc.scalar.dma_start(out=scale_cols[:], in_=gen_scale.rearrange("o (g p t) -> p (o g) t", p=P, t=PACK))
 
         gen_rows = gen_bytes.rearrange("(c p t) k -> c p t k", p=P, t=PACK)
         gen_tiles = {}
@@ -75,21 +73,14 @@ def tile_kid_bootstrap_witness_s13_kernel(tc, gen_bytes, gen_scale, real, imp, m
                 nc.sync.dma_start(out=wscales[32 * q : 32 * q + 4].bitcast(I32),
                                   in_=mult_scales[:, 4 * q : 4 * q + 4, :].rearrange("c q n -> q c n").bitcast(I32))
 
-        def spread_scales():
-            for g in range(G):
-                bank = psum.tile([P, BANK], F32, name="bank")
-                for t in range(PACK):
-                    nc.tensor.transpose(bank[:, t * P : (t + 1) * P], scale_cols[:, g, t : t + 1].to_broadcast([P, P]), ident[:])
-                nc.scalar.activation(out=scale_row[:, g * BANK : (g + 1) * BANK].rearrange("p (q t) -> p q t", t=PACK),
-                                     in_=bank[:].rearrange("p (t q) -> p q t", t=PACK), func=IDENTITY)
-
         wide = {}
 
-        def widen(k, parts=1):
+        def widen(k):
             tile = work.tile([P, D], BF16, name="wide", bufs=4)
-            for i in range(parts):
-                cols = slice(i * D // parts, (i + 1) * D // parts)
-                nc.vector.tensor_tensor(out=tile[:, cols], in0=gen_tiles[k][:, cols].bitcast(FP8), in1=scale_row[:, cols], op=MULT)
+            if k < ON_VECTOR:
+                nc.vector.tensor_copy(out=tile[:], in_=gen_tiles[k][:].bitcast(FP8))
+            else:
+                nc.scalar.copy(out=tile[:], in_=gen_tiles[k][:].bitcast(FP8))
             wide[k] = tile
 
         def turn(words, x, window):
@@ -112,15 +103,20 @@ def tile_kid_bootstrap_witness_s13_kernel(tc, gen_bytes, gen_scale, real, imp, m
         gen_grouped = {}
         real_grouped = {}
 
-        def turn_gen(k, on_vector=0):
+        turned = {}
+
+        def turn_gen(k):
+            turned[k] = [turn(wide[k][:].bitcast(F32), x, every_second) for x in range(2)]
+
+        def scale_gen(k):
             if k % 2 == 0:
-                gen_grouped[k // 2] = work.tile([P, 2 * G, P, PACK], BF16, name="gen_grouped", bufs=2, align_bytes=64)
-            words = as_words(gen_grouped[k // 2], 2 * G)
-            banks = [turn(wide[k][:].bitcast(F32), x, every_second) for x in range(2)]
+                gen_grouped[k // 2] = work.tile([P, 2 * G, P, PACK], BF16, name="gen_grouped", tag="pair%d" % (k // 2 % 2), bufs=1, align_bytes=64)
             for x in (1, 0):
                 first = G * (k % 2) + 2 * x
-                copy = nc.vector.tensor_copy if x < on_vector else nc.scalar.copy
-                copy(out=words[:, first : first + 2], in_=untangle(banks[x]))
+                values = turned[k][x][:].bitcast(BF16).rearrange("p (u g r e) -> p g r u e", g=2, u=2, e=2)
+                by_k = scale_cols[:, 2 * x : 2 * x + 2].rearrange("p g (u e) -> p g u e", u=2).unsqueeze(2).to_broadcast([P, 2, P, 2, 2])
+                nc.vector.tensor_tensor(out=gen_grouped[k // 2][:, first : first + 2].rearrange("p g r (u e) -> p g r u e", u=2),
+                                        in0=values, in1=by_k, op=MULT)
 
         def turn_real(j):
             h = j // JT
@@ -168,10 +164,10 @@ def tile_kid_bootstrap_witness_s13_kernel(tc, gen_bytes, gen_scale, real, imp, m
         ker = {}
         kcodes = {}
 
-        def product(c, h):
+        def product(c, h, engine, tag, bufs):
             pair = factors[c, h]
-            tile = work.tile([P, HN, PACK], BF16, name="ker", bufs=2, align_bytes=64)
-            nc.vector.tensor_tensor(out=tile[:].rearrange("p (n i) t -> p n t i", i=2),
+            tile = work.tile([P, HN, PACK], BF16, name="ker", tag=tag, bufs=bufs, align_bytes=64)
+            engine.tensor_tensor(out=tile[:].rearrange("p (n i) t -> p n t i", i=2),
                                     in0=pair[:, 0].rearrange("p t (n i) -> p n t i", i=2),
                                     in1=pair[:, 1].rearrange("p t (n i) -> p n t i", i=2), op=MULT)
             ker[c, h] = tile
@@ -202,75 +198,66 @@ def tile_kid_bootstrap_witness_s13_kernel(tc, gen_bytes, gen_scale, real, imp, m
                 nc.scalar.copy(out=tile[:], in_=sums[h, b][:])
             nc.sync.dma_start(out=out[b * P : (b + 1) * P, h * HN : (h + 1) * HN], in_=tile[:])
 
-        load_gen(0)
+        nc.scalar.dma_start(out=imp_raw[:], in_=imp.rearrange("(c p t) -> p c t", p=P, t=PACK))
         load_real(0)
+        load_gen(0)
         load_gen(1)
         load_real(1)
         for pair in range(1, H * JT // 2):
             load_gen(pair + 1)
             load_real(2 * pair)
             load_real(2 * pair + 1)
-        nc.sync.dma_start(out=imp_raw[:], in_=imp.rearrange("(c p t) -> p c t", p=P, t=PACK))
         for k in range(5, 8):
             load_gen(k)
-        spread_scales()
 
-        widen(0, G)
+        nc.scalar.activation(out=imp32[:], in_=imp_raw[:].rearrange("p c t -> p (c t)"), func=IDENTITY)
+        widen(0)
         widen(1)
         for k in range(PACK):
-            if k + 2 < PACK:
-                widen(k + 2)
             turn_real(2 * k)
-            turn_real(2 * k + 1)
             turn_gen(k)
+            turn_real(2 * k + 1)
+            scale_gen(k)
+            widen(k + 2)
             load_gen(k + 8)
             if k == 1:
                 quant_gen(0)
+            if k == 2:
                 quant_real(0)
         load_mult()
-        nc.scalar.activation(out=imp32[:], in_=imp_raw[:].rearrange("p c t -> p (c t)"), func=IDENTITY)
-        widen(4)
-        widen(5)
         dots(0, 0)
         dots(1, 0)
         quant_gen(1)
         quant_real(1)
-        turn_gen(4)
-        turn_gen(5)
-        for pair in range(3, KT // 2):
-            last = pair == KT // 2 - 1
-            widen(2 * pair)
-            if pair == 5:
-                quant_ker(0, 0)
-            widen(2 * pair + 1)
-            for k, h in ((2 * pair - 4, 0), (2 * pair - 3, 0), (2 * pair - 6, 1), (2 * pair - 5, 1)):
-                dots(k, h)
-            quant_gen(pair - 1)
-            if pair >= 4:
-                product(0, pair - 4)
-            turn_gen(2 * pair, 0 if last else 0)
-            turn_gen(2 * pair + 1, 0 if last else 0)
-        quant_ker(0, 1)
-        dots(8, 0)
-        dots(9, 0)
-        quant_gen(5)
-        product(1, 0)
-        dots(6, 1)
-        dots(7, 1)
-        dots(10, 0)
-        dots(11, 0)
-        for k in range(KT - PACK, KT):
-            dots(k, 1)
-        product(1, 1)
-        quant_ker(1, 0)
-        quant_ker(1, 1)
-        product(2, 0)
+        early = [(0, 0), (0, 1), (1, 0)]
+        for pair in range(2, KT // 2):
+            turn_gen(2 * pair)
+            turn_gen(2 * pair + 1)
+            if pair + 1 < KT // 2:
+                widen(2 * pair + 2)
+                widen(2 * pair + 3)
+            scale_gen(2 * pair)
+            scale_gen(2 * pair + 1)
+            groups = [((2 * pair - 2, 0), (2 * pair - 1, 0)), ((2 * pair - 4, 1), (2 * pair - 3, 1))]
+            for group in groups[:: -1 if pair % 2 else 1]:
+                for k, h in group:
+                    dots(k, h)
+            quant_gen(pair)
+            if pair >= 3:
+                quant_ker(*early[pair - 3])
+            if pair < KT // 2 - 1:
+                product(*early[pair - 2], nc.gpsimd, "pair%d" % (pair % 2), 1)
+        for k, h in ((8, 1), (10, 0), (11, 0), (9, 1), (10, 1), (11, 1)):
+            dots(k, h)
+        product(1, 1, nc.vector, "ker", 2)
         for b in range(B):
             witness(0, b, range(C - 1))
+        product(2, 0, nc.vector, "ker", 2)
+        quant_ker(1, 1)
         quant_ker(2, 0)
         for b in range(B):
             witness(0, b, [C - 1])
-        product(2, 1)
+        product(2, 1, nc.vector, "ker", 2)
         for b in range(B):
             emit(0, b, False)
         for b in range(B):

@@ -15,6 +15,7 @@ FP8 = mybir.dt.float8_e4m3fn
 FP8X4 = mybir.dt.float8_e4m3fn_x4
 FP4X4 = mybir.dt.float4_e2m1fn_x4
 MULT = mybir.AluOpType.mult
+ADD = mybir.AluOpType.add
 SQUARE = mybir.ActivationFunctionType.Square
 IDENTITY = mybir.ActivationFunctionType.Identity
 
@@ -28,7 +29,7 @@ JT = HN // P
 KT = C * PACK
 B = R // P
 BANK = 512
-ON_VECTOR = 2
+SHARE = 352
 
 
 def tile_kid_bootstrap_witness_s13_kernel(tc, gen_bytes, gen_scale, real, imp, mult_words, mult_scales, out):
@@ -36,7 +37,7 @@ def tile_kid_bootstrap_witness_s13_kernel(tc, gen_bytes, gen_scale, real, imp, m
     with ExitStack() as ctx:
         keep = ctx.enter_context(tc.tile_pool(name="keep", bufs=1))
         work = ctx.enter_context(tc.tile_pool(name="work", bufs=1))
-        psum = ctx.enter_context(tc.psum_pool(name="psum", bufs=8))
+        psum = ctx.enter_context(tc.psum_pool(name="psum", bufs=4))
         ctx.enter_context(tc.manual_schedule())
 
         ident = keep.tile([P, P], F32, name="ident")
@@ -75,16 +76,21 @@ def tile_kid_bootstrap_witness_s13_kernel(tc, gen_bytes, gen_scale, real, imp, m
 
         wide = {}
 
-        def widen(k):
+        def widen(k, *copies):
             tile = work.tile([P, D], BF16, name="wide", bufs=4)
-            if k < ON_VECTOR:
-                nc.vector.tensor_copy(out=tile[:], in_=gen_tiles[k][:].bitcast(FP8))
-            else:
-                nc.scalar.copy(out=tile[:], in_=gen_tiles[k][:].bitcast(FP8))
-            wide[k] = tile
+            for i, copy in enumerate(copies):
+                cols = slice(i * D // len(copies), (i + 1) * D // len(copies))
+                copy(out=tile[:, cols], in_=gen_tiles[k][:, cols].bitcast(FP8))
+            wide[k] = tile[:]
 
-        def turn(words, x, window):
-            bank = psum.tile([P, BANK], F32, name="bank")
+        def widen_pair(pair):
+            tile = work.tile([P, 2, D], BF16, name="wide_pair", tag="pair%d" % (pair % 2), bufs=1, align_bytes=64)
+            for i in range(2):
+                nc.gpsimd.tensor_copy(out=tile[:, i], in_=gen_tiles[2 * pair + i][:].bitcast(FP8))
+                wide[2 * pair + i] = tile[:, i]
+
+        def turn(words, x, window, tag):
+            bank = psum.tile([P, BANK], F32, name="bank", tag=tag)
             for i in range(2):
                 for u in range(2):
                     col = (2 * u + i) * P
@@ -106,12 +112,12 @@ def tile_kid_bootstrap_witness_s13_kernel(tc, gen_bytes, gen_scale, real, imp, m
         turned = {}
 
         def turn_gen(k):
-            turned[k] = [turn(wide[k][:].bitcast(F32), x, every_second) for x in range(2)]
+            turned[k] = [turn(wide[k].bitcast(F32), x, every_second, "held") for x in range(2)]
 
-        def scale_gen(k):
+        def scale_gen(k, order=(1, 0)):
             if k % 2 == 0:
                 gen_grouped[k // 2] = work.tile([P, 2 * G, P, PACK], BF16, name="gen_grouped", tag="pair%d" % (k // 2 % 2), bufs=1, align_bytes=64)
-            for x in (1, 0):
+            for x in order:
                 first = G * (k % 2) + 2 * x
                 values = turned[k][x][:].bitcast(BF16).rearrange("p (u g r e) -> p g r u e", g=2, u=2, e=2)
                 by_k = scale_cols[:, 2 * x : 2 * x + 2].rearrange("p g (u e) -> p g u e", u=2).unsqueeze(2).to_broadcast([P, 2, P, 2, 2])
@@ -123,7 +129,7 @@ def tile_kid_bootstrap_witness_s13_kernel(tc, gen_bytes, gen_scale, real, imp, m
             if h not in real_grouped:
                 real_grouped[h] = work.tile([P, G, HN, PACK], BF16, name="real_grouped", tag="stage", bufs=5, align_bytes=64)
             r0 = (j % JT) * P
-            banks = [turn(real_tiles[j][:].bitcast(F32), x, every_second) for x in range(2)]
+            banks = [turn(real_tiles[j][:].bitcast(F32), x, every_second, "passing") for x in range(2)]
             for x in (1, 0):
                 nc.scalar.copy(out=as_words(real_grouped[h])[:, 2 * x : 2 * x + 2, r0 : r0 + P], in_=untangle(banks[x]))
 
@@ -137,18 +143,17 @@ def tile_kid_bootstrap_witness_s13_kernel(tc, gen_bytes, gen_scale, real, imp, m
             for i in range(2):
                 gcodes[2 * pair + i] = (codes[:, i], scales[:, i])
 
-        def quant_real(h):
-            for x in range(2):
-                pair = slice(2 * x, 2 * x + 2)
-                nc.vector.quantize_mx(out=rcodes[:, h, pair].rearrange("p g n -> p (g n)").bitcast(FP8X4),
-                                      scales=rscales[:, h, pair].rearrange("p g n -> p (g n)"),
-                                      in_=real_grouped[h][:, pair].rearrange("p g r t -> p (g r t)"))
+        def quant_real(h, x):
+            pair = slice(2 * x, 2 * x + 2)
+            nc.vector.quantize_mx(out=rcodes[:, h, pair].rearrange("p g n -> p (g n)").bitcast(FP8X4),
+                                  scales=rscales[:, h, pair].rearrange("p g n -> p (g n)"),
+                                  in_=real_grouped[h][:, pair].rearrange("p g r t -> p (g r t)"))
 
         factors = {}
 
-        def dots(k, h):
+        def dots(k, h, share=False):
             codes, scales = gcodes[k]
-            bank = psum.tile([P, BANK], F32, name="bank")
+            bank = psum.tile([P, BANK], F32, name="bank", tag="passing")
             for g in range(G):
                 m = slice(g * P, (g + 1) * P)
                 nc.tensor.matmul_mx(out=bank[:], lhsT=codes[:, m].bitcast(FP8X4), lhsT_scale=scales[:, m],
@@ -159,18 +164,27 @@ def tile_kid_bootstrap_witness_s13_kernel(tc, gen_bytes, gen_scale, real, imp, m
                 factors[c, h] = work.tile([P, 2, PACK, HN], F32, name="factors", tag="stage", bufs=5, align_bytes=64)
             pair = factors[c, h]
             nc.scalar.activation(out=pair[:, 0, t], in_=bank[:], func=SQUARE, bias=1.0)
-            nc.scalar.activation(out=pair[:, 1, t], in_=bank[:], func=IDENTITY, scale=imp32[:, k : k + 1], bias=imp32[:, k : k + 1])
+            if share:
+                nc.vector.tensor_scalar(out=pair[:, 1, t], in0=bank[:], scalar1=1.0, scalar2=imp32[:, k : k + 1], op0=ADD, op1=MULT)
+            else:
+                nc.scalar.activation(out=pair[:, 1, t], in_=bank[:], func=IDENTITY, scale=imp32[:, k : k + 1], bias=imp32[:, k : k + 1])
 
         ker = {}
         kcodes = {}
 
-        def product(c, h, engine, tag, bufs):
+        def multiply(engine, c, h, cols):
             pair = factors[c, h]
-            tile = work.tile([P, HN, PACK], BF16, name="ker", tag=tag, bufs=bufs, align_bytes=64)
-            engine.tensor_tensor(out=tile[:].rearrange("p (n i) t -> p n t i", i=2),
-                                    in0=pair[:, 0].rearrange("p t (n i) -> p n t i", i=2),
-                                    in1=pair[:, 1].rearrange("p t (n i) -> p n t i", i=2), op=MULT)
-            ker[c, h] = tile
+            engine.tensor_tensor(out=ker[c, h][:, cols].rearrange("p (n i) t -> p n t i", i=2),
+                                 in0=pair[:, 0, :, cols].rearrange("p t (n i) -> p n t i", i=2),
+                                 in1=pair[:, 1, :, cols].rearrange("p t (n i) -> p n t i", i=2), op=MULT)
+
+        def product(c, h):
+            ker[c, h] = work.tile([P, HN, PACK], BF16, name="ker", bufs=2, align_bytes=64)
+            multiply(nc.vector, c, h, slice(0, HN))
+
+        def product_aside(c, h, pair):
+            ker[c, h] = work.tile([P, HN, PACK], BF16, name="ker_aside", tag="pair%d" % (pair % 2), bufs=1, align_bytes=64)
+            multiply(nc.gpsimd, c, h, slice(0, SHARE))
 
         def quant_ker(c, h):
             codes = work.tile([P, HN], U32, name="kcodes", bufs=C * H, align_bytes=64)
@@ -182,7 +196,7 @@ def tile_kid_bootstrap_witness_s13_kernel(tc, gen_bytes, gen_scale, real, imp, m
 
         def witness(h, b, chunks):
             if (h, b) not in sums:
-                sums[h, b] = psum.tile([P, BANK], F32, name="bank")
+                sums[h, b] = psum.tile([P, BANK], F32, name="bank", tag=("held", "passing")[h])
             for c in chunks:
                 codes, scales = kcodes[c, h]
                 nc.tensor.matmul_mx(out=sums[h, b][:], lhsT=wwords[:, c, 2 * P * b : 2 * P * (b + 1)].bitcast(FP4X4),
@@ -199,68 +213,97 @@ def tile_kid_bootstrap_witness_s13_kernel(tc, gen_bytes, gen_scale, real, imp, m
             nc.sync.dma_start(out=out[b * P : (b + 1) * P, h * HN : (h + 1) * HN], in_=tile[:])
 
         nc.scalar.dma_start(out=imp_raw[:], in_=imp.rearrange("(c p t) -> p c t", p=P, t=PACK))
-        load_real(0)
         load_gen(0)
         load_gen(1)
+        load_real(0)
+        load_gen(2)
         load_real(1)
-        for pair in range(1, H * JT // 2):
-            load_gen(pair + 1)
-            load_real(2 * pair)
-            load_real(2 * pair + 1)
-        for k in range(5, 8):
-            load_gen(k)
+        load_gen(3)
+        load_gen(4)
+        load_real(2)
+        load_real(3)
+        load_gen(5)
+        for j in range(JT, H * JT):
+            load_real(j)
+        load_gen(6)
+        load_gen(7)
 
         nc.scalar.activation(out=imp32[:], in_=imp_raw[:].rearrange("p c t -> p (c t)"), func=IDENTITY)
-        widen(0)
-        widen(1)
-        for k in range(PACK):
-            turn_real(2 * k)
-            turn_gen(k)
-            turn_real(2 * k + 1)
-            scale_gen(k)
-            widen(k + 2)
-            load_gen(k + 8)
-            if k == 1:
-                quant_gen(0)
-            if k == 2:
-                quant_real(0)
+        widen(0, nc.vector.tensor_copy, nc.scalar.copy)
+        widen(1, nc.scalar.copy)
+        turn_gen(0)
+        turn_gen(1)
+        widen(2, nc.scalar.copy)
+        widen(3, nc.scalar.copy)
+        for k in range(2):
+            scale_gen(k, (0, 1))
+            turn_real(k)
+            turn_gen(k + 2)
+        turn_real(2)
+        turn_real(3)
+        scale_gen(2)
+        scale_gen(3)
+        widen(4, nc.gpsimd.tensor_copy)
+        widen(5, nc.gpsimd.tensor_copy)
+        for k in range(8, KT):
+            load_gen(k)
         load_mult()
-        dots(0, 0)
-        dots(1, 0)
+        turn_real(4)
+        turn_real(5)
+        turn_gen(4)
+        turn_gen(5)
+        quant_gen(0)
+        quant_real(0, 0)
         quant_gen(1)
-        quant_real(1)
-        early = [(0, 0), (0, 1), (1, 0)]
-        for pair in range(2, KT // 2):
+        widen_pair(3)
+        quant_real(0, 1)
+        scale_gen(4)
+        scale_gen(5)
+        turn_real(6)
+        turn_real(7)
+        for k in range(PACK):
+            dots(k, 0)
+        quant_real(1, 0)
+        quant_gen(2)
+        product_aside(0, 0, 2)
+        quant_real(1, 1)
+        early = [(0, 0), (0, 1), (1, 0), (1, 1)]
+        for pair in range(3, KT // 2):
             turn_gen(2 * pair)
             turn_gen(2 * pair + 1)
-            if pair + 1 < KT // 2:
-                widen(2 * pair + 2)
-                widen(2 * pair + 3)
+            if pair < KT // 2 - 1:
+                widen(2 * pair + 2, nc.scalar.copy)
+                widen(2 * pair + 3, nc.scalar.copy)
             scale_gen(2 * pair)
             scale_gen(2 * pair + 1)
-            groups = [((2 * pair - 2, 0), (2 * pair - 1, 0)), ((2 * pair - 4, 1), (2 * pair - 3, 1))]
-            for group in groups[:: -1 if pair % 2 else 1]:
-                for k, h in group:
-                    dots(k, h)
+            c, h = early[pair - 2]
+            for t in range(PACK):
+                dots(PACK * c + t, h)
+            multiply(nc.vector, *early[pair - 3], slice(SHARE, HN))
             quant_gen(pair)
-            if pair >= 3:
-                quant_ker(*early[pair - 3])
             if pair < KT // 2 - 1:
-                product(*early[pair - 2], nc.gpsimd, "pair%d" % (pair % 2), 1)
-        for k, h in ((8, 1), (10, 0), (11, 0), (9, 1), (10, 1), (11, 1)):
+                product_aside(c, h, pair)
+            quant_ker(*early[pair - 3])
+        for k, h in ((8, 0), (9, 0), (8, 1)):
             dots(k, h)
-        product(1, 1, nc.vector, "ker", 2)
+        product(1, 1)
+        for k, h in ((10, 0), (11, 0)):
+            dots(k, h, (k, h) in ())
+        quant_ker(1, 1)
+        product(2, 0)
+        for k, h in ((9, 1), (10, 1), (11, 1)):
+            dots(k, h, (k, h) in ())
         for b in range(B):
             witness(0, b, range(C - 1))
-        product(2, 0, nc.vector, "ker", 2)
-        quant_ker(1, 1)
         quant_ker(2, 0)
+        for b in range(B // 2):
+            witness(1, b, range(C - 1))
         for b in range(B):
-            witness(0, b, [C - 1])
-        product(2, 1, nc.vector, "ker", 2)
+            witness(0, b, [2])
+        product(2, 1)
         for b in range(B):
             emit(0, b, False)
-        for b in range(B):
+        for b in range(B // 2, B):
             witness(1, b, range(C - 1))
         quant_ker(2, 1)
         for b in range(B):

@@ -29,7 +29,7 @@ JT = HN // P
 KT = C * PACK
 B = R // P
 BANK = 512
-SHARE = 352
+SHARE = 416
 
 
 def tile_kid_bootstrap_witness_s13_kernel(tc, gen_bytes, gen_scale, real, imp, mult_words, mult_scales, out):
@@ -57,9 +57,11 @@ def tile_kid_bootstrap_witness_s13_kernel(tc, gen_bytes, gen_scale, real, imp, m
         gen_tiles = {}
         real_tiles = {}
 
-        def load_gen(k):
+        def load_gen(k, parts=1):
             tile = work.tile([P, D], U8, name="gen_in", bufs=8)
-            nc.sync.dma_start(out=tile[:], in_=gen_rows[k // PACK][:, k % PACK])
+            for i in range(parts):
+                cols = slice(i * D // parts, (i + 1) * D // parts)
+                nc.sync.dma_start(out=tile[:, cols], in_=gen_rows[k // PACK][:, k % PACK, cols])
             gen_tiles[k] = tile
 
         def load_real(j):
@@ -100,6 +102,16 @@ def tile_kid_bootstrap_witness_s13_kernel(tc, gen_bytes, gen_scale, real, imp, m
         def every_second(g, u):
             return slice(256 * g + u, 256 * g + u + 255, 2)
 
+        def in_a_run(g, u):
+            return slice(512 * u + P * g, 512 * u + P * (g + 1))
+
+        sorted_rows = {}
+
+        def sort_real(j, copy, dtype):
+            tile = work.tile([P, 2, D // PACK], dtype, name="sorted_rows", bufs=2)
+            copy(out=tile[:], in_=real_tiles[j][:].bitcast(dtype).rearrange("p (w u) -> p u w", u=2))
+            sorted_rows[j] = tile[:].rearrange("p u w -> p (u w)").bitcast(F32)
+
         def untangle(bank):
             return bank[:].rearrange("p (u g r) -> p g r u", g=2, u=2)
 
@@ -129,8 +141,9 @@ def tile_kid_bootstrap_witness_s13_kernel(tc, gen_bytes, gen_scale, real, imp, m
             if h not in real_grouped:
                 real_grouped[h] = work.tile([P, G, HN, PACK], BF16, name="real_grouped", tag="stage", bufs=5, align_bytes=64)
             r0 = (j % JT) * P
-            banks = [turn(real_tiles[j][:].bitcast(F32), x, every_second, "passing") for x in range(2)]
-            for x in (1, 0):
+            words, window = (sorted_rows[j], in_a_run) if j in sorted_rows else (real_tiles[j][:].bitcast(F32), every_second)
+            banks = [turn(words, x, window, "passing") for x in range(2)]
+            for x in (0, 1):
                 nc.scalar.copy(out=as_words(real_grouped[h])[:, 2 * x : 2 * x + 2, r0 : r0 + P], in_=untangle(banks[x]))
 
         gcodes = {}
@@ -151,7 +164,7 @@ def tile_kid_bootstrap_witness_s13_kernel(tc, gen_bytes, gen_scale, real, imp, m
 
         factors = {}
 
-        def dots(k, h, share=False):
+        def inner_products(k, h):
             codes, scales = gcodes[k]
             bank = psum.tile([P, BANK], F32, name="bank", tag="passing")
             for g in range(G):
@@ -159,6 +172,10 @@ def tile_kid_bootstrap_witness_s13_kernel(tc, gen_bytes, gen_scale, real, imp, m
                 nc.tensor.matmul_mx(out=bank[:], lhsT=codes[:, m].bitcast(FP8X4), lhsT_scale=scales[:, m],
                                     rhs=rcodes[:, h, g].bitcast(FP8X4), rhs_scale=rscales[:, h, g],
                                     start=(g == 0), stop=(g == G - 1))
+            return bank
+
+        def dots(k, h, share=False):
+            bank = inner_products(k, h)
             c, t = k // PACK, k % PACK
             if (c, h) not in factors:
                 factors[c, h] = work.tile([P, 2, PACK, HN], F32, name="factors", tag="stage", bufs=5, align_bytes=64)
@@ -172,11 +189,11 @@ def tile_kid_bootstrap_witness_s13_kernel(tc, gen_bytes, gen_scale, real, imp, m
         ker = {}
         kcodes = {}
 
-        def multiply(engine, c, h, cols):
+        def multiply(engine, c, h, cols, run=2):
             pair = factors[c, h]
-            engine.tensor_tensor(out=ker[c, h][:, cols].rearrange("p (n i) t -> p n t i", i=2),
-                                 in0=pair[:, 0, :, cols].rearrange("p t (n i) -> p n t i", i=2),
-                                 in1=pair[:, 1, :, cols].rearrange("p t (n i) -> p n t i", i=2), op=MULT)
+            engine.tensor_tensor(out=ker[c, h][:, cols].rearrange("p (n i) t -> p n t i", i=run),
+                                 in0=pair[:, 0, :, cols].rearrange("p t (n i) -> p n t i", i=run),
+                                 in1=pair[:, 1, :, cols].rearrange("p t (n i) -> p n t i", i=run), op=MULT)
 
         def product(c, h):
             ker[c, h] = work.tile([P, HN, PACK], BF16, name="ker", bufs=2, align_bytes=64)
@@ -184,7 +201,7 @@ def tile_kid_bootstrap_witness_s13_kernel(tc, gen_bytes, gen_scale, real, imp, m
 
         def product_aside(c, h, pair):
             ker[c, h] = work.tile([P, HN, PACK], BF16, name="ker_aside", tag="pair%d" % (pair % 2), bufs=1, align_bytes=64)
-            multiply(nc.gpsimd, c, h, slice(0, SHARE))
+            multiply(nc.gpsimd, c, h, slice(0, SHARE), 1)
 
         def quant_ker(c, h):
             codes = work.tile([P, HN], U32, name="kcodes", bufs=C * H, align_bytes=64)
@@ -213,7 +230,7 @@ def tile_kid_bootstrap_witness_s13_kernel(tc, gen_bytes, gen_scale, real, imp, m
             nc.sync.dma_start(out=out[b * P : (b + 1) * P, h * HN : (h + 1) * HN], in_=tile[:])
 
         nc.scalar.dma_start(out=imp_raw[:], in_=imp.rearrange("(c p t) -> p c t", p=P, t=PACK))
-        load_gen(0)
+        load_gen(0, 2)
         load_gen(1)
         load_real(0)
         load_gen(2)
@@ -267,6 +284,7 @@ def tile_kid_bootstrap_witness_s13_kernel(tc, gen_bytes, gen_scale, real, imp, m
         quant_gen(2)
         product_aside(0, 0, 2)
         quant_real(1, 1)
+        groups = [[(k, 1) for k in range(4)], [(k, 0) for k in range(4, 8)], [(k, 1) for k in range(4, 8)]]
         early = [(0, 0), (0, 1), (1, 0), (1, 1)]
         for pair in range(3, KT // 2):
             turn_gen(2 * pair)
@@ -276,23 +294,23 @@ def tile_kid_bootstrap_witness_s13_kernel(tc, gen_bytes, gen_scale, real, imp, m
                 widen(2 * pair + 3, nc.scalar.copy)
             scale_gen(2 * pair)
             scale_gen(2 * pair + 1)
-            c, h = early[pair - 2]
-            for t in range(PACK):
-                dots(PACK * c + t, h)
+            for k, h in groups[pair - 3]:
+                dots(k, h)
             multiply(nc.vector, *early[pair - 3], slice(SHARE, HN))
             quant_gen(pair)
             if pair < KT // 2 - 1:
-                product_aside(c, h, pair)
-            quant_ker(*early[pair - 3])
+                product_aside(*early[pair - 2], pair)
+                quant_ker(*early[pair - 3])
         for k, h in ((8, 0), (9, 0), (8, 1)):
-            dots(k, h)
+            dots(k, h, (k, h) in ((10, 0), (11, 0)))
         product(1, 1)
-        for k, h in ((10, 0), (11, 0)):
-            dots(k, h, (k, h) in ())
+        quant_ker(1, 0)
         quant_ker(1, 1)
+        for k, h in ((10, 0), (11, 0)):
+            dots(k, h, (k, h) in ((10, 0), (11, 0)))
         product(2, 0)
         for k, h in ((9, 1), (10, 1), (11, 1)):
-            dots(k, h, (k, h) in ())
+            dots(k, h, (k, h) in ((10, 0), (11, 0)))
         for b in range(B):
             witness(0, b, range(C - 1))
         quant_ker(2, 0)

@@ -29,7 +29,7 @@ JT = HN // P
 KT = C * PACK
 B = R // P
 BANK = 512
-SHARE = 416
+SHARE = 448
 
 
 def tile_kid_bootstrap_witness_s13_kernel(tc, gen_bytes, gen_scale, real, imp, mult_words, mult_scales, out):
@@ -201,7 +201,7 @@ def tile_kid_bootstrap_witness_s13_kernel(tc, gen_bytes, gen_scale, real, imp, m
 
         def product_aside(c, h, pair):
             ker[c, h] = work.tile([P, HN, PACK], BF16, name="ker_aside", tag="pair%d" % (pair % 2), bufs=1, align_bytes=64)
-            multiply(nc.gpsimd, c, h, slice(0, SHARE), 1)
+            multiply(nc.gpsimd, c, h, slice(0, SHARE), 4)
 
         def quant_ker(c, h):
             codes = work.tile([P, HN], U32, name="kcodes", bufs=C * H, align_bytes=64)

@@ -58,11 +58,17 @@ def tile_kid_bootstrap_witness_s13_kernel(tc, gen_bytes, gen_scale, real, imp, m
         real_tiles = {}
 
         def load_gen(k, parts=1):
-            tile = work.tile([P, D], U8, name="gen_in", bufs=8)
+            tile = work.tile([P, D], U8, name="gen_in", bufs=6)
             for i in range(parts):
                 cols = slice(i * D // parts, (i + 1) * D // parts)
                 nc.sync.dma_start(out=tile[:, cols], in_=gen_rows[k // PACK][:, k % PACK, cols])
             gen_tiles[k] = tile
+
+        def load_gen_pair(pair):
+            tile = work.tile([P, 2, D], U8, name="gen_pair_in")
+            t = 2 * pair % PACK
+            nc.sync.dma_start(out=tile[:], in_=gen_rows[2 * pair // PACK][:, t : t + 2])
+            gen_tiles[2 * pair, 2 * pair + 1] = tile
 
         def load_real(j):
             tile = work.tile([P, D], BF16, name="real_in", tag="rows", bufs=8)
@@ -87,8 +93,9 @@ def tile_kid_bootstrap_witness_s13_kernel(tc, gen_bytes, gen_scale, real, imp, m
 
         def widen_pair(pair):
             tile = work.tile([P, 2, D], BF16, name="wide_pair", tag="pair%d" % (pair % 2), bufs=1, align_bytes=64)
+            nc.gpsimd.tensor_copy(out=tile[:].rearrange("p i k -> p (i k)"),
+                                  in_=gen_tiles[2 * pair, 2 * pair + 1][:].rearrange("p i k -> p (i k)").bitcast(FP8))
             for i in range(2):
-                nc.gpsimd.tensor_copy(out=tile[:, i], in_=gen_tiles[2 * pair + i][:].bitcast(FP8))
                 wide[2 * pair + i] = tile[:, i]
 
         def turn(words, x, window, tag):
@@ -221,13 +228,13 @@ def tile_kid_bootstrap_witness_s13_kernel(tc, gen_bytes, gen_scale, real, imp, m
                                     rhs=codes[:].bitcast(FP8X4), rhs_scale=scales[:],
                                     start=(c == 0), stop=(c == C - 1))
 
-        def emit(h, b, on_vector):
+        def emit(h, b, on_vector, parts=1):
             tile = work.tile([P, HN], F32, name="result", tag="rows", bufs=8)
-            if on_vector:
-                nc.vector.tensor_copy(out=tile[:], in_=sums[h, b][:])
-            else:
-                nc.scalar.copy(out=tile[:], in_=sums[h, b][:])
-            nc.sync.dma_start(out=out[b * P : (b + 1) * P, h * HN : (h + 1) * HN], in_=tile[:])
+            copy = nc.vector.tensor_copy if on_vector else nc.scalar.copy
+            for i in range(parts):
+                cols = slice(i * HN // parts, (i + 1) * HN // parts)
+                copy(out=tile[:, cols], in_=sums[h, b][:, cols])
+                nc.sync.dma_start(out=out[b * P : (b + 1) * P, h * HN : (h + 1) * HN][:, cols], in_=tile[:, cols])
 
         nc.scalar.dma_start(out=imp_raw[:], in_=imp.rearrange("(c p t) -> p c t", p=P, t=PACK))
         load_gen(0, 2)
@@ -242,11 +249,10 @@ def tile_kid_bootstrap_witness_s13_kernel(tc, gen_bytes, gen_scale, real, imp, m
         load_gen(5)
         for j in range(JT, H * JT):
             load_real(j)
-        load_gen(6)
-        load_gen(7)
+        load_gen_pair(3)
 
         nc.scalar.activation(out=imp32[:], in_=imp_raw[:].rearrange("p c t -> p (c t)"), func=IDENTITY)
-        widen(0, nc.vector.tensor_copy, nc.scalar.copy)
+        widen(0, nc.vector.tensor_copy, nc.scalar.copy, nc.vector.tensor_copy, nc.scalar.copy)
         widen(1, nc.scalar.copy)
         turn_gen(0)
         turn_gen(1)
@@ -314,16 +320,16 @@ def tile_kid_bootstrap_witness_s13_kernel(tc, gen_bytes, gen_scale, real, imp, m
         for b in range(B):
             witness(0, b, range(C - 1))
         quant_ker(2, 0)
-        for b in range(B // 2):
+        for b in range(1):
             witness(1, b, range(C - 1))
         for b in range(B):
             witness(0, b, [2])
         product(2, 1)
         for b in range(B):
             emit(0, b, False)
-        for b in range(B // 2, B):
+        for b in range(1, B):
             witness(1, b, range(C - 1))
         quant_ker(2, 1)
         for b in range(B):
             witness(1, b, [C - 1])
-            emit(1, b, b % 2 == 1)
+            emit(1, b, b % 2 == 1, 2 if b == 0 else 1)

@@ -29,7 +29,7 @@ JT = HN // P
 KT = C * PACK
 B = R // P
 BANK = 512
-SHARE = 448
+SHARE = 432
 
 
 def tile_kid_bootstrap_witness_s13_kernel(tc, gen_bytes, gen_scale, real, imp, mult_words, mult_scales, out):
@@ -55,20 +55,23 @@ def tile_kid_bootstrap_witness_s13_kernel(tc, gen_bytes, gen_scale, real, imp, m
 
         gen_rows = gen_bytes.rearrange("(c p t) k -> c p t k", p=P, t=PACK)
         gen_tiles = {}
+        gen_pairs = {}
         real_tiles = {}
 
         def load_gen(k, parts=1):
-            tile = work.tile([P, D], U8, name="gen_in", bufs=6)
+            tile = work.tile([P, D], U8, name="gen_in", bufs=4)
             for i in range(parts):
                 cols = slice(i * D // parts, (i + 1) * D // parts)
                 nc.sync.dma_start(out=tile[:, cols], in_=gen_rows[k // PACK][:, k % PACK, cols])
-            gen_tiles[k] = tile
+            gen_tiles[k] = tile[:]
 
         def load_gen_pair(pair):
-            tile = work.tile([P, 2, D], U8, name="gen_pair_in")
+            tile = work.tile([P, 2, D], U8, name="gen_pair_in", bufs=3)
             t = 2 * pair % PACK
             nc.sync.dma_start(out=tile[:], in_=gen_rows[2 * pair // PACK][:, t : t + 2])
-            gen_tiles[2 * pair, 2 * pair + 1] = tile
+            gen_pairs[pair] = tile
+            for i in range(2):
+                gen_tiles[2 * pair + i] = tile[:, i]
 
         def load_real(j):
             tile = work.tile([P, D], BF16, name="real_in", tag="rows", bufs=8)
@@ -91,10 +94,10 @@ def tile_kid_bootstrap_witness_s13_kernel(tc, gen_bytes, gen_scale, real, imp, m
                 copy(out=tile[:, cols], in_=gen_tiles[k][:, cols].bitcast(FP8))
             wide[k] = tile[:]
 
-        def widen_pair(pair):
-            tile = work.tile([P, 2, D], BF16, name="wide_pair", tag="pair%d" % (pair % 2), bufs=1, align_bytes=64)
+        def widen_pair(pair, tag, bufs):
+            tile = work.tile([P, 2, D], BF16, name="wide_pair", tag=tag, bufs=bufs, align_bytes=64)
             nc.gpsimd.tensor_copy(out=tile[:].rearrange("p i k -> p (i k)"),
-                                  in_=gen_tiles[2 * pair, 2 * pair + 1][:].rearrange("p i k -> p (i k)").bitcast(FP8))
+                                  in_=gen_pairs[pair][:].rearrange("p i k -> p (i k)").bitcast(FP8))
             for i in range(2):
                 wide[2 * pair + i] = tile[:, i]
 
@@ -243,17 +246,14 @@ def tile_kid_bootstrap_witness_s13_kernel(tc, gen_bytes, gen_scale, real, imp, m
         load_gen(2)
         load_real(1)
         load_gen(3)
-        load_gen(4)
-        load_real(2)
-        load_real(3)
-        load_gen(5)
-        for j in range(JT, H * JT):
+        load_gen_pair(2)
+        for j in range(2, H * JT):
             load_real(j)
         load_gen_pair(3)
 
         nc.scalar.activation(out=imp32[:], in_=imp_raw[:].rearrange("p c t -> p (c t)"), func=IDENTITY)
         widen(0, nc.vector.tensor_copy, nc.scalar.copy, nc.vector.tensor_copy, nc.scalar.copy)
-        widen(1, nc.scalar.copy)
+        widen(1, nc.vector.tensor_copy, nc.scalar.copy)
         turn_gen(0)
         turn_gen(1)
         widen(2, nc.scalar.copy)
@@ -266,10 +266,9 @@ def tile_kid_bootstrap_witness_s13_kernel(tc, gen_bytes, gen_scale, real, imp, m
         turn_real(3)
         scale_gen(2)
         scale_gen(3)
-        widen(4, nc.gpsimd.tensor_copy)
-        widen(5, nc.gpsimd.tensor_copy)
-        for k in range(8, KT):
-            load_gen(k)
+        widen_pair(2, "stage", 5)
+        load_gen_pair(4)
+        load_gen_pair(5)
         load_mult()
         turn_real(4)
         turn_real(5)
@@ -278,12 +277,13 @@ def tile_kid_bootstrap_witness_s13_kernel(tc, gen_bytes, gen_scale, real, imp, m
         quant_gen(0)
         quant_real(0, 0)
         quant_gen(1)
-        widen_pair(3)
+        widen_pair(3, "pair1", 1)
         quant_real(0, 1)
         scale_gen(4)
         scale_gen(5)
         turn_real(6)
         turn_real(7)
+        widen(8, nc.scalar.copy)
         for k in range(PACK):
             dots(k, 0)
         quant_real(1, 0)
@@ -296,7 +296,8 @@ def tile_kid_bootstrap_witness_s13_kernel(tc, gen_bytes, gen_scale, real, imp, m
             turn_gen(2 * pair)
             turn_gen(2 * pair + 1)
             if pair < KT // 2 - 1:
-                widen(2 * pair + 2, nc.scalar.copy)
+                if pair > 3:
+                    widen(2 * pair + 2, nc.scalar.copy)
                 widen(2 * pair + 3, nc.scalar.copy)
             scale_gen(2 * pair)
             scale_gen(2 * pair + 1)

@@ -27,8 +27,10 @@ H = 2
 HN = N // H
 JT = HN // P
 KT = C * PACK
+PAIRS = KT // 2
 B = R // P
 BANK = 512
+STAGE_BUFS = 5
 SHARE = 432
 
 
@@ -59,7 +61,7 @@ def tile_kid_bootstrap_witness_s13_kernel(tc, gen_bytes, gen_scale, real, imp, m
         real_tiles = {}
 
         def load_gen(k, parts=1):
-            tile = work.tile([P, D], U8, name="gen_in", bufs=4)
+            tile = work.tile([P, D], U8, name="gen_in", bufs=PACK)
             for i in range(parts):
                 cols = slice(i * D // parts, (i + 1) * D // parts)
                 nc.sync.dma_start(out=tile[:, cols], in_=gen_rows[k // PACK][:, k % PACK, cols])
@@ -74,7 +76,7 @@ def tile_kid_bootstrap_witness_s13_kernel(tc, gen_bytes, gen_scale, real, imp, m
                 gen_tiles[2 * pair + i] = tile[:, i]
 
         def load_real(j):
-            tile = work.tile([P, D], BF16, name="real_in", tag="rows", bufs=8)
+            tile = work.tile([P, D], BF16, name="real_in", tag="rows", bufs=H * JT)
             nc.sync.dma_start(out=tile[:], in_=real[j * P : (j + 1) * P, :])
             real_tiles[j] = tile
 
@@ -88,7 +90,7 @@ def tile_kid_bootstrap_witness_s13_kernel(tc, gen_bytes, gen_scale, real, imp, m
         wide = {}
 
         def widen(k, *copies):
-            tile = work.tile([P, D], BF16, name="wide", bufs=4)
+            tile = work.tile([P, D], BF16, name="wide", bufs=PACK)
             for i, copy in enumerate(copies):
                 cols = slice(i * D // len(copies), (i + 1) * D // len(copies))
                 copy(out=tile[:, cols], in_=gen_tiles[k][:, cols].bitcast(FP8))
@@ -101,60 +103,47 @@ def tile_kid_bootstrap_witness_s13_kernel(tc, gen_bytes, gen_scale, real, imp, m
             for i in range(2):
                 wide[2 * pair + i] = tile[:, i]
 
-        def turn(words, x, window, tag):
-            bank = psum.tile([P, BANK], F32, name="bank", tag=tag)
-            for i in range(2):
-                for u in range(2):
-                    col = (2 * u + i) * P
-                    nc.tensor.transpose(bank[:, col : col + P], words[:, window(2 * x + i, u)], ident[:])
-            return bank
+        def turn(rows, tag):
+            words = rows.bitcast(F32)
+            banks = []
+            for x in range(2):
+                bank = psum.tile([P, BANK], F32, name="bank", tag=tag)
+                for i in range(2):
+                    for u in range(2):
+                        first = 2 * P * (2 * x + i) + u
+                        col = (2 * u + i) * P
+                        nc.tensor.transpose(bank[:, col : col + P], words[:, first : first + 2 * P - 1 : 2], ident[:])
+                banks.append(bank)
+            return banks
 
-        def every_second(g, u):
-            return slice(256 * g + u, 256 * g + u + 255, 2)
+        def pair_tag(pair):
+            return "pair%d" % (pair % 2)
 
-        def in_a_run(g, u):
-            return slice(512 * u + P * g, 512 * u + P * (g + 1))
-
-        sorted_rows = {}
-
-        def sort_real(j, copy, dtype):
-            tile = work.tile([P, 2, D // PACK], dtype, name="sorted_rows", bufs=2)
-            copy(out=tile[:], in_=real_tiles[j][:].bitcast(dtype).rearrange("p (w u) -> p u w", u=2))
-            sorted_rows[j] = tile[:].rearrange("p u w -> p (u w)").bitcast(F32)
-
-        def untangle(bank):
-            return bank[:].rearrange("p (u g r) -> p g r u", g=2, u=2)
-
-        def as_words(tile, groups=G):
-            return tile[:].rearrange("p g r t -> p (g r t)").bitcast(F32).rearrange("p (g r u) -> p g r u", g=groups, u=2)
-
+        turned = {}
         gen_grouped = {}
         real_grouped = {}
 
-        turned = {}
-
         def turn_gen(k):
-            turned[k] = [turn(wide[k].bitcast(F32), x, every_second, "held") for x in range(2)]
+            turned[k] = turn(wide[k], "held")
 
         def scale_gen(k, order=(1, 0)):
             if k % 2 == 0:
-                gen_grouped[k // 2] = work.tile([P, 2 * G, P, PACK], BF16, name="gen_grouped", tag="pair%d" % (k // 2 % 2), bufs=1, align_bytes=64)
+                gen_grouped[k // 2] = work.tile([P, 2 * G, P, PACK], BF16, name="gen_grouped", tag=pair_tag(k // 2), bufs=1, align_bytes=64)
             for x in order:
-                first = G * (k % 2) + 2 * x
+                g0 = G * (k % 2) + 2 * x
                 values = turned[k][x][:].bitcast(BF16).rearrange("p (u g r e) -> p g r u e", g=2, u=2, e=2)
-                by_k = scale_cols[:, 2 * x : 2 * x + 2].rearrange("p g (u e) -> p g u e", u=2).unsqueeze(2).to_broadcast([P, 2, P, 2, 2])
-                nc.vector.tensor_tensor(out=gen_grouped[k // 2][:, first : first + 2].rearrange("p g r (u e) -> p g r u e", u=2),
-                                        in0=values, in1=by_k, op=MULT)
+                by_d = scale_cols[:, 2 * x : 2 * x + 2].rearrange("p g (u e) -> p g u e", u=2).unsqueeze(2).to_broadcast([P, 2, P, 2, 2])
+                nc.vector.tensor_tensor(out=gen_grouped[k // 2][:, g0 : g0 + 2].rearrange("p g r (u e) -> p g r u e", u=2),
+                                        in0=values, in1=by_d, op=MULT)
 
         def turn_real(j):
             h = j // JT
             if h not in real_grouped:
-                real_grouped[h] = work.tile([P, G, HN, PACK], BF16, name="real_grouped", tag="stage", bufs=5, align_bytes=64)
-            r0 = (j % JT) * P
-            words, window = (sorted_rows[j], in_a_run) if j in sorted_rows else (real_tiles[j][:].bitcast(F32), every_second)
-            banks = [turn(words, x, window, "passing") for x in range(2)]
-            for x in (0, 1):
-                nc.scalar.copy(out=as_words(real_grouped[h])[:, 2 * x : 2 * x + 2, r0 : r0 + P], in_=untangle(banks[x]))
+                real_grouped[h] = work.tile([P, G, HN, PACK], BF16, name="real_grouped", tag="stage", bufs=STAGE_BUFS, align_bytes=64)
+            words = real_grouped[h][:].rearrange("p g r t -> p (g r t)").bitcast(F32).rearrange("p (g r u) -> p g r u", g=G, u=2)
+            place = slice(j % JT * P, (j % JT + 1) * P)
+            for x, bank in enumerate(turn(real_tiles[j][:], "passing")):
+                nc.scalar.copy(out=words[:, 2 * x : 2 * x + 2, place], in_=bank[:].rearrange("p (u g r) -> p g r u", g=2, u=2))
 
         gcodes = {}
 
@@ -167,14 +156,14 @@ def tile_kid_bootstrap_witness_s13_kernel(tc, gen_bytes, gen_scale, real, imp, m
                 gcodes[2 * pair + i] = (codes[:, i], scales[:, i])
 
         def quant_real(h, x):
-            pair = slice(2 * x, 2 * x + 2)
-            nc.vector.quantize_mx(out=rcodes[:, h, pair].rearrange("p g n -> p (g n)").bitcast(FP8X4),
-                                  scales=rscales[:, h, pair].rearrange("p g n -> p (g n)"),
-                                  in_=real_grouped[h][:, pair].rearrange("p g r t -> p (g r t)"))
+            passes = slice(2 * x, 2 * x + 2)
+            nc.vector.quantize_mx(out=rcodes[:, h, passes].rearrange("p g n -> p (g n)").bitcast(FP8X4),
+                                  scales=rscales[:, h, passes].rearrange("p g n -> p (g n)"),
+                                  in_=real_grouped[h][:, passes].rearrange("p g r t -> p (g r t)"))
 
         factors = {}
 
-        def inner_products(k, h):
+        def dots(k, h, weighted_on_vector=False):
             codes, scales = gcodes[k]
             bank = psum.tile([P, BANK], F32, name="bank", tag="passing")
             for g in range(G):
@@ -182,35 +171,34 @@ def tile_kid_bootstrap_witness_s13_kernel(tc, gen_bytes, gen_scale, real, imp, m
                 nc.tensor.matmul_mx(out=bank[:], lhsT=codes[:, m].bitcast(FP8X4), lhsT_scale=scales[:, m],
                                     rhs=rcodes[:, h, g].bitcast(FP8X4), rhs_scale=rscales[:, h, g],
                                     start=(g == 0), stop=(g == G - 1))
-            return bank
-
-        def dots(k, h, share=False):
-            bank = inner_products(k, h)
             c, t = k // PACK, k % PACK
             if (c, h) not in factors:
-                factors[c, h] = work.tile([P, 2, PACK, HN], F32, name="factors", tag="stage", bufs=5, align_bytes=64)
-            pair = factors[c, h]
-            nc.scalar.activation(out=pair[:, 0, t], in_=bank[:], func=SQUARE, bias=1.0)
-            if share:
-                nc.vector.tensor_scalar(out=pair[:, 1, t], in0=bank[:], scalar1=1.0, scalar2=imp32[:, k : k + 1], op0=ADD, op1=MULT)
+                factors[c, h] = work.tile([P, 2, PACK, HN], F32, name="factors", tag="stage", bufs=STAGE_BUFS, align_bytes=64)
+            weight = imp32[:, k : k + 1]
+            nc.scalar.activation(out=factors[c, h][:, 0, t], in_=bank[:], func=SQUARE, bias=1.0)
+            if weighted_on_vector:
+                nc.vector.tensor_scalar(out=factors[c, h][:, 1, t], in0=bank[:], scalar1=1.0, scalar2=weight, op0=ADD, op1=MULT)
             else:
-                nc.scalar.activation(out=pair[:, 1, t], in_=bank[:], func=IDENTITY, scale=imp32[:, k : k + 1], bias=imp32[:, k : k + 1])
+                nc.scalar.activation(out=factors[c, h][:, 1, t], in_=bank[:], func=IDENTITY, scale=weight, bias=weight)
 
         ker = {}
         kcodes = {}
 
-        def multiply(engine, c, h, cols, run=2):
-            pair = factors[c, h]
+        def multiply(engine, c, h, cols, run):
+            both = factors[c, h]
             engine.tensor_tensor(out=ker[c, h][:, cols].rearrange("p (n i) t -> p n t i", i=run),
-                                 in0=pair[:, 0, :, cols].rearrange("p t (n i) -> p n t i", i=run),
-                                 in1=pair[:, 1, :, cols].rearrange("p t (n i) -> p n t i", i=run), op=MULT)
+                                 in0=both[:, 0, :, cols].rearrange("p t (n i) -> p n t i", i=run),
+                                 in1=both[:, 1, :, cols].rearrange("p t (n i) -> p n t i", i=run), op=MULT)
+
+        def multiply_on_vector(c, h, cols):
+            multiply(nc.vector, c, h, cols, 2)
 
         def product(c, h):
             ker[c, h] = work.tile([P, HN, PACK], BF16, name="ker", bufs=2, align_bytes=64)
-            multiply(nc.vector, c, h, slice(0, HN))
+            multiply_on_vector(c, h, slice(0, HN))
 
         def product_aside(c, h, pair):
-            ker[c, h] = work.tile([P, HN, PACK], BF16, name="ker_aside", tag="pair%d" % (pair % 2), bufs=1, align_bytes=64)
+            ker[c, h] = work.tile([P, HN, PACK], BF16, name="ker_aside", tag=pair_tag(pair), bufs=1, align_bytes=64)
             multiply(nc.gpsimd, c, h, slice(0, SHARE), 4)
 
         def quant_ker(c, h):
@@ -221,43 +209,45 @@ def tile_kid_bootstrap_witness_s13_kernel(tc, gen_bytes, gen_scale, real, imp, m
 
         sums = {}
 
-        def witness(h, b, chunks):
-            if (h, b) not in sums:
-                sums[h, b] = psum.tile([P, BANK], F32, name="bank", tag=("held", "passing")[h])
-            for c in chunks:
-                codes, scales = kcodes[c, h]
-                nc.tensor.matmul_mx(out=sums[h, b][:], lhsT=wwords[:, c, 2 * P * b : 2 * P * (b + 1)].bitcast(FP4X4),
-                                    lhsT_scale=wscales[:, c, P * b : P * (b + 1)],
-                                    rhs=codes[:].bitcast(FP8X4), rhs_scale=scales[:],
-                                    start=(c == 0), stop=(c == C - 1))
+        def witness(h, blocks, chunks):
+            for b in blocks:
+                if (h, b) not in sums:
+                    sums[h, b] = psum.tile([P, BANK], F32, name="bank", tag=("held", "passing")[h])
+                for c in chunks:
+                    codes, scales = kcodes[c, h]
+                    nc.tensor.matmul_mx(out=sums[h, b][:], lhsT=wwords[:, c, 2 * P * b : 2 * P * (b + 1)].bitcast(FP4X4),
+                                        lhsT_scale=wscales[:, c, P * b : P * (b + 1)],
+                                        rhs=codes[:].bitcast(FP8X4), rhs_scale=scales[:],
+                                        start=(c == 0), stop=(c == C - 1))
 
-        def emit(h, b, on_vector, parts=1):
-            tile = work.tile([P, HN], F32, name="result", tag="rows", bufs=8)
-            copy = nc.vector.tensor_copy if on_vector else nc.scalar.copy
+        def emit(h, b, copy, parts=1):
+            tile = work.tile([P, HN], F32, name="result", tag="rows", bufs=H * JT)
             for i in range(parts):
                 cols = slice(i * HN // parts, (i + 1) * HN // parts)
                 copy(out=tile[:, cols], in_=sums[h, b][:, cols])
                 nc.sync.dma_start(out=out[b * P : (b + 1) * P, h * HN : (h + 1) * HN][:, cols], in_=tile[:, cols])
 
+        on_vector, on_scalar = nc.vector.tensor_copy, nc.scalar.copy
+
         nc.scalar.dma_start(out=imp_raw[:], in_=imp.rearrange("(c p t) -> p c t", p=P, t=PACK))
         load_gen(0, 2)
-        load_gen(1)
-        load_real(0)
-        load_gen(2)
-        load_real(1)
-        load_gen(3)
+        for k in range(1, PACK):
+            load_gen(k)
+            if k < PACK - 1:
+                load_real(k - 1)
         load_gen_pair(2)
         for j in range(2, H * JT):
             load_real(j)
         load_gen_pair(3)
 
         nc.scalar.activation(out=imp32[:], in_=imp_raw[:].rearrange("p c t -> p (c t)"), func=IDENTITY)
-        widen(0, nc.vector.tensor_copy, nc.scalar.copy, nc.vector.tensor_copy, nc.scalar.copy)
-        widen(1, nc.vector.tensor_copy, nc.scalar.copy)
+
+        widen(0, on_vector, on_scalar, on_vector, on_scalar)
+        widen(1, on_vector, on_scalar)
         turn_gen(0)
         turn_gen(1)
-        widen(2, nc.scalar.copy)
-        widen(3, nc.scalar.copy)
+        widen(2, on_scalar)
+        widen(3, on_scalar)
         for k in range(2):
             scale_gen(k, (0, 1))
             turn_real(k)
@@ -266,10 +256,11 @@ def tile_kid_bootstrap_witness_s13_kernel(tc, gen_bytes, gen_scale, real, imp, m
         turn_real(3)
         scale_gen(2)
         scale_gen(3)
-        widen_pair(2, "stage", 5)
+        widen_pair(2, "stage", STAGE_BUFS)
         load_gen_pair(4)
         load_gen_pair(5)
         load_mult()
+
         turn_real(4)
         turn_real(5)
         turn_gen(4)
@@ -277,60 +268,63 @@ def tile_kid_bootstrap_witness_s13_kernel(tc, gen_bytes, gen_scale, real, imp, m
         quant_gen(0)
         quant_real(0, 0)
         quant_gen(1)
-        widen_pair(3, "pair1", 1)
+        widen_pair(3, pair_tag(1), 1)
         quant_real(0, 1)
         scale_gen(4)
         scale_gen(5)
         turn_real(6)
         turn_real(7)
-        widen(8, nc.scalar.copy)
-        for k in range(PACK):
-            dots(k, 0)
+        widen(8, on_scalar)
+        for t in range(PACK):
+            dots(t, 0)
         quant_real(1, 0)
         quant_gen(2)
         product_aside(0, 0, 2)
         quant_real(1, 1)
-        groups = [[(k, 1) for k in range(4)], [(k, 0) for k in range(4, 8)], [(k, 1) for k in range(4, 8)]]
-        early = [(0, 0), (0, 1), (1, 0), (1, 1)]
-        for pair in range(3, KT // 2):
+
+        groups = [(c, h) for c in range(C) for h in range(H)]
+        for pair in range(3, PAIRS):
+            before, (c, h) = groups[pair - 3], groups[pair - 2]
+            last = pair == PAIRS - 1
+            between = 1 if pair > 3 else 0
             turn_gen(2 * pair)
+            for k in range(2 * pair + 2, min(2 * pair + 4, KT)):
+                if k not in wide:
+                    widen(k, on_scalar)
+            for t in range(between):
+                dots(PACK * c + t, h)
             turn_gen(2 * pair + 1)
-            if pair < KT // 2 - 1:
-                if pair > 3:
-                    widen(2 * pair + 2, nc.scalar.copy)
-                widen(2 * pair + 3, nc.scalar.copy)
             scale_gen(2 * pair)
             scale_gen(2 * pair + 1)
-            for k, h in groups[pair - 3]:
-                dots(k, h)
-            multiply(nc.vector, *early[pair - 3], slice(SHARE, HN))
+            for t in range(between, PACK):
+                dots(PACK * c + t, h)
+            multiply_on_vector(*before, slice(SHARE, HN))
             quant_gen(pair)
-            if pair < KT // 2 - 1:
-                product_aside(*early[pair - 2], pair)
-                quant_ker(*early[pair - 3])
-        for k, h in ((8, 0), (9, 0), (8, 1)):
-            dots(k, h, (k, h) in ((10, 0), (11, 0)))
-        product(1, 1)
-        quant_ker(1, 0)
-        quant_ker(1, 1)
-        for k, h in ((10, 0), (11, 0)):
-            dots(k, h, (k, h) in ((10, 0), (11, 0)))
-        product(2, 0)
-        for k, h in ((9, 1), (10, 1), (11, 1)):
-            dots(k, h, (k, h) in ((10, 0), (11, 0)))
+            if not last:
+                product_aside(c, h, pair)
+                quant_ker(*before)
+
+        c, k0 = C - 1, KT - PACK
+        dots(k0, 0)
+        dots(k0 + 1, 0)
+        dots(k0, 1)
+        product(c - 1, 1)
+        quant_ker(c - 1, 0)
+        quant_ker(c - 1, 1)
+        dots(k0 + 2, 0, True)
+        dots(k0 + 3, 0, True)
+        product(c, 0)
+        for k in range(k0 + 1, KT):
+            dots(k, 1)
+        witness(0, range(B), range(c))
+        quant_ker(c, 0)
+        witness(1, [0], range(c))
+        witness(0, range(B), [c])
+        product(c, 1)
         for b in range(B):
-            witness(0, b, range(C - 1))
-        quant_ker(2, 0)
-        for b in range(1):
-            witness(1, b, range(C - 1))
+            emit(0, b, on_scalar)
+        witness(1, range(1, B), range(c))
+        quant_ker(c, 1)
         for b in range(B):
-            witness(0, b, [2])
-        product(2, 1)
-        for b in range(B):
-            emit(0, b, False)
-        for b in range(1, B):
-            witness(1, b, range(C - 1))
-        quant_ker(2, 1)
-        for b in range(B):
-            witness(1, b, [C - 1])
-            emit(1, b, b % 2 == 1, 2 if b == 0 else 1)
+            witness(1, [b], [c])
+            emit(1, b, on_vector if b % 2 else on_scalar, 2 if b == 0 else 1)

@@ -30,7 +30,7 @@ KT = C * PACK
 PAIRS = KT // 2
 B = R // P
 BANK = 512
-STAGE_BUFS = 5
+STAGE_BUFS = 4
 SHARE = 432
 
 
@@ -139,7 +139,8 @@ def tile_kid_bootstrap_witness_s13_kernel(tc, gen_bytes, gen_scale, real, imp, m
         def turn_real(j):
             h = j // JT
             if h not in real_grouped:
-                real_grouped[h] = work.tile([P, G, HN, PACK], BF16, name="real_grouped", tag="stage", bufs=STAGE_BUFS, align_bytes=64)
+                tag, bufs = (("first_half", 1), ("stage", STAGE_BUFS))[h]
+                real_grouped[h] = work.tile([P, G, HN, PACK], BF16, name="real_grouped", tag=tag, bufs=bufs, align_bytes=64)
             words = real_grouped[h][:].rearrange("p g r t -> p (g r t)").bitcast(F32).rearrange("p (g r u) -> p g r u", g=G, u=2)
             place = slice(j % JT * P, (j % JT + 1) * P)
             for x, bank in enumerate(turn(real_tiles[j][:], "passing")):
@@ -267,36 +268,32 @@ def tile_kid_bootstrap_witness_s13_kernel(tc, gen_bytes, gen_scale, real, imp, m
         turn_gen(5)
         quant_gen(0)
         quant_real(0, 0)
-        quant_gen(1)
-        widen_pair(3, pair_tag(1), 1)
         quant_real(0, 1)
+        widen_pair(3, "first_half", 1)
+        quant_gen(1)
         scale_gen(4)
         scale_gen(5)
         turn_real(6)
         turn_real(7)
-        widen(8, on_scalar)
         for t in range(PACK):
             dots(t, 0)
         quant_real(1, 0)
+        quant_real(1, 1)
         quant_gen(2)
         product_aside(0, 0, 2)
-        quant_real(1, 1)
 
         groups = [(c, h) for c in range(C) for h in range(H)]
         for pair in range(3, PAIRS):
             before, (c, h) = groups[pair - 3], groups[pair - 2]
             last = pair == PAIRS - 1
-            between = 1 if pair > 3 else 0
             turn_gen(2 * pair)
             for k in range(2 * pair + 2, min(2 * pair + 4, KT)):
-                if k not in wide:
-                    widen(k, on_scalar)
-            for t in range(between):
-                dots(PACK * c + t, h)
+                widen(k, on_scalar)
+            dots(PACK * c, h)
             turn_gen(2 * pair + 1)
             scale_gen(2 * pair)
             scale_gen(2 * pair + 1)
-            for t in range(between, PACK):
+            for t in range(1, PACK):
                 dots(PACK * c + t, h)
             multiply_on_vector(*before, slice(SHARE, HN))
             quant_gen(pair)

@@ -48,12 +48,13 @@ def tile_kid_bootstrap_witness_s13_kernel(tc, gen_bytes, gen_scale, real, imp, m
         wwords = keep.tile([P, C, 2 * R], U8, name="wwords", align_bytes=64)
         wscales = keep.tile([P, C, R], U8, name="wscales", align_bytes=64)
         imp_raw = keep.tile([P, C, PACK], BF16, name="imp_raw")
+        zero = keep.tile([P, 1], F32, name="zero")
+        one = keep.tile([P, 1], F32, name="one")
         imp32 = keep.tile([P, KT], F32, name="imp32")
         rcodes = keep.tile([P, H, G, HN], U32, name="rcodes", align_bytes=64)
         rscales = keep.tile([P, H, G, HN], U8, name="rscales", align_bytes=64)
 
         nc.gpsimd.memset(wscales[:].rearrange("p c n -> p (c n)").bitcast(I32), 0)
-        nc.scalar.dma_start(out=scale_cols[:], in_=gen_scale.rearrange("o (g p t) -> p (o g) t", p=P, t=PACK))
 
         gen_rows = gen_bytes.rearrange("(c p t) k -> c p t k", p=P, t=PACK)
         gen_tiles = {}
@@ -176,7 +177,7 @@ def tile_kid_bootstrap_witness_s13_kernel(tc, gen_bytes, gen_scale, real, imp, m
             if (c, h) not in factors:
                 factors[c, h] = work.tile([P, 2, PACK, HN], F32, name="factors", tag="stage", bufs=STAGE_BUFS, align_bytes=64)
             weight = imp32[:, k : k + 1]
-            nc.scalar.activation(out=factors[c, h][:, 0, t], in_=bank[:], func=SQUARE, bias=1.0)
+            nc.scalar.activation(out=factors[c, h][:, 0, t], in_=bank[:], func=SQUARE, bias=one[:])
             if weighted_on_vector:
                 nc.vector.tensor_scalar(out=factors[c, h][:, 1, t], in0=bank[:], scalar1=1.0, scalar2=weight, op0=ADD, op1=MULT)
             else:
@@ -230,8 +231,8 @@ def tile_kid_bootstrap_witness_s13_kernel(tc, gen_bytes, gen_scale, real, imp, m
 
         on_vector, on_scalar = nc.vector.tensor_copy, nc.scalar.copy
 
-        nc.scalar.dma_start(out=imp_raw[:], in_=imp.rearrange("(c p t) -> p c t", p=P, t=PACK))
-        load_gen(0, 2)
+        load_gen(0, G)
+        nc.sync.dma_start(out=scale_cols[:], in_=gen_scale.rearrange("o (g p t) -> p (o g) t", p=P, t=PACK))
         for k in range(1, PACK):
             load_gen(k)
             if k < PACK - 1:
@@ -239,9 +240,11 @@ def tile_kid_bootstrap_witness_s13_kernel(tc, gen_bytes, gen_scale, real, imp, m
         load_gen_pair(2)
         for j in range(2, H * JT):
             load_real(j)
+        nc.sync.dma_start(out=imp_raw[:], in_=imp.rearrange("(c p t) -> p c t", p=P, t=PACK))
         load_gen_pair(3)
 
-        nc.scalar.activation(out=imp32[:], in_=imp_raw[:].rearrange("p c t -> p (c t)"), func=IDENTITY)
+        nc.vector.memset(zero[:], 0.0)
+        nc.scalar.activation(out=one[:], in_=zero[:], func=IDENTITY, bias=1.0)
 
         widen(0, on_vector, on_scalar, on_vector, on_scalar)
         widen(1, on_vector, on_scalar)
@@ -273,6 +276,7 @@ def tile_kid_bootstrap_witness_s13_kernel(tc, gen_bytes, gen_scale, real, imp, m
         quant_gen(1)
         scale_gen(4)
         scale_gen(5)
+        nc.scalar.activation(out=imp32[:], in_=imp_raw[:].rearrange("p c t -> p (c t)"), func=IDENTITY)
         turn_real(6)
         turn_real(7)
         for t in range(PACK):

@@ -32,6 +32,7 @@ B = R // P
 BANK = 512
 STAGE_BUFS = 4
 SHARE = 432
+FIRST = 416
 
 
 def tile_kid_bootstrap_witness_s13_kernel(tc, gen_bytes, gen_scale, real, imp, mult_words, mult_scales, out):
@@ -76,9 +77,11 @@ def tile_kid_bootstrap_witness_s13_kernel(tc, gen_bytes, gen_scale, real, imp, m
             for i in range(2):
                 gen_tiles[2 * pair + i] = tile[:, i]
 
-        def load_real(j):
+        def load_real(j, parts=1):
             tile = work.tile([P, D], BF16, name="real_in", tag="rows", bufs=H * JT)
-            nc.sync.dma_start(out=tile[:], in_=real[j * P : (j + 1) * P, :])
+            for i in range(parts):
+                cols = slice(i * D // parts, (i + 1) * D // parts)
+                nc.sync.dma_start(out=tile[:, cols], in_=real[j * P : (j + 1) * P, cols])
             real_tiles[j] = tile
 
         def load_mult():
@@ -104,16 +107,17 @@ def tile_kid_bootstrap_witness_s13_kernel(tc, gen_bytes, gen_scale, real, imp, m
             for i in range(2):
                 wide[2 * pair + i] = tile[:, i]
 
-        def turn(rows, tag):
+        def turn(rows, tag, runs=False):
             words = rows.bitcast(F32)
             banks = []
             for x in range(2):
                 bank = psum.tile([P, BANK], F32, name="bank", tag=tag)
                 for i in range(2):
                     for u in range(2):
-                        first = 2 * P * (2 * x + i) + u
+                        g = 2 * x + i
+                        pick = slice((u * G + g) * P, (u * G + g + 1) * P) if runs else slice(2 * P * g + u, 2 * P * (g + 1) + u - 1, 2)
                         col = (2 * u + i) * P
-                        nc.tensor.transpose(bank[:, col : col + P], words[:, first : first + 2 * P - 1 : 2], ident[:])
+                        nc.tensor.transpose(bank[:, col : col + P], words[:, pick], ident[:])
                 banks.append(bank)
             return banks
 
@@ -124,8 +128,17 @@ def tile_kid_bootstrap_witness_s13_kernel(tc, gen_bytes, gen_scale, real, imp, m
         gen_grouped = {}
         real_grouped = {}
 
+        in_runs = set()
+
+        def sort(k, copy, tile=None):
+            if tile is None:
+                tile = work.tile([P, 2, G * P], F32, name="sorted", tag="rows", bufs=H * JT)[:]
+            copy(out=tile, in_=wide[k].bitcast(F32).rearrange("p (q u) -> p u q", u=2))
+            wide[k] = tile.rearrange("p u q -> p (u q)").bitcast(BF16)
+            in_runs.add(k)
+
         def turn_gen(k):
-            turned[k] = turn(wide[k], "held")
+            turned[k] = turn(wide[k], "held", k in in_runs)
 
         def scale_gen(k, order=(1, 0)):
             if k % 2 == 0:
@@ -149,13 +162,18 @@ def tile_kid_bootstrap_witness_s13_kernel(tc, gen_bytes, gen_scale, real, imp, m
 
         gcodes = {}
 
-        def quant_gen(pair):
-            codes = work.tile([P, 2, G * P], U32, name="gcodes", bufs=4, align_bytes=64)
-            scales = work.tile([P, 2, G * P], U8, name="gscales", bufs=4, align_bytes=64)
-            nc.vector.quantize_mx(out=codes[:].rearrange("p i n -> p (i n)").bitcast(FP8X4), scales=scales[:].rearrange("p i n -> p (i n)"),
-                                  in_=gen_grouped[pair][:].rearrange("p g r t -> p (g r t)"))
-            for i in range(2):
-                gcodes[2 * pair + i] = (codes[:, i], scales[:, i])
+        pair_codes = {}
+
+        def quant_gen(pair, tiles=slice(0, 2)):
+            if pair not in pair_codes:
+                codes = work.tile([P, 2, G * P], U32, name="gcodes", bufs=4, align_bytes=64)
+                scales = work.tile([P, 2, G * P], U8, name="gscales", bufs=4, align_bytes=64)
+                pair_codes[pair] = (codes, scales)
+                for i in range(2):
+                    gcodes[2 * pair + i] = (codes[:, i], scales[:, i])
+            codes, scales = pair_codes[pair]
+            nc.vector.quantize_mx(out=codes[:, tiles].rearrange("p i n -> p (i n)").bitcast(FP8X4), scales=scales[:, tiles].rearrange("p i n -> p (i n)"),
+                                  in_=gen_grouped[pair][:, G * tiles.start : G * tiles.stop].rearrange("p g r t -> p (g r t)"))
 
         def quant_real(h, x):
             passes = slice(2 * x, 2 * x + 2)
@@ -199,9 +217,9 @@ def tile_kid_bootstrap_witness_s13_kernel(tc, gen_bytes, gen_scale, real, imp, m
             ker[c, h] = work.tile([P, HN, PACK], BF16, name="ker", bufs=2, align_bytes=64)
             multiply_on_vector(c, h, slice(0, HN))
 
-        def product_aside(c, h, pair):
+        def product_aside(c, h, pair, share):
             ker[c, h] = work.tile([P, HN, PACK], BF16, name="ker_aside", tag=pair_tag(pair), bufs=1, align_bytes=64)
-            multiply(nc.gpsimd, c, h, slice(0, SHARE), 4)
+            multiply(nc.gpsimd, c, h, slice(0, share), 4)
 
         def quant_ker(c, h):
             codes = work.tile([P, HN], U32, name="kcodes", bufs=C * H, align_bytes=64)
@@ -232,26 +250,30 @@ def tile_kid_bootstrap_witness_s13_kernel(tc, gen_bytes, gen_scale, real, imp, m
         on_vector, on_scalar = nc.vector.tensor_copy, nc.scalar.copy
 
         load_gen(0, G)
-        nc.sync.dma_start(out=scale_cols[:], in_=gen_scale.rearrange("o (g p t) -> p (o g) t", p=P, t=PACK))
         for k in range(1, PACK):
-            load_gen(k)
+            load_gen(k, 2 if k == 1 else 1)
+            if k == 1:
+                nc.sync.dma_start(out=scale_cols[:], in_=gen_scale.rearrange("o (g p t) -> p (o g) t", p=P, t=PACK))
             if k < PACK - 1:
                 load_real(k - 1)
         load_gen_pair(2)
         for j in range(2, H * JT):
             load_real(j)
+            if j == 5:
+                load_gen_pair(3)
+        load_gen_pair(4)
+
         nc.sync.dma_start(out=imp_raw[:], in_=imp.rearrange("(c p t) -> p c t", p=P, t=PACK))
-        load_gen_pair(3)
 
         nc.vector.memset(zero[:], 0.0)
         nc.scalar.activation(out=one[:], in_=zero[:], func=IDENTITY, bias=1.0)
 
         widen(0, on_vector, on_scalar, on_vector, on_scalar)
-        widen(1, on_vector, on_scalar)
+        widen(1, on_scalar, on_scalar)
         turn_gen(0)
         turn_gen(1)
-        widen(2, on_scalar)
-        widen(3, on_scalar)
+        widen(2, on_scalar, on_scalar)
+        widen(3, on_scalar, on_scalar)
         for k in range(2):
             scale_gen(k, (0, 1))
             turn_real(k)
@@ -261,7 +283,6 @@ def tile_kid_bootstrap_witness_s13_kernel(tc, gen_bytes, gen_scale, real, imp, m
         scale_gen(2)
         scale_gen(3)
         widen_pair(2, "stage", STAGE_BUFS)
-        load_gen_pair(4)
         load_gen_pair(5)
         load_mult()
 
@@ -272,51 +293,68 @@ def tile_kid_bootstrap_witness_s13_kernel(tc, gen_bytes, gen_scale, real, imp, m
         quant_gen(0)
         quant_real(0, 0)
         quant_real(0, 1)
-        widen_pair(3, "first_half", 1)
+        widen(6, on_scalar)
+        widen(7, on_scalar)
+        turn_real(6)
+        aside = work.tile([P, 2, 2, G * P], F32, name="aside", tag="first_half", bufs=1, align_bytes=64)
+        for k in (6, 7):
+            sort(k, nc.gpsimd.tensor_copy, aside[:, k - 6])
         quant_gen(1)
         scale_gen(4)
         scale_gen(5)
-        nc.scalar.activation(out=imp32[:], in_=imp_raw[:].rearrange("p c t -> p (c t)"), func=IDENTITY)
-        turn_real(6)
         turn_real(7)
+        widen(8, on_scalar)
+        nc.scalar.activation(out=imp32[:], in_=imp_raw[:].rearrange("p c t -> p (c t)"), func=IDENTITY)
         for t in range(PACK):
             dots(t, 0)
         quant_real(1, 0)
         quant_real(1, 1)
         quant_gen(2)
-        product_aside(0, 0, 2)
+        product_aside(0, 0, 2, FIRST)
 
+        units = [(k, h) for c in range(C) for h in range(H) for k in range(PACK * c, PACK * c + PACK)][PACK:]
         groups = [(c, h) for c in range(C) for h in range(H)]
-        for pair in range(3, PAIRS):
+        for pair in range(3, PAIRS - 1):
             before, (c, h) = groups[pair - 3], groups[pair - 2]
-            last = pair == PAIRS - 1
+            mine = units[5 * (pair - 3) : 5 * (pair - 2)]
             turn_gen(2 * pair)
-            for k in range(2 * pair + 2, min(2 * pair + 4, KT)):
-                widen(k, on_scalar)
-            dots(PACK * c, h)
+            if pair == 3:
+                widen(9, on_scalar)
+            if pair == 4:
+                widen(10, on_scalar)
+                widen(11, on_scalar)
+            if pair != 3:
+                dots(*mine[0])
             turn_gen(2 * pair + 1)
+            if pair == 3:
+                dots(*mine[0])
             scale_gen(2 * pair)
             scale_gen(2 * pair + 1)
-            for t in range(1, PACK):
-                dots(PACK * c + t, h)
-            multiply_on_vector(*before, slice(SHARE, HN))
+            for unit in mine[1:]:
+                dots(*unit)
+            multiply_on_vector(*before, slice(FIRST if pair == 3 else SHARE, HN))
             quant_gen(pair)
-            if not last:
-                product_aside(c, h, pair)
-                quant_ker(*before)
-
+            product_aside(c, h, pair, SHARE)
+            quant_ker(*before)
         c, k0 = C - 1, KT - PACK
-        dots(k0, 0)
-        dots(k0 + 1, 0)
-        dots(k0, 1)
+        turn_gen(10)
+        dots(6, 1)
+        turn_gen(11)
+        scale_gen(10)
+        scale_gen(11)
+        for unit in [(7, 1), (8, 0), (9, 0), (8, 1)]:
+            dots(*unit)
+        multiply_on_vector(1, 0, slice(SHARE, HN))
+        quant_gen(5)
         product(c - 1, 1)
         quant_ker(c - 1, 0)
-        quant_ker(c - 1, 1)
-        dots(k0 + 2, 0, True)
-        dots(k0 + 3, 0, True)
+        dots(10, 0, True)
+        dots(11, 0, True)
+        dots(9, 1)
+        dots(10, 1)
+        dots(11, 1)
         product(c, 0)
-        for k in range(k0 + 1, KT):
-            dots(k, 1)
+        quant_ker(c - 1, 1)
         witness(0, range(B), range(c))
         quant_ker(c, 0)
         witness(1, [0], range(c))

@@ -141,7 +141,7 @@ def tile_kid_bootstrap_witness_s13_kernel(tc, gen_bytes, gen_scale, real, imp, m
             turned[k] = turn(wide[k], "held", k in in_runs)
 
         def scale_gen(k, order=(1, 0)):
-            if k % 2 == 0:
+            if k // 2 not in gen_grouped:
                 gen_grouped[k // 2] = work.tile([P, 2 * G, P, PACK], BF16, name="gen_grouped", tag=pair_tag(k // 2), bufs=1, align_bytes=64)
             for x in order:
                 g0 = G * (k % 2) + 2 * x
@@ -218,7 +218,7 @@ def tile_kid_bootstrap_witness_s13_kernel(tc, gen_bytes, gen_scale, real, imp, m
             multiply_on_vector(c, h, slice(0, HN))
 
         def product_aside(c, h, pair, share):
-            ker[c, h] = work.tile([P, HN, PACK], BF16, name="ker_aside", tag=pair_tag(pair), bufs=1, align_bytes=64)
+            ker[c, h] = gen_grouped[pair][:, :G].rearrange("p g r t -> p (g r) t")
             multiply(nc.gpsimd, c, h, slice(0, share), 4)
 
         def quant_ker(c, h):
@@ -296,74 +296,81 @@ def tile_kid_bootstrap_witness_s13_kernel(tc, gen_bytes, gen_scale, real, imp, m
         widen(6, on_scalar)
         widen(7, on_scalar)
         turn_real(6)
-        aside = work.tile([P, 2, 2, G * P], F32, name="aside", tag="first_half", bufs=1, align_bytes=64)
-        for k in (6, 7):
+        aside = work.tile([P, 3, 2, G * P], F32, name="aside", tag="first_half", bufs=1, align_bytes=64)
+        widen(8, on_scalar)
+        for k in (6, 7, 8):
             sort(k, nc.gpsimd.tensor_copy, aside[:, k - 6])
         quant_gen(1)
         scale_gen(4)
         scale_gen(5)
         turn_real(7)
-        widen(8, on_scalar)
         nc.scalar.activation(out=imp32[:], in_=imp_raw[:].rearrange("p c t -> p (c t)"), func=IDENTITY)
         for t in range(PACK):
             dots(t, 0)
         quant_real(1, 0)
         quant_real(1, 1)
         quant_gen(2)
-        product_aside(0, 0, 2, FIRST)
+        product_aside(0, 0, 2, 416)
 
-        units = [(k, h) for c in range(C) for h in range(H) for k in range(PACK * c, PACK * c + PACK)][PACK:]
-        groups = [(c, h) for c in range(C) for h in range(H)]
-        for pair in range(3, PAIRS - 1):
-            before, (c, h) = groups[pair - 3], groups[pair - 2]
-            mine = units[5 * (pair - 3) : 5 * (pair - 2)]
-            turn_gen(2 * pair)
-            if pair == 3:
-                widen(9, on_scalar)
-            if pair == 4:
-                widen(10, on_scalar)
-                widen(11, on_scalar)
-            if pair != 3:
-                dots(*mine[0])
-            turn_gen(2 * pair + 1)
-            if pair == 3:
-                dots(*mine[0])
-            scale_gen(2 * pair)
-            scale_gen(2 * pair + 1)
-            for unit in mine[1:]:
-                dots(*unit)
-            multiply_on_vector(*before, slice(FIRST if pair == 3 else SHARE, HN))
-            quant_gen(pair)
-            product_aside(c, h, pair, SHARE)
-            quant_ker(*before)
-        c, k0 = C - 1, KT - PACK
+        turn_gen(6)
+        widen(9, on_scalar)
+        turn_gen(7)
+        scale_gen(6)
+        scale_gen(7)
+        dots(0, 1)
+        dots(1, 1)
+        dots(2, 1)
+        dots(3, 1)
+        dots(4, 0)
+        multiply_on_vector(0, 0, slice(416, HN))
+        quant_gen(3)
+        product_aside(0, 1, 3, 432)
+        turn_gen(8)
+        late = work.tile([P, 2, 2 * G, P, PACK], BF16, name="late", tag="first_half", bufs=1, align_bytes=64)
+        gen_grouped[4], gen_grouped[5] = late[:, 0], late[:, 1]
+        widen(10, on_scalar)
+        dots(5, 0)
+        turn_gen(9)
+        widen(11, on_scalar)
+        scale_gen(8)
+        scale_gen(9)
+        dots(6, 0)
+        dots(7, 0)
+        dots(4, 1)
+        multiply_on_vector(0, 1, slice(432, HN))
+        quant_gen(4)
+        product_aside(1, 0, 4, 432)
         turn_gen(10)
-        dots(6, 1)
+        dots(5, 1)
         turn_gen(11)
         scale_gen(10)
         scale_gen(11)
-        for unit in [(7, 1), (8, 0), (9, 0), (8, 1)]:
-            dots(*unit)
-        multiply_on_vector(1, 0, slice(SHARE, HN))
+        dots(6, 1)
+        dots(7, 1)
+        dots(8, 0)
+        dots(9, 0)
+        dots(8, 1)
+        multiply_on_vector(1, 0, slice(432, HN))
         quant_gen(5)
-        product(c - 1, 1)
-        quant_ker(c - 1, 0)
-        dots(10, 0, True)
-        dots(11, 0, True)
+        product(1, 1)
+        quant_ker(0, 0)
+        quant_ker(0, 1)
+        quant_ker(1, 0)
+        dots(10, 0, False)
+        dots(11, 0, False)
+        quant_ker(1, 1)
         dots(9, 1)
         dots(10, 1)
         dots(11, 1)
-        product(c, 0)
-        quant_ker(c - 1, 1)
-        witness(0, range(B), range(c))
-        quant_ker(c, 0)
-        witness(1, [0], range(c))
-        witness(0, range(B), [c])
-        product(c, 1)
+        product(2, 0)
+        witness(0, range(B), range(2))
+        quant_ker(2, 0)
+        witness(0, range(B), [2])
+        product(2, 1)
         for b in range(B):
             emit(0, b, on_scalar)
-        witness(1, range(1, B), range(c))
-        quant_ker(c, 1)
+        witness(1, range(3), range(2))
+        quant_ker(2, 1)
         for b in range(B):
-            witness(1, [b], [c])
-            emit(1, b, on_vector if b % 2 else on_scalar, 2 if b == 0 else 1)
+            witness(1, [b], [2] if b < 3 else range(3))
+            emit(1, b, on_vector if b % 2 else on_scalar, 2 if b in (0, 3) else 1)

@@ -46,14 +46,14 @@ def tile_kid_bootstrap_witness_s13_kernel(tc, gen_bytes, gen_scale, real, imp, m
         ident = keep.tile([P, P], F32, name="ident")
         make_identity(nc, ident[:])
         scale_cols = keep.tile([P, G, PACK], F32, name="scale_cols")
-        wwords = keep.tile([P, C, 2 * R], U8, name="wwords", align_bytes=64)
-        wscales = keep.tile([P, C, R], U8, name="wscales", align_bytes=64)
+        wwords = keep.tile([P, C, 2 * R], U8, name="wwords", align_bytes=256)
+        wscales = keep.tile([P, C, R], U8, name="wscales", align_bytes=256)
         imp_raw = keep.tile([P, C, PACK], BF16, name="imp_raw")
         zero = keep.tile([P, 1], F32, name="zero")
         one = keep.tile([P, 1], F32, name="one")
         imp32 = keep.tile([P, KT], F32, name="imp32")
-        rcodes = keep.tile([P, H, G, HN], U32, name="rcodes", align_bytes=64)
-        rscales = keep.tile([P, H, G, HN], U8, name="rscales", align_bytes=64)
+        rcodes = keep.tile([P, H, G, HN], U32, name="rcodes", align_bytes=256)
+        rscales = keep.tile([P, H, G, HN], U8, name="rscales", align_bytes=256)
 
         nc.gpsimd.memset(wscales[:].rearrange("p c n -> p (c n)").bitcast(I32), 0)
 
@@ -166,8 +166,8 @@ def tile_kid_bootstrap_witness_s13_kernel(tc, gen_bytes, gen_scale, real, imp, m
 
         def quant_gen(pair, tiles=slice(0, 2)):
             if pair not in pair_codes:
-                codes = work.tile([P, 2, G * P], U32, name="gcodes", bufs=4, align_bytes=64)
-                scales = work.tile([P, 2, G * P], U8, name="gscales", bufs=4, align_bytes=64)
+                codes = work.tile([P, 2, G * P], U32, name="gcodes", bufs=4, align_bytes=256)
+                scales = work.tile([P, 2, G * P], U8, name="gscales", bufs=4, align_bytes=256)
                 pair_codes[pair] = (codes, scales)
                 for i in range(2):
                     gcodes[2 * pair + i] = (codes[:, i], scales[:, i])
@@ -222,8 +222,8 @@ def tile_kid_bootstrap_witness_s13_kernel(tc, gen_bytes, gen_scale, real, imp, m
             multiply(nc.gpsimd, c, h, slice(0, share), 4)
 
         def quant_ker(c, h):
-            codes = work.tile([P, HN], U32, name="kcodes", bufs=C * H, align_bytes=64)
-            scales = work.tile([P, HN], U8, name="kscales", bufs=C * H, align_bytes=64)
+            codes = work.tile([P, HN], U32, name="kcodes", bufs=C * H, align_bytes=256)
+            scales = work.tile([P, HN], U8, name="kscales", bufs=C * H, align_bytes=256)
             nc.vector.quantize_mx(out=codes[:].bitcast(FP8X4), scales=scales[:], in_=ker[c, h][:].rearrange("p n t -> p (n t)"))
             kcodes[c, h] = (codes, scales)
 

@@ -15,7 +15,6 @@ FP8 = mybir.dt.float8_e4m3fn
 FP8X4 = mybir.dt.float8_e4m3fn_x4
 FP4X4 = mybir.dt.float4_e2m1fn_x4
 MULT = mybir.AluOpType.mult
-ADD = mybir.AluOpType.add
 SQUARE = mybir.ActivationFunctionType.Square
 IDENTITY = mybir.ActivationFunctionType.Identity
 
@@ -30,9 +29,12 @@ KT = C * PACK
 PAIRS = KT // 2
 B = R // P
 BANK = 512
+MX_ALIGN = 256
+SINGLE_BUFS = 6
 STAGE_BUFS = 4
-SHARE = 432
-FIRST = 416
+SORTED = (6, 7, 8)
+SHARES = (384, 400, 400)
+AFTER = (5, 3, 5)
 
 
 def tile_kid_bootstrap_witness_s13_kernel(tc, gen_bytes, gen_scale, real, imp, mult_words, mult_scales, out):
@@ -46,43 +48,43 @@ def tile_kid_bootstrap_witness_s13_kernel(tc, gen_bytes, gen_scale, real, imp, m
         ident = keep.tile([P, P], F32, name="ident")
         make_identity(nc, ident[:])
         scale_cols = keep.tile([P, G, PACK], F32, name="scale_cols")
-        wwords = keep.tile([P, C, 2 * R], U8, name="wwords", align_bytes=256)
-        wscales = keep.tile([P, C, R], U8, name="wscales", align_bytes=256)
+        wwords = keep.tile([P, C, 2 * R], U8, name="wwords", align_bytes=MX_ALIGN)
+        wscales = keep.tile([P, C, R], U8, name="wscales", align_bytes=MX_ALIGN)
         imp_raw = keep.tile([P, C, PACK], BF16, name="imp_raw")
         zero = keep.tile([P, 1], F32, name="zero")
         one = keep.tile([P, 1], F32, name="one")
         imp32 = keep.tile([P, KT], F32, name="imp32")
-        rcodes = keep.tile([P, H, G, HN], U32, name="rcodes", align_bytes=256)
-        rscales = keep.tile([P, H, G, HN], U8, name="rscales", align_bytes=256)
+        rcodes = keep.tile([P, H, G, HN], U32, name="rcodes", align_bytes=MX_ALIGN)
+        rscales = keep.tile([P, H, G, HN], U8, name="rscales", align_bytes=MX_ALIGN)
 
         nc.gpsimd.memset(wscales[:].rearrange("p c n -> p (c n)").bitcast(I32), 0)
 
+        on_vector, on_scalar, on_gpsimd = nc.vector.tensor_copy, nc.scalar.copy, nc.gpsimd.tensor_copy
+
+        def split(width, parts):
+            return [slice(i * width // parts, (i + 1) * width // parts) for i in range(parts)]
+
         gen_rows = gen_bytes.rearrange("(c p t) k -> c p t k", p=P, t=PACK)
         gen_tiles = {}
-        gen_pairs = {}
         real_tiles = {}
 
         def load_gen(k, parts=1):
-            tile = work.tile([P, D], U8, name="gen_in", bufs=PACK)
-            for i in range(parts):
-                cols = slice(i * D // parts, (i + 1) * D // parts)
+            tile = work.tile([P, D], U8, name="gen_in", bufs=SINGLE_BUFS)
+            for cols in split(D, parts):
                 nc.sync.dma_start(out=tile[:, cols], in_=gen_rows[k // PACK][:, k % PACK, cols])
             gen_tiles[k] = tile[:]
 
         def load_gen_pair(pair):
-            tile = work.tile([P, 2, D], U8, name="gen_pair_in", bufs=3)
+            tile = work.tile([P, 2, D], U8, name="gen_pair_in", bufs=2)
             t = 2 * pair % PACK
             nc.sync.dma_start(out=tile[:], in_=gen_rows[2 * pair // PACK][:, t : t + 2])
-            gen_pairs[pair] = tile
             for i in range(2):
                 gen_tiles[2 * pair + i] = tile[:, i]
 
-        def load_real(j, parts=1):
+        def load_real(j):
             tile = work.tile([P, D], BF16, name="real_in", tag="rows", bufs=H * JT)
-            for i in range(parts):
-                cols = slice(i * D // parts, (i + 1) * D // parts)
-                nc.sync.dma_start(out=tile[:, cols], in_=real[j * P : (j + 1) * P, cols])
-            real_tiles[j] = tile
+            nc.sync.dma_start(out=tile[:], in_=real[j * P : (j + 1) * P, :])
+            real_tiles[j] = tile[:]
 
         def load_mult():
             nc.sync.dma_start(out=wwords[:].rearrange("p c n -> p (c n)").bitcast(I32).rearrange("p (c n) -> p c n", c=C),
@@ -95,59 +97,51 @@ def tile_kid_bootstrap_witness_s13_kernel(tc, gen_bytes, gen_scale, real, imp, m
 
         def widen(k, *copies):
             tile = work.tile([P, D], BF16, name="wide", bufs=PACK)
-            for i, copy in enumerate(copies):
-                cols = slice(i * D // len(copies), (i + 1) * D // len(copies))
+            for copy, cols in zip(copies, split(D, len(copies))):
                 copy(out=tile[:, cols], in_=gen_tiles[k][:, cols].bitcast(FP8))
             wide[k] = tile[:]
 
-        def widen_pair(pair, tag, bufs):
-            tile = work.tile([P, 2, D], BF16, name="wide_pair", tag=tag, bufs=bufs, align_bytes=64)
-            nc.gpsimd.tensor_copy(out=tile[:].rearrange("p i k -> p (i k)"),
-                                  in_=gen_pairs[pair][:].rearrange("p i k -> p (i k)").bitcast(FP8))
+        def widen_pair_aside(pair):
+            tile = work.tile([P, 2, D], BF16, name="wide_pair", tag="stage", bufs=STAGE_BUFS, align_bytes=64)
             for i in range(2):
+                on_gpsimd(out=tile[:, i], in_=gen_tiles[2 * pair + i].bitcast(FP8))
                 wide[2 * pair + i] = tile[:, i]
 
-        def turn(rows, tag, runs=False):
+        def sort_aside():
+            tile = work.tile([P, len(SORTED), 2, G * P], F32, name="sorted", tag="first_half", bufs=1, align_bytes=64)
+            for i, k in enumerate(SORTED):
+                on_gpsimd(out=tile[:, i], in_=wide[k].bitcast(F32).rearrange("p (w u) -> p u w", u=2))
+                wide[k] = tile[:, i].rearrange("p u w -> p (u w)").bitcast(BF16)
+
+        def turn(rows, tag, is_sorted):
             words = rows.bitcast(F32)
+            by_u = words.rearrange("p (u g q) -> p u g q" if is_sorted else "p (g q u) -> p u g q", u=2, g=G)
             banks = []
             for x in range(2):
                 bank = psum.tile([P, BANK], F32, name="bank", tag=tag)
                 for i in range(2):
                     for u in range(2):
-                        g = 2 * x + i
-                        pick = slice((u * G + g) * P, (u * G + g + 1) * P) if runs else slice(2 * P * g + u, 2 * P * (g + 1) + u - 1, 2)
                         col = (2 * u + i) * P
-                        nc.tensor.transpose(bank[:, col : col + P], words[:, pick], ident[:])
+                        nc.tensor.transpose(bank[:, col : col + P], by_u[:, u, 2 * x + i], ident[:])
                 banks.append(bank)
             return banks
-
-        def pair_tag(pair):
-            return "pair%d" % (pair % 2)
 
         turned = {}
         gen_grouped = {}
         real_grouped = {}
 
-        in_runs = set()
-
-        def sort(k, copy, tile=None):
-            if tile is None:
-                tile = work.tile([P, 2, G * P], F32, name="sorted", tag="rows", bufs=H * JT)[:]
-            copy(out=tile, in_=wide[k].bitcast(F32).rearrange("p (q u) -> p u q", u=2))
-            wide[k] = tile.rearrange("p u q -> p (u q)").bitcast(BF16)
-            in_runs.add(k)
-
         def turn_gen(k):
-            turned[k] = turn(wide[k], "held", k in in_runs)
+            turned[k] = turn(wide[k], "held", k in SORTED)
 
         def scale_gen(k, order=(1, 0)):
-            if k // 2 not in gen_grouped:
-                gen_grouped[k // 2] = work.tile([P, 2 * G, P, PACK], BF16, name="gen_grouped", tag=pair_tag(k // 2), bufs=1, align_bytes=64)
+            pair = k // 2
+            if pair not in gen_grouped:
+                gen_grouped[pair] = work.tile([P, 2 * G, P, PACK], BF16, name="gen_grouped", bufs=2, align_bytes=64)[:]
             for x in order:
                 g0 = G * (k % 2) + 2 * x
                 values = turned[k][x][:].bitcast(BF16).rearrange("p (u g r e) -> p g r u e", g=2, u=2, e=2)
                 by_d = scale_cols[:, 2 * x : 2 * x + 2].rearrange("p g (u e) -> p g u e", u=2).unsqueeze(2).to_broadcast([P, 2, P, 2, 2])
-                nc.vector.tensor_tensor(out=gen_grouped[k // 2][:, g0 : g0 + 2].rearrange("p g r (u e) -> p g r u e", u=2),
+                nc.vector.tensor_tensor(out=gen_grouped[pair][:, g0 : g0 + 2].rearrange("p g r (u e) -> p g r u e", u=2),
                                         in0=values, in1=by_d, op=MULT)
 
         def turn_real(j):
@@ -157,33 +151,28 @@ def tile_kid_bootstrap_witness_s13_kernel(tc, gen_bytes, gen_scale, real, imp, m
                 real_grouped[h] = work.tile([P, G, HN, PACK], BF16, name="real_grouped", tag=tag, bufs=bufs, align_bytes=64)
             words = real_grouped[h][:].rearrange("p g r t -> p (g r t)").bitcast(F32).rearrange("p (g r u) -> p g r u", g=G, u=2)
             place = slice(j % JT * P, (j % JT + 1) * P)
-            for x, bank in enumerate(turn(real_tiles[j][:], "passing")):
-                nc.scalar.copy(out=words[:, 2 * x : 2 * x + 2, place], in_=bank[:].rearrange("p (u g r) -> p g r u", g=2, u=2))
+            for x, bank in enumerate(turn(real_tiles[j], "passing", False)):
+                on_scalar(out=words[:, 2 * x : 2 * x + 2, place], in_=bank[:].rearrange("p (u g r) -> p g r u", g=2, u=2))
 
         gcodes = {}
 
-        pair_codes = {}
+        def quant_gen(pair):
+            codes = work.tile([P, 2, G * P], U32, name="gcodes", bufs=4, align_bytes=MX_ALIGN)
+            scales = work.tile([P, 2, G * P], U8, name="gscales", bufs=4, align_bytes=MX_ALIGN)
+            nc.vector.quantize_mx(out=codes[:].rearrange("p i n -> p (i n)").bitcast(FP8X4), scales=scales[:].rearrange("p i n -> p (i n)"),
+                                  in_=gen_grouped[pair].rearrange("p g r t -> p (g r t)"))
+            for i in range(2):
+                gcodes[2 * pair + i] = (codes[:, i], scales[:, i])
 
-        def quant_gen(pair, tiles=slice(0, 2)):
-            if pair not in pair_codes:
-                codes = work.tile([P, 2, G * P], U32, name="gcodes", bufs=4, align_bytes=256)
-                scales = work.tile([P, 2, G * P], U8, name="gscales", bufs=4, align_bytes=256)
-                pair_codes[pair] = (codes, scales)
-                for i in range(2):
-                    gcodes[2 * pair + i] = (codes[:, i], scales[:, i])
-            codes, scales = pair_codes[pair]
-            nc.vector.quantize_mx(out=codes[:, tiles].rearrange("p i n -> p (i n)").bitcast(FP8X4), scales=scales[:, tiles].rearrange("p i n -> p (i n)"),
-                                  in_=gen_grouped[pair][:, G * tiles.start : G * tiles.stop].rearrange("p g r t -> p (g r t)"))
-
-        def quant_real(h, x):
-            passes = slice(2 * x, 2 * x + 2)
-            nc.vector.quantize_mx(out=rcodes[:, h, passes].rearrange("p g n -> p (g n)").bitcast(FP8X4),
-                                  scales=rscales[:, h, passes].rearrange("p g n -> p (g n)"),
-                                  in_=real_grouped[h][:, passes].rearrange("p g r t -> p (g r t)"))
+        def quant_real(h):
+            for passes in split(G, 2):
+                nc.vector.quantize_mx(out=rcodes[:, h, passes].rearrange("p g n -> p (g n)").bitcast(FP8X4),
+                                      scales=rscales[:, h, passes].rearrange("p g n -> p (g n)"),
+                                      in_=real_grouped[h][:, passes].rearrange("p g r t -> p (g r t)"))
 
         factors = {}
 
-        def dots(k, h, weighted_on_vector=False):
+        def dots(k, h):
             codes, scales = gcodes[k]
             bank = psum.tile([P, BANK], F32, name="bank", tag="passing")
             for g in range(G):
@@ -196,10 +185,7 @@ def tile_kid_bootstrap_witness_s13_kernel(tc, gen_bytes, gen_scale, real, imp, m
                 factors[c, h] = work.tile([P, 2, PACK, HN], F32, name="factors", tag="stage", bufs=STAGE_BUFS, align_bytes=64)
             weight = imp32[:, k : k + 1]
             nc.scalar.activation(out=factors[c, h][:, 0, t], in_=bank[:], func=SQUARE, bias=one[:])
-            if weighted_on_vector:
-                nc.vector.tensor_scalar(out=factors[c, h][:, 1, t], in0=bank[:], scalar1=1.0, scalar2=weight, op0=ADD, op1=MULT)
-            else:
-                nc.scalar.activation(out=factors[c, h][:, 1, t], in_=bank[:], func=IDENTITY, scale=weight, bias=weight)
+            nc.scalar.activation(out=factors[c, h][:, 1, t], in_=bank[:], func=IDENTITY, scale=weight, bias=weight)
 
         ker = {}
         kcodes = {}
@@ -213,18 +199,21 @@ def tile_kid_bootstrap_witness_s13_kernel(tc, gen_bytes, gen_scale, real, imp, m
         def multiply_on_vector(c, h, cols):
             multiply(nc.vector, c, h, cols, 2)
 
-        def product(c, h):
-            ker[c, h] = work.tile([P, HN, PACK], BF16, name="ker", bufs=2, align_bytes=64)
-            multiply_on_vector(c, h, slice(0, HN))
+        def product(c, h, parts=1):
+            ker[c, h] = work.tile([P, HN, PACK], BF16, name="ker", bufs=2, align_bytes=64)[:]
+            for cols in split(HN, parts):
+                multiply_on_vector(c, h, cols)
 
         def product_aside(c, h, pair, share):
             ker[c, h] = gen_grouped[pair][:, :G].rearrange("p g r t -> p (g r) t")
             multiply(nc.gpsimd, c, h, slice(0, share), 4)
 
-        def quant_ker(c, h):
-            codes = work.tile([P, HN], U32, name="kcodes", bufs=C * H, align_bytes=256)
-            scales = work.tile([P, HN], U8, name="kscales", bufs=C * H, align_bytes=256)
-            nc.vector.quantize_mx(out=codes[:].bitcast(FP8X4), scales=scales[:], in_=ker[c, h][:].rearrange("p n t -> p (n t)"))
+        def quant_ker(c, h, parts=1):
+            codes = work.tile([P, HN], U32, name="kcodes", bufs=C * H, align_bytes=MX_ALIGN)
+            scales = work.tile([P, HN], U8, name="kscales", bufs=C * H, align_bytes=MX_ALIGN)
+            for cols in split(HN, parts):
+                nc.vector.quantize_mx(out=codes[:, cols].bitcast(FP8X4), scales=scales[:, cols],
+                                      in_=ker[c, h][:, cols].rearrange("p n t -> p (n t)"))
             kcodes[c, h] = (codes, scales)
 
         sums = {}
@@ -242,34 +231,34 @@ def tile_kid_bootstrap_witness_s13_kernel(tc, gen_bytes, gen_scale, real, imp, m
 
         def emit(h, b, copy, parts=1):
             tile = work.tile([P, HN], F32, name="result", tag="rows", bufs=H * JT)
-            for i in range(parts):
-                cols = slice(i * HN // parts, (i + 1) * HN // parts)
+            for cols in split(HN, parts):
                 copy(out=tile[:, cols], in_=sums[h, b][:, cols])
                 nc.sync.dma_start(out=out[b * P : (b + 1) * P, h * HN : (h + 1) * HN][:, cols], in_=tile[:, cols])
 
-        on_vector, on_scalar = nc.vector.tensor_copy, nc.scalar.copy
-
         load_gen(0, G)
-        for k in range(1, PACK):
-            load_gen(k, 2 if k == 1 else 1)
-            if k == 1:
-                nc.sync.dma_start(out=scale_cols[:], in_=gen_scale.rearrange("o (g p t) -> p (o g) t", p=P, t=PACK))
-            if k < PACK - 1:
-                load_real(k - 1)
-        load_gen_pair(2)
-        for j in range(2, H * JT):
+        load_gen(1, 2)
+        nc.sync.dma_start(out=scale_cols[:], in_=gen_scale.rearrange("o (g p t) -> p (o g) t", p=P, t=PACK))
+        for j in range(2):
             load_real(j)
-            if j == 5:
-                load_gen_pair(3)
-        load_gen_pair(4)
-
-        nc.sync.dma_start(out=imp_raw[:], in_=imp.rearrange("(c p t) -> p c t", p=P, t=PACK))
+            load_gen(j + 2)
+        for j in range(2, JT):
+            load_gen(j + 2)
+            load_real(j)
 
         nc.vector.memset(zero[:], 0.0)
         nc.scalar.activation(out=one[:], in_=zero[:], func=IDENTITY, bias=1.0)
 
         widen(0, on_vector, on_scalar, on_vector, on_scalar)
-        widen(1, on_scalar, on_scalar)
+        widen(1, on_vector, on_scalar)
+        for j in range(JT, JT + 2):
+            load_real(j)
+            load_gen(j + 2)
+        for j in range(JT + 2, H * JT):
+            load_real(j)
+        load_gen_pair(4)
+        nc.sync.dma_start(out=imp_raw[:], in_=imp.rearrange("(c p t) -> p c t", p=P, t=PACK))
+        load_gen_pair(5)
+        load_mult()
         turn_gen(0)
         turn_gen(1)
         widen(2, on_scalar, on_scalar)
@@ -280,97 +269,70 @@ def tile_kid_bootstrap_witness_s13_kernel(tc, gen_bytes, gen_scale, real, imp, m
             turn_gen(k + 2)
         turn_real(2)
         turn_real(3)
-        scale_gen(2)
+        scale_gen(2, (0, 1))
         scale_gen(3)
-        widen_pair(2, "stage", STAGE_BUFS)
-        load_gen_pair(5)
-        load_mult()
+        widen_pair_aside(2)
 
-        turn_real(4)
-        turn_real(5)
         turn_gen(4)
+        for i in range(2):
+            widen(SORTED[i], on_scalar)
+            turn_real(JT + i)
         turn_gen(5)
         quant_gen(0)
-        quant_real(0, 0)
-        quant_real(0, 1)
-        widen(6, on_scalar)
-        widen(7, on_scalar)
-        turn_real(6)
-        aside = work.tile([P, 3, 2, G * P], F32, name="aside", tag="first_half", bufs=1, align_bytes=64)
-        widen(8, on_scalar)
-        for k in (6, 7, 8):
-            sort(k, nc.gpsimd.tensor_copy, aside[:, k - 6])
+        quant_real(0)
+        turn_real(JT + 2)
+        widen(SORTED[2], on_scalar)
+        sort_aside()
         quant_gen(1)
         scale_gen(4)
         scale_gen(5)
-        turn_real(7)
+        turn_real(JT + 3)
         nc.scalar.activation(out=imp32[:], in_=imp_raw[:].rearrange("p c t -> p (c t)"), func=IDENTITY)
         for t in range(PACK):
             dots(t, 0)
-        quant_real(1, 0)
-        quant_real(1, 1)
+        quant_real(1)
         quant_gen(2)
-        product_aside(0, 0, 2, 416)
 
-        turn_gen(6)
-        widen(9, on_scalar)
-        turn_gen(7)
-        scale_gen(6)
-        scale_gen(7)
-        dots(0, 1)
-        dots(1, 1)
-        dots(2, 1)
-        dots(3, 1)
-        dots(4, 0)
-        multiply_on_vector(0, 0, slice(416, HN))
-        quant_gen(3)
-        product_aside(0, 1, 3, 432)
-        turn_gen(8)
-        late = work.tile([P, 2, 2 * G, P, PACK], BF16, name="late", tag="first_half", bufs=1, align_bytes=64)
-        gen_grouped[4], gen_grouped[5] = late[:, 0], late[:, 1]
-        widen(10, on_scalar)
-        dots(5, 0)
-        turn_gen(9)
-        widen(11, on_scalar)
-        scale_gen(8)
-        scale_gen(9)
-        dots(6, 0)
-        dots(7, 0)
-        dots(4, 1)
-        multiply_on_vector(0, 1, slice(432, HN))
-        quant_gen(4)
-        product_aside(1, 0, 4, 432)
-        turn_gen(10)
-        dots(5, 1)
-        turn_gen(11)
-        scale_gen(10)
-        scale_gen(11)
-        dots(6, 1)
-        dots(7, 1)
-        dots(8, 0)
-        dots(9, 0)
-        dots(8, 1)
-        multiply_on_vector(1, 0, slice(432, HN))
-        quant_gen(5)
-        product(1, 1)
-        quant_ker(0, 0)
-        quant_ker(0, 1)
-        quant_ker(1, 0)
-        dots(10, 0, False)
-        dots(11, 0, False)
-        quant_ker(1, 1)
-        dots(9, 1)
-        dots(10, 1)
-        dots(11, 1)
-        product(2, 0)
-        witness(0, range(B), range(2))
-        quant_ker(2, 0)
-        witness(0, range(B), [2])
-        product(2, 1)
+        groups = [(c, h) for c in range(C) for h in range(H)]
+        todo = [(k, h) for c, h in groups[1:] for k in range(PACK * c, PACK * (c + 1))]
+        todo.remove((KT - PACK, 1))
+        todo.insert(todo.index((KT - 2, 0)), (KT - PACK, 1))
+        uncast = list(range(SORTED[-1] + 1, KT))
+        for step, pair in enumerate(range(3, PAIRS)):
+            product_aside(*groups[step], pair - 1, SHARES[step])
+            one_run = 2 * pair + 1 in SORTED
+            for k in (2 * pair, 2 * pair + 1):
+                turn_gen(k)
+                if uncast and (k % 2 == 0 or not one_run):
+                    widen(uncast.pop(0), on_scalar)
+                if k % 2 == 0 and not one_run:
+                    dots(*todo.pop(0))
+                if k == SORTED[-1]:
+                    late = work.tile([P, 2, 2 * G, P, PACK], BF16, name="late", tag="first_half", bufs=1, align_bytes=64)
+                    gen_grouped[pair], gen_grouped[pair + 1] = late[:, 0], late[:, 1]
+            scale_gen(2 * pair)
+            scale_gen(2 * pair + 1)
+            for i in range(AFTER[step]):
+                dots(*todo.pop(0))
+            multiply_on_vector(*groups[step], slice(SHARES[step], HN))
+            quant_gen(pair)
+
+        last = C - 1
+        product(last - 1, 1)
+        for group in groups[: 2 * last]:
+            quant_ker(*group)
+        for unit in todo:
+            dots(*unit)
+        product(last, 0)
+        witness(0, range(B - 1), range(last))
+        quant_ker(last, 0)
+        witness(0, range(B - 1), [last])
+        witness(0, [B - 1], range(C))
+        product(last, 1, 2)
         for b in range(B):
             emit(0, b, on_scalar)
-        witness(1, range(3), range(2))
-        quant_ker(2, 1)
+        witness(1, range(B - 1), range(last))
+        quant_ker(last, 1, 2)
         for b in range(B):
-            witness(1, [b], [2] if b < 3 else range(3))
-            emit(1, b, on_vector if b % 2 else on_scalar, 2 if b in (0, 3) else 1)
+            witness(1, [b], [last] if b < B - 1 else range(C))
+            emit(1, b, on_vector if b % 2 else on_scalar, 2 if b in (0, B - 1) else 1)

@@ -32,8 +32,10 @@ BANK = 512
 MX_ALIGN = 256
 SINGLE_BUFS = 6
 STAGE_BUFS = 4
+BY_PRODUCT = (4, 5)
+CAST_ASIDE = D - P * PACK
 SORTED = (6, 7, 8)
-SHARES = (384, 400, 400)
+SHARES = (416, 432, 432)
 AFTER = (5, 3, 5)
 
 
@@ -47,6 +49,8 @@ def tile_kid_bootstrap_witness_s13_kernel(tc, gen_bytes, gen_scale, real, imp, m
 
         ident = keep.tile([P, P], F32, name="ident")
         make_identity(nc, ident[:])
+        ident16 = keep.tile([P, P], BF16, name="ident16")
+        nc.vector.tensor_copy(out=ident16[:], in_=ident[:])
         scale_cols = keep.tile([P, G, PACK], F32, name="scale_cols")
         wwords = keep.tile([P, C, 2 * R], U8, name="wwords", align_bytes=MX_ALIGN)
         wscales = keep.tile([P, C, R], U8, name="wscales", align_bytes=MX_ALIGN)
@@ -101,11 +105,8 @@ def tile_kid_bootstrap_witness_s13_kernel(tc, gen_bytes, gen_scale, real, imp, m
                 copy(out=tile[:, cols], in_=gen_tiles[k][:, cols].bitcast(FP8))
             wide[k] = tile[:]
 
-        def widen_pair_aside(pair):
-            tile = work.tile([P, 2, D], BF16, name="wide_pair", tag="stage", bufs=STAGE_BUFS, align_bytes=64)
-            for i in range(2):
-                on_gpsimd(out=tile[:, i], in_=gen_tiles[2 * pair + i].bitcast(FP8))
-                wide[2 * pair + i] = tile[:, i]
+        def widen_part(k, copy, cols):
+            copy(out=wide[k][:, cols], in_=gen_tiles[k][:, cols].bitcast(FP8))
 
         def sort_aside():
             tile = work.tile([P, len(SORTED), 2, G * P], F32, name="sorted", tag="first_half", bufs=1, align_bytes=64)
@@ -133,13 +134,23 @@ def tile_kid_bootstrap_witness_s13_kernel(tc, gen_bytes, gen_scale, real, imp, m
         def turn_gen(k):
             turned[k] = turn(wide[k], "held", k in SORTED)
 
+        def turn_gen_by_product(k, x):
+            bank = psum.tile([P, BANK], F32, name="bank", tag="held")
+            planes = bank[:].bitcast(BF16).rearrange("p (g t r) -> p g t r", g=2, t=PACK)
+            by_t = wide[k].rearrange("p (g q t) -> p g t q", g=G, t=PACK)
+            for i in range(2):
+                for t in range(PACK):
+                    nc.tensor.matmul(out=planes[:, i, t], lhsT=by_t[:, 2 * x + i, t], rhs=ident16[:], start=True, stop=True)
+            turned[k] = turned.get(k, []) + [bank]
+
         def scale_gen(k, order=(1, 0)):
             pair = k // 2
             if pair not in gen_grouped:
                 gen_grouped[pair] = work.tile([P, 2 * G, P, PACK], BF16, name="gen_grouped", bufs=2, align_bytes=64)[:]
             for x in order:
                 g0 = G * (k % 2) + 2 * x
-                values = turned[k][x][:].bitcast(BF16).rearrange("p (u g r e) -> p g r u e", g=2, u=2, e=2)
+                held = "p (g u e r) -> p g r u e" if k in BY_PRODUCT else "p (u g r e) -> p g r u e"
+                values = turned[k][x][:].bitcast(BF16).rearrange(held, g=2, u=2, e=2)
                 by_d = scale_cols[:, 2 * x : 2 * x + 2].rearrange("p g (u e) -> p g u e", u=2).unsqueeze(2).to_broadcast([P, 2, P, 2, 2])
                 nc.vector.tensor_tensor(out=gen_grouped[pair][:, g0 : g0 + 2].rearrange("p g r (u e) -> p g r u e", u=2),
                                         in0=values, in1=by_d, op=MULT)
@@ -241,9 +252,10 @@ def tile_kid_bootstrap_witness_s13_kernel(tc, gen_bytes, gen_scale, real, imp, m
         for j in range(2):
             load_real(j)
             load_gen(j + 2)
+        load_gen(4)
         for j in range(2, JT):
-            load_gen(j + 2)
             load_real(j)
+        load_gen(5)
 
         nc.vector.memset(zero[:], 0.0)
         nc.scalar.activation(out=one[:], in_=zero[:], func=IDENTITY, bias=1.0)
@@ -268,26 +280,29 @@ def tile_kid_bootstrap_witness_s13_kernel(tc, gen_bytes, gen_scale, real, imp, m
             turn_real(k)
             turn_gen(k + 2)
         turn_real(2)
-        turn_real(3)
         scale_gen(2, (0, 1))
-        scale_gen(3)
-        widen_pair_aside(2)
+        scale_gen(3, (0, 1))
+        pair_tile = work.tile([P, 2, D], BF16, name="wide_pair", tag="stage", bufs=STAGE_BUFS, align_bytes=64)
+        wide[4], wide[5] = pair_tile[:, 0], pair_tile[:, 1]
+        widen_part(4, on_gpsimd, slice(0, D))
+        widen_part(5, on_gpsimd, slice(0, CAST_ASIDE))
 
-        turn_gen(4)
-        for i in range(2):
-            widen(SORTED[i], on_scalar)
-            turn_real(JT + i)
-        turn_gen(5)
-        quant_gen(0)
-        quant_real(0)
-        turn_real(JT + 2)
-        widen(SORTED[2], on_scalar)
+        for i in range(4):
+            if i == 3:
+                quant_gen(0)
+                quant_real(0)
+            turn_real(JT - 1 + i)
+            turn_gen_by_product(BY_PRODUCT[i // 2], i % 2)
+            if i == 1:
+                widen_part(5, on_scalar, slice(CAST_ASIDE, D))
+            if i != 2:
+                widen(SORTED[min(i, 2)], on_scalar)
         sort_aside()
         quant_gen(1)
-        scale_gen(4)
-        scale_gen(5)
-        turn_real(JT + 3)
+        for k in BY_PRODUCT:
+            scale_gen(k, (0, 1))
         nc.scalar.activation(out=imp32[:], in_=imp_raw[:].rearrange("p c t -> p (c t)"), func=IDENTITY)
+        turn_real(H * JT - 1)
         for t in range(PACK):
             dots(t, 0)
         quant_real(1)

@@ -30,13 +30,11 @@ PAIRS = KT // 2
 B = R // P
 BANK = 512
 MX_ALIGN = 256
-SINGLE_BUFS = 6
-STAGE_BUFS = 4
+KIB = 1024
 BY_PRODUCT = (4, 5)
 CAST_ASIDE = D - P * PACK
-SORTED = (6, 7, 8)
-SHARES = (416, 432, 432)
-AFTER = (5, 3, 5)
+SORTED = (6, 7, 8, 10, 11)
+SHARE = 432
 
 
 def tile_kid_bootstrap_witness_s13_kernel(tc, gen_bytes, gen_scale, real, imp, mult_words, mult_scales, out):
@@ -44,24 +42,33 @@ def tile_kid_bootstrap_witness_s13_kernel(tc, gen_bytes, gen_scale, real, imp, m
     with ExitStack() as ctx:
         keep = ctx.enter_context(tc.tile_pool(name="keep", bufs=1))
         work = ctx.enter_context(tc.tile_pool(name="work", bufs=1))
-        psum = ctx.enter_context(tc.psum_pool(name="psum", bufs=4))
+        arena = ctx.enter_context(tc.tile_pool(name="arena", bufs=1))
+        psum = ctx.enter_context(tc.psum_pool(name="psum", bufs=1))
         ctx.enter_context(tc.manual_schedule())
+
+        def placed(name, kib, width, dtype):
+            return arena.tile([P, width], dtype, name=name, offset=kib * KIB, align_bytes=64)[:]
+
+        taken = {"passing": 0, "held": 0}
+
+        def new_bank(role, width=BANK):
+            number = taken[role] % 4
+            taken[role] = taken[role] + 1
+            return psum.tile([P, width], F32, name="bank", tag="%s%d" % (role, number))
 
         ident = keep.tile([P, P], F32, name="ident")
         make_identity(nc, ident[:])
         ident16 = keep.tile([P, P], BF16, name="ident16")
-        nc.vector.tensor_copy(out=ident16[:], in_=ident[:])
         scale_cols = keep.tile([P, G, PACK], F32, name="scale_cols")
         wwords = keep.tile([P, C, 2 * R], U8, name="wwords", align_bytes=MX_ALIGN)
         wscales = keep.tile([P, C, R], U8, name="wscales", align_bytes=MX_ALIGN)
         imp_raw = keep.tile([P, C, PACK], BF16, name="imp_raw")
-        zero = keep.tile([P, 1], F32, name="zero")
-        one = keep.tile([P, 1], F32, name="one")
         imp32 = keep.tile([P, KT], F32, name="imp32")
         rcodes = keep.tile([P, H, G, HN], U32, name="rcodes", align_bytes=MX_ALIGN)
         rscales = keep.tile([P, H, G, HN], U8, name="rscales", align_bytes=MX_ALIGN)
 
-        nc.gpsimd.memset(wscales[:].rearrange("p c n -> p (c n)").bitcast(I32), 0)
+        nc.vector.memset(wscales[:].rearrange("p c n -> p (c n)").bitcast(I32), 0)
+        nc.scalar.activation(out=ident16[:], in_=ident[:], func=IDENTITY)
 
         on_vector, on_scalar, on_gpsimd = nc.vector.tensor_copy, nc.scalar.copy, nc.gpsimd.tensor_copy
 
@@ -73,7 +80,7 @@ def tile_kid_bootstrap_witness_s13_kernel(tc, gen_bytes, gen_scale, real, imp, m
         real_tiles = {}
 
         def load_gen(k, parts=1):
-            tile = work.tile([P, D], U8, name="gen_in", bufs=SINGLE_BUFS)
+            tile = work.tile([P, D], U8, name="gen_in", bufs=6)
             for cols in split(D, parts):
                 nc.sync.dma_start(out=tile[:, cols], in_=gen_rows[k // PACK][:, k % PACK, cols])
             gen_tiles[k] = tile[:]
@@ -86,9 +93,8 @@ def tile_kid_bootstrap_witness_s13_kernel(tc, gen_bytes, gen_scale, real, imp, m
                 gen_tiles[2 * pair + i] = tile[:, i]
 
         def load_real(j):
-            tile = work.tile([P, D], BF16, name="real_in", tag="rows", bufs=H * JT)
-            nc.sync.dma_start(out=tile[:], in_=real[j * P : (j + 1) * P, :])
-            real_tiles[j] = tile[:]
+            real_tiles[j] = placed("real_in%d" % j, 4 * j, D, BF16)
+            nc.sync.dma_start(out=real_tiles[j], in_=real[j * P : (j + 1) * P, :])
 
         def load_mult():
             nc.sync.dma_start(out=wwords[:].rearrange("p c n -> p (c n)").bitcast(I32).rearrange("p (c n) -> p c n", c=C),
@@ -99,27 +105,37 @@ def tile_kid_bootstrap_witness_s13_kernel(tc, gen_bytes, gen_scale, real, imp, m
 
         wide = {}
 
+        def wide_run(first, count, kib):
+            run = placed("wide%d" % first, kib, count * D, BF16)
+            for i in range(count):
+                wide[first + i] = run[:, i * D : (i + 1) * D]
+            return run
+
         def widen(k, *copies):
-            tile = work.tile([P, D], BF16, name="wide", bufs=PACK)
             for copy, cols in zip(copies, split(D, len(copies))):
-                copy(out=tile[:, cols], in_=gen_tiles[k][:, cols].bitcast(FP8))
-            wide[k] = tile[:]
+                copy(out=wide[k][:, cols], in_=gen_tiles[k][:, cols].bitcast(FP8))
 
         def widen_part(k, copy, cols):
             copy(out=wide[k][:, cols], in_=gen_tiles[k][:, cols].bitcast(FP8))
 
-        def sort_aside():
-            tile = work.tile([P, len(SORTED), 2, G * P], F32, name="sorted", tag="first_half", bufs=1, align_bytes=64)
-            for i, k in enumerate(SORTED):
-                on_gpsimd(out=tile[:, i], in_=wide[k].bitcast(F32).rearrange("p (w u) -> p u w", u=2))
-                wide[k] = tile[:, i].rearrange("p u w -> p (u w)").bitcast(BF16)
+        def sort_aside(run, first, count, kib):
+            tile = placed("sorted%d" % first, kib, count * D // 2, F32)
+            on_gpsimd(out=tile.rearrange("p (i u w) -> p i u w", i=count, u=2),
+                      in_=run[:, : count * D].bitcast(F32).rearrange("p (i w u) -> p i u w", i=count, u=2))
+            for i in range(count):
+                wide[first + i] = tile[:, i * D // 2 : (i + 1) * D // 2].bitcast(BF16)
+
+        def sort_on(copy, k, kib):
+            tile = placed("sorted%d" % k, kib, D // 2, F32)
+            copy(out=tile.rearrange("p (u w) -> p u w", u=2), in_=wide[k].bitcast(F32).rearrange("p (w u) -> p u w", u=2))
+            wide[k] = tile.bitcast(BF16)
 
         def turn(rows, tag, is_sorted):
             words = rows.bitcast(F32)
             by_u = words.rearrange("p (u g q) -> p u g q" if is_sorted else "p (g q u) -> p u g q", u=2, g=G)
             banks = []
             for x in range(2):
-                bank = psum.tile([P, BANK], F32, name="bank", tag=tag)
+                bank = new_bank(tag)
                 for i in range(2):
                     for u in range(2):
                         col = (2 * u + i) * P
@@ -130,12 +146,13 @@ def tile_kid_bootstrap_witness_s13_kernel(tc, gen_bytes, gen_scale, real, imp, m
         turned = {}
         gen_grouped = {}
         real_grouped = {}
+        real_banks = {}
 
         def turn_gen(k):
-            turned[k] = turn(wide[k], "held", k in SORTED)
+            turned[k] = turn(wide[k], "passing" if k < 2 else "held", k in SORTED)
 
         def turn_gen_by_product(k, x):
-            bank = psum.tile([P, BANK], F32, name="bank", tag="held")
+            bank = new_bank("held")
             planes = bank[:].bitcast(BF16).rearrange("p (g t r) -> p g t r", g=2, t=PACK)
             by_t = wide[k].rearrange("p (g q t) -> p g t q", g=G, t=PACK)
             for i in range(2):
@@ -146,57 +163,69 @@ def tile_kid_bootstrap_witness_s13_kernel(tc, gen_bytes, gen_scale, real, imp, m
         def scale_gen(k, order=(1, 0)):
             pair = k // 2
             if pair not in gen_grouped:
-                gen_grouped[pair] = work.tile([P, 2 * G, P, PACK], BF16, name="gen_grouped", bufs=2, align_bytes=64)[:]
+                gen_grouped[pair] = placed("gen_grouped%d" % pair, (88, 96, 88, 96, 48, 56)[pair], 2 * D, BF16)
+            rows = gen_grouped[pair].rearrange("p (g r u e) -> p g r u e", r=P, u=2, e=2)
             for x in order:
                 g0 = G * (k % 2) + 2 * x
                 held = "p (g u e r) -> p g r u e" if k in BY_PRODUCT else "p (u g r e) -> p g r u e"
                 values = turned[k][x][:].bitcast(BF16).rearrange(held, g=2, u=2, e=2)
                 by_d = scale_cols[:, 2 * x : 2 * x + 2].rearrange("p g (u e) -> p g u e", u=2).unsqueeze(2).to_broadcast([P, 2, P, 2, 2])
-                nc.vector.tensor_tensor(out=gen_grouped[pair][:, g0 : g0 + 2].rearrange("p g r (u e) -> p g r u e", u=2),
-                                        in0=values, in1=by_d, op=MULT)
+                nc.vector.tensor_tensor(out=rows[:, g0 : g0 + 2], in0=values, in1=by_d, op=MULT)
 
         def turn_real(j):
+            real_banks[j] = turn(real_tiles[j], "passing", False)
+
+        def empty_real(j, which=(0, 1)):
             h = j // JT
-            if h not in real_grouped:
-                tag, bufs = (("first_half", 1), ("stage", STAGE_BUFS))[h]
-                real_grouped[h] = work.tile([P, G, HN, PACK], BF16, name="real_grouped", tag=tag, bufs=bufs, align_bytes=64)
-            words = real_grouped[h][:].rearrange("p g r t -> p (g r t)").bitcast(F32).rearrange("p (g r u) -> p g r u", g=G, u=2)
-            place = slice(j % JT * P, (j % JT + 1) * P)
-            for x, bank in enumerate(turn(real_tiles[j], "passing", False)):
-                on_scalar(out=words[:, 2 * x : 2 * x + 2, place], in_=bank[:].rearrange("p (u g r) -> p g r u", g=2, u=2))
+            for x in which:
+                if (h, x) not in real_grouped:
+                    real_grouped[h, x] = placed("real_grouped%d%d" % (h, x), 32 + 16 * h + 8 * x, 2 * HN * PACK, BF16)
+                words = real_grouped[h, x].bitcast(F32).rearrange("p (g r u) -> p g r u", g=2, u=2)
+                on_scalar(out=words[:, :, j % JT * P : (j % JT + 1) * P], in_=real_banks[j][x][:].rearrange("p (u g r) -> p g r u", g=2, u=2))
 
         gcodes = {}
 
-        def quant_gen(pair):
+        def quant_gen(pair, parts=1):
             codes = work.tile([P, 2, G * P], U32, name="gcodes", bufs=4, align_bytes=MX_ALIGN)
             scales = work.tile([P, 2, G * P], U8, name="gscales", bufs=4, align_bytes=MX_ALIGN)
-            nc.vector.quantize_mx(out=codes[:].rearrange("p i n -> p (i n)").bitcast(FP8X4), scales=scales[:].rearrange("p i n -> p (i n)"),
-                                  in_=gen_grouped[pair].rearrange("p g r t -> p (g r t)"))
+            for cols, values in zip(split(2 * G * P, parts), split(2 * D, parts)):
+                nc.vector.quantize_mx(out=codes[:].rearrange("p i n -> p (i n)")[:, cols].bitcast(FP8X4),
+                                      scales=scales[:].rearrange("p i n -> p (i n)")[:, cols], in_=gen_grouped[pair][:, values])
             for i in range(2):
                 gcodes[2 * pair + i] = (codes[:, i], scales[:, i])
 
-        def quant_real(h):
-            for passes in split(G, 2):
-                nc.vector.quantize_mx(out=rcodes[:, h, passes].rearrange("p g n -> p (g n)").bitcast(FP8X4),
-                                      scales=rscales[:, h, passes].rearrange("p g n -> p (g n)"),
-                                      in_=real_grouped[h][:, passes].rearrange("p g r t -> p (g r t)"))
+        def quant_real(h, x):
+            passes = slice(2 * x, 2 * x + 2)
+            nc.vector.quantize_mx(out=rcodes[:, h, passes].rearrange("p g n -> p (g n)").bitcast(FP8X4),
+                                  scales=rscales[:, h, passes].rearrange("p g n -> p (g n)"), in_=real_grouped[h, x])
 
         factors = {}
+        dot_banks = {}
 
-        def dots(k, h):
+        def dots(k, halves=range(H)):
             codes, scales = gcodes[k]
-            bank = psum.tile([P, BANK], F32, name="bank", tag="passing")
+            for h in halves:
+                dot_banks[k, h] = new_bank("passing")
             for g in range(G):
                 m = slice(g * P, (g + 1) * P)
-                nc.tensor.matmul_mx(out=bank[:], lhsT=codes[:, m].bitcast(FP8X4), lhsT_scale=scales[:, m],
-                                    rhs=rcodes[:, h, g].bitcast(FP8X4), rhs_scale=rscales[:, h, g],
-                                    start=(g == 0), stop=(g == G - 1))
+                for h in halves:
+                    nc.tensor.matmul_mx(out=dot_banks[k, h][:], lhsT=codes[:, m].bitcast(FP8X4), lhsT_scale=scales[:, m],
+                                        rhs=rcodes[:, h, g].bitcast(FP8X4), rhs_scale=rscales[:, h, g],
+                                        start=(g == 0), stop=(g == G - 1))
+
+        def factor(k, halves=range(H)):
             c, t = k // PACK, k % PACK
-            if (c, h) not in factors:
-                factors[c, h] = work.tile([P, 2, PACK, HN], F32, name="factors", tag="stage", bufs=STAGE_BUFS, align_bytes=64)
             weight = imp32[:, k : k + 1]
-            nc.scalar.activation(out=factors[c, h][:, 0, t], in_=bank[:], func=SQUARE, bias=one[:])
-            nc.scalar.activation(out=factors[c, h][:, 1, t], in_=bank[:], func=IDENTITY, scale=weight, bias=weight)
+            for h in halves:
+                if (c, h) not in factors:
+                    kib = ((104, 120), (136, 0), (16, 104))[c][h]
+                    factors[c, h] = placed("factors%d%d" % (c, h), kib, 2 * PACK * HN, F32).rearrange("p (f t n) -> p f t n", f=2, t=PACK)
+                nc.scalar.activation(out=factors[c, h][:, 0, t], in_=dot_banks[k, h][:], func=SQUARE, bias=1.0)
+                nc.scalar.activation(out=factors[c, h][:, 1, t], in_=dot_banks[k, h][:], func=IDENTITY, scale=weight, bias=weight)
+
+        def inner(k, halves=range(H)):
+            dots(k, halves)
+            factor(k, halves)
 
         ker = {}
         kcodes = {}
@@ -207,16 +236,16 @@ def tile_kid_bootstrap_witness_s13_kernel(tc, gen_bytes, gen_scale, real, imp, m
                                  in0=both[:, 0, :, cols].rearrange("p t (n i) -> p n t i", i=run),
                                  in1=both[:, 1, :, cols].rearrange("p t (n i) -> p n t i", i=run), op=MULT)
 
-        def multiply_on_vector(c, h, cols):
-            multiply(nc.vector, c, h, cols, 2)
+        def new_ker(c, h, kib):
+            ker[c, h] = placed("ker%d%d" % (c, h), kib, HN * PACK, BF16).rearrange("p (n t) -> p n t", t=PACK)
 
         def product(c, h, parts=1):
-            ker[c, h] = work.tile([P, HN, PACK], BF16, name="ker", bufs=2, align_bytes=64)[:]
+            new_ker(c, h, (76, 80, 84)[2 * (c - 1) + h - 1])
             for cols in split(HN, parts):
-                multiply_on_vector(c, h, cols)
+                multiply(nc.vector, c, h, cols, 2)
 
-        def product_aside(c, h, pair, share):
-            ker[c, h] = gen_grouped[pair][:, :G].rearrange("p g r t -> p (g r) t")
+        def product_aside(c, h, kib, share):
+            new_ker(c, h, kib)
             multiply(nc.gpsimd, c, h, slice(0, share), 4)
 
         def quant_ker(c, h, parts=1):
@@ -227,127 +256,154 @@ def tile_kid_bootstrap_witness_s13_kernel(tc, gen_bytes, gen_scale, real, imp, m
                                       in_=ker[c, h][:, cols].rearrange("p n t -> p (n t)"))
             kcodes[c, h] = (codes, scales)
 
+        def quant_cols(c, h, cols):
+            codes, scales = kcodes[c, h]
+            nc.vector.quantize_mx(out=codes[:, cols].bitcast(FP8X4), scales=scales[:, cols], in_=ker[c, h][:, cols].rearrange("p n t -> p (n t)"))
+
         sums = {}
 
-        def witness(h, blocks, chunks):
+        def witness(part, blocks, chunks):
+            h, cols, tag = part
             for b in blocks:
-                if (h, b) not in sums:
-                    sums[h, b] = psum.tile([P, BANK], F32, name="bank", tag=("held", "passing")[h])
+                if (h, cols.start, b) not in sums:
+                    sums[h, cols.start, b] = new_bank(tag, cols.stop - cols.start)
                 for c in chunks:
                     codes, scales = kcodes[c, h]
-                    nc.tensor.matmul_mx(out=sums[h, b][:], lhsT=wwords[:, c, 2 * P * b : 2 * P * (b + 1)].bitcast(FP4X4),
+                    nc.tensor.matmul_mx(out=sums[h, cols.start, b][:], lhsT=wwords[:, c, 2 * P * b : 2 * P * (b + 1)].bitcast(FP4X4),
                                         lhsT_scale=wscales[:, c, P * b : P * (b + 1)],
-                                        rhs=codes[:].bitcast(FP8X4), rhs_scale=scales[:],
+                                        rhs=codes[:, cols].bitcast(FP8X4), rhs_scale=scales[:, cols],
                                         start=(c == 0), stop=(c == C - 1))
 
-        def emit(h, b, copy, parts=1):
-            tile = work.tile([P, HN], F32, name="result", tag="rows", bufs=H * JT)
-            for cols in split(HN, parts):
-                copy(out=tile[:, cols], in_=sums[h, b][:, cols])
-                nc.sync.dma_start(out=out[b * P : (b + 1) * P, h * HN : (h + 1) * HN][:, cols], in_=tile[:, cols])
+        def emit(part, b, copy):
+            h, cols, tag = part
+            tile = placed("result%d%d%d" % (h, b, cols.start), (32, 40)[h] + 2 * b + cols.start * 4 // KIB, cols.stop - cols.start, F32)
+            copy(out=tile, in_=sums[h, cols.start, b][:])
+            nc.sync.dma_start(out=out[b * P : (b + 1) * P, h * HN : (h + 1) * HN][:, cols], in_=tile)
 
-        load_gen(0, G)
-        load_gen(1, 2)
+        load_gen(0, 2)
+        load_gen(1)
         nc.sync.dma_start(out=scale_cols[:], in_=gen_scale.rearrange("o (g p t) -> p (o g) t", p=P, t=PACK))
-        for j in range(2):
-            load_real(j)
-            load_gen(j + 2)
-        load_gen(4)
-        for j in range(2, JT):
-            load_real(j)
+        for k in range(2, 5):
+            load_gen(k)
+        load_real(0)
+        load_real(1)
         load_gen(5)
-
-        nc.vector.memset(zero[:], 0.0)
-        nc.scalar.activation(out=one[:], in_=zero[:], func=IDENTITY, bias=1.0)
-
+        load_real(2)
+        load_real(3)
+        for k in range(PACK):
+            wide_run(k, 1, 64 + 4 * k)
         widen(0, on_vector, on_scalar, on_vector, on_scalar)
         widen(1, on_vector, on_scalar)
-        for j in range(JT, JT + 2):
-            load_real(j)
-            load_gen(j + 2)
-        for j in range(JT + 2, H * JT):
-            load_real(j)
+        load_gen(6)
+        load_real(4)
+        load_real(5)
+        load_gen(7)
+        load_real(6)
+        load_real(7)
         load_gen_pair(4)
         nc.sync.dma_start(out=imp_raw[:], in_=imp.rearrange("(c p t) -> p c t", p=P, t=PACK))
         load_gen_pair(5)
         load_mult()
-        turn_gen(0)
-        turn_gen(1)
         widen(2, on_scalar, on_scalar)
         widen(3, on_scalar, on_scalar)
-        for k in range(2):
+        for k in range(PACK):
+            turn_gen(k)
+        wide_run(4, 2, 80)
+        widen(4, on_gpsimd)
+        widen(5, on_gpsimd)
+        for k in range(PACK):
             scale_gen(k, (0, 1))
             turn_real(k)
-            turn_gen(k + 2)
-        turn_real(2)
-        scale_gen(2, (0, 1))
-        scale_gen(3, (0, 1))
-        pair_tile = work.tile([P, 2, D], BF16, name="wide_pair", tag="stage", bufs=STAGE_BUFS, align_bytes=64)
-        wide[4], wide[5] = pair_tile[:, 0], pair_tile[:, 1]
-        widen_part(4, on_gpsimd, slice(0, D))
-        widen_part(5, on_gpsimd, slice(0, CAST_ASIDE))
-
-        for i in range(4):
-            if i == 3:
-                quant_gen(0)
-                quant_real(0)
-            turn_real(JT - 1 + i)
-            turn_gen_by_product(BY_PRODUCT[i // 2], i % 2)
-            if i == 1:
-                widen_part(5, on_scalar, slice(CAST_ASIDE, D))
-            if i != 2:
-                widen(SORTED[min(i, 2)], on_scalar)
-        sort_aside()
+            empty_real(k)
+        first_run = wide_run(6, 3, 64)
+        widen_part(6, on_gpsimd, slice(0, 1024))
+        widen_part(6, on_scalar, slice(1024, D))
+        turn_gen_by_product(4, 0)
+        turn_real(4)
+        empty_real(4)
+        turn_gen_by_product(4, 1)
+        widen(7, on_scalar)
+        turn_real(5)
+        empty_real(5)
+        turn_gen_by_product(5, 0)
+        quant_gen(0)
+        quant_real(0, 0)
+        quant_real(0, 1)
+        turn_real(6)
+        empty_real(6)
+        turn_gen_by_product(5, 1)
+        widen(8, on_scalar)
+        sort_aside(first_run, 6, 2, 40)
+        sort_aside(first_run[:, 2 * D :], 8, 1, 36)
         quant_gen(1)
-        for k in BY_PRODUCT:
-            scale_gen(k, (0, 1))
+        scale_gen(4, (0, 1))
+        scale_gen(5, (0, 1))
         nc.scalar.activation(out=imp32[:], in_=imp_raw[:].rearrange("p c t -> p (c t)"), func=IDENTITY)
-        turn_real(H * JT - 1)
+        turn_real(7)
+        empty_real(7)
         for t in range(PACK):
-            dots(t, 0)
-        quant_real(1)
+            inner(t, [0])
+        quant_real(1, 0)
+        quant_real(1, 1)
         quant_gen(2)
-
-        groups = [(c, h) for c in range(C) for h in range(H)]
-        todo = [(k, h) for c, h in groups[1:] for k in range(PACK * c, PACK * (c + 1))]
-        todo.remove((KT - PACK, 1))
-        todo.insert(todo.index((KT - 2, 0)), (KT - PACK, 1))
-        uncast = list(range(SORTED[-1] + 1, KT))
-        for step, pair in enumerate(range(3, PAIRS)):
-            product_aside(*groups[step], pair - 1, SHARES[step])
-            one_run = 2 * pair + 1 in SORTED
-            for k in (2 * pair, 2 * pair + 1):
-                turn_gen(k)
-                if uncast and (k % 2 == 0 or not one_run):
-                    widen(uncast.pop(0), on_scalar)
-                if k % 2 == 0 and not one_run:
-                    dots(*todo.pop(0))
-                if k == SORTED[-1]:
-                    late = work.tile([P, 2, 2 * G, P, PACK], BF16, name="late", tag="first_half", bufs=1, align_bytes=64)
-                    gen_grouped[pair], gen_grouped[pair + 1] = late[:, 0], late[:, 1]
-            scale_gen(2 * pair)
-            scale_gen(2 * pair + 1)
-            for i in range(AFTER[step]):
-                dots(*todo.pop(0))
-            multiply_on_vector(*groups[step], slice(SHARES[step], HN))
-            quant_gen(pair)
-
+        wide_run(9, 3, 76)
+        product_aside(0, 0, 88, 416)
+        turn_gen(6)
+        turn_gen(7)
+        widen(9, on_scalar)
+        scale_gen(6)
+        scale_gen(7)
+        for k, h in ((0, 1), (1, 1), (2, 1), (3, 1), (4, 0)):
+            inner(k, [h])
+        multiply(nc.vector, 0, 0, slice(416, HN), 2)
+        quant_gen(3)
+        product_aside(0, 1, 96, SHARE)
+        turn_gen(8)
+        widen(10, on_scalar)
+        inner(5, [0])
+        turn_gen(9)
+        widen(11, on_scalar)
+        scale_gen(8)
+        scale_gen(9)
+        for k, h in ((6, 0), (7, 0), (4, 1)):
+            inner(k, [h])
+        sort_on(on_vector, 10, 68)
+        sort_on(on_vector, 11, 72)
+        quant_gen(4)
+        product_aside(1, 0, 48, SHARE)
+        inner(5, [1])
+        turn_gen(10)
+        turn_gen(11)
+        scale_gen(10)
+        scale_gen(11)
+        for k, h in ((6, 1), (7, 1), (8, 0), (9, 0), (8, 1)):
+            inner(k, [h])
+        quant_gen(5, 2)
+        multiply(nc.vector, 0, 1, slice(SHARE, HN), 2)
+        multiply(nc.vector, 1, 0, slice(SHARE, HN), 2)
         last = C - 1
-        product(last - 1, 1)
-        for group in groups[: 2 * last]:
-            quant_ker(*group)
-        for unit in todo:
-            dots(*unit)
+        first, second = (0, slice(0, HN), "held"), (1, slice(0, HN), "passing")
+        halves = [(1, cols, "held") for cols in split(HN, 2)]
+        product(1, 1)
+        for c, h in ((0, 0), (1, 0)):
+            quant_ker(c, h)
+        for k, h in ((10, 0), (11, 0), (9, 1), (10, 1), (11, 1)):
+            inner(k, [h])
         product(last, 0)
-        witness(0, range(B - 1), range(last))
+        quant_ker(0, 1)
+        witness(first, range(3), range(last))
         quant_ker(last, 0)
-        witness(0, range(B - 1), [last])
-        witness(0, [B - 1], range(C))
+        quant_ker(1, 1)
+        witness(first, range(3), [last])
+        witness(first, range(3, B), range(C))
         product(last, 1, 2)
         for b in range(B):
-            emit(0, b, on_scalar)
-        witness(1, range(B - 1), range(last))
+            emit(first, b, on_scalar)
+        witness(second, range(2), range(last))
         quant_ker(last, 1, 2)
-        for b in range(B):
-            witness(1, [b], [last] if b < B - 1 else range(C))
-            emit(1, b, on_vector if b % 2 else on_scalar, 2 if b in (0, B - 1) else 1)
+        for b in range(B - 1):
+            witness(second, [b], [last] if b < 2 else range(C))
+            emit(second, b, on_vector if b % 2 else on_scalar)
+        for i, part in enumerate(halves):
+            witness(part, [B - 1], range(C))
+            emit(part, B - 1, on_vector if i else on_scalar)

@@ -31,9 +31,9 @@ B = R // P
 BANK = 512
 MX_ALIGN = 256
 KIB = 1024
-BY_PRODUCT = (4, 5)
+BY_PRODUCT = (5,)
 CAST_ASIDE = D - P * PACK
-SORTED = (6, 7, 8, 10, 11)
+SORTED = (6, 7, 8, 9)
 SHARE = 432
 
 
@@ -293,7 +293,7 @@ def tile_kid_bootstrap_witness_s13_kernel(tc, gen_bytes, gen_scale, real, imp, m
         for k in range(PACK):
             wide_run(k, 1, 64 + 4 * k)
         widen(0, on_vector, on_scalar, on_vector, on_scalar)
-        widen(1, on_vector, on_scalar)
+        widen(1, on_scalar, on_scalar)
         load_gen(6)
         load_real(4)
         load_real(5)
@@ -318,10 +318,9 @@ def tile_kid_bootstrap_witness_s13_kernel(tc, gen_bytes, gen_scale, real, imp, m
         first_run = wide_run(6, 3, 64)
         widen_part(6, on_gpsimd, slice(0, 1024))
         widen_part(6, on_scalar, slice(1024, D))
-        turn_gen_by_product(4, 0)
+        turn_gen(4)
         turn_real(4)
         empty_real(4)
-        turn_gen_by_product(4, 1)
         widen(7, on_scalar)
         turn_real(5)
         empty_real(5)
@@ -351,49 +350,48 @@ def tile_kid_bootstrap_witness_s13_kernel(tc, gen_bytes, gen_scale, real, imp, m
         turn_gen(6)
         turn_gen(7)
         widen(9, on_scalar)
+        inner(0, [1])
+        sort_on(on_scalar, 9, 64)
         scale_gen(6)
         scale_gen(7)
-        for k, h in ((0, 1), (1, 1), (2, 1), (3, 1), (4, 0)):
+        for k, h in ((1, 1), (2, 1), (3, 1), (4, 0)):
             inner(k, [h])
         multiply(nc.vector, 0, 0, slice(416, HN), 2)
         quant_gen(3)
         product_aside(0, 1, 96, SHARE)
         turn_gen(8)
+        turn_gen(9)
         widen(10, on_scalar)
         inner(5, [0])
-        turn_gen(9)
         widen(11, on_scalar)
         scale_gen(8)
         scale_gen(9)
         for k, h in ((6, 0), (7, 0), (4, 1)):
             inner(k, [h])
-        sort_on(on_vector, 10, 68)
-        sort_on(on_vector, 11, 72)
+        multiply(nc.vector, 0, 1, slice(SHARE, HN), 2)
         quant_gen(4)
         product_aside(1, 0, 48, SHARE)
-        inner(5, [1])
         turn_gen(10)
+        inner(5, [1])
         turn_gen(11)
         scale_gen(10)
         scale_gen(11)
         for k, h in ((6, 1), (7, 1), (8, 0), (9, 0), (8, 1)):
             inner(k, [h])
-        quant_gen(5, 2)
-        multiply(nc.vector, 0, 1, slice(SHARE, HN), 2)
         multiply(nc.vector, 1, 0, slice(SHARE, HN), 2)
+        quant_gen(5)
         last = C - 1
         first, second = (0, slice(0, HN), "held"), (1, slice(0, HN), "passing")
         halves = [(1, cols, "held") for cols in split(HN, 2)]
         product(1, 1)
-        for c, h in ((0, 0), (1, 0)):
+        for c, h in ((0, 0), (1, 0), (0, 1)):
             quant_ker(c, h)
         for k, h in ((10, 0), (11, 0), (9, 1), (10, 1), (11, 1)):
             inner(k, [h])
         product(last, 0)
-        quant_ker(0, 1)
+        quant_ker(1, 1)
         witness(first, range(3), range(last))
         quant_ker(last, 0)
-        quant_ker(1, 1)
         witness(first, range(3), [last])
         witness(first, range(3, B), range(C))
         product(last, 1, 2)

@@ -63,12 +63,16 @@ def tile_kid_bootstrap_witness_s13_kernel(tc, gen_bytes, gen_scale, real, imp, m
         wwords = keep.tile([P, C, 2 * R], U8, name="wwords", align_bytes=MX_ALIGN)
         wscales = keep.tile([P, C, R], U8, name="wscales", align_bytes=MX_ALIGN)
         imp_raw = keep.tile([P, C, PACK], BF16, name="imp_raw")
+        zero = keep.tile([P, 1], F32, name="zero")
+        one = keep.tile([P, 1], F32, name="one")
         imp32 = keep.tile([P, KT], F32, name="imp32")
         rcodes = keep.tile([P, H, G, HN], U32, name="rcodes", align_bytes=MX_ALIGN)
         rscales = keep.tile([P, H, G, HN], U8, name="rscales", align_bytes=MX_ALIGN)
 
         nc.vector.memset(wscales[:].rearrange("p c n -> p (c n)").bitcast(I32), 0)
-        nc.scalar.activation(out=ident16[:], in_=ident[:], func=IDENTITY)
+        nc.vector.memset(zero[:], 0.0)
+        nc.scalar.activation(out=one[:], in_=zero[:], func=IDENTITY, bias=1.0)
+        nc.vector.tensor_copy(out=ident16[:], in_=ident[:])
 
         on_vector, on_scalar, on_gpsimd = nc.vector.tensor_copy, nc.scalar.copy, nc.gpsimd.tensor_copy
 
@@ -220,7 +224,7 @@ def tile_kid_bootstrap_witness_s13_kernel(tc, gen_bytes, gen_scale, real, imp, m
                 if (c, h) not in factors:
                     kib = ((104, 120), (136, 0), (16, 104))[c][h]
                     factors[c, h] = placed("factors%d%d" % (c, h), kib, 2 * PACK * HN, F32).rearrange("p (f t n) -> p f t n", f=2, t=PACK)
-                nc.scalar.activation(out=factors[c, h][:, 0, t], in_=dot_banks[k, h][:], func=SQUARE, bias=1.0)
+                nc.scalar.activation(out=factors[c, h][:, 0, t], in_=dot_banks[k, h][:], func=SQUARE, bias=one[:])
                 nc.scalar.activation(out=factors[c, h][:, 1, t], in_=dot_banks[k, h][:], func=IDENTITY, scale=weight, bias=weight)
 
         def inner(k, halves=range(H)):

@@ -31,9 +31,9 @@ B = R // P
 BANK = 512
 MX_ALIGN = 256
 KIB = 1024
-BY_PRODUCT = (5,)
+BY_PRODUCT = (4, 5)
 CAST_ASIDE = D - P * PACK
-SORTED = (6, 7, 8, 9)
+SORTED = (6, 7, 8)
 SHARE = 432
 
 
@@ -82,9 +82,10 @@ def tile_kid_bootstrap_witness_s13_kernel(tc, gen_bytes, gen_scale, real, imp, m
         gen_rows = gen_bytes.rearrange("(c p t) k -> c p t k", p=P, t=PACK)
         gen_tiles = {}
         real_tiles = {}
+        gen_pairs = {}
 
         def load_gen(k, parts=1):
-            tile = work.tile([P, D], U8, name="gen_in", bufs=6)
+            tile = work.tile([P, D], U8, name="gen_in", bufs=5)
             for cols in split(D, parts):
                 nc.sync.dma_start(out=tile[:, cols], in_=gen_rows[k // PACK][:, k % PACK, cols])
             gen_tiles[k] = tile[:]
@@ -93,6 +94,7 @@ def tile_kid_bootstrap_witness_s13_kernel(tc, gen_bytes, gen_scale, real, imp, m
             tile = work.tile([P, 2, D], U8, name="gen_pair_in", bufs=2)
             t = 2 * pair % PACK
             nc.sync.dma_start(out=tile[:], in_=gen_rows[2 * pair // PACK][:, t : t + 2])
+            gen_pairs[pair] = tile[:].rearrange("p i k -> p (i k)")
             for i in range(2):
                 gen_tiles[2 * pair + i] = tile[:, i]
 
@@ -244,7 +246,7 @@ def tile_kid_bootstrap_witness_s13_kernel(tc, gen_bytes, gen_scale, real, imp, m
             ker[c, h] = placed("ker%d%d" % (c, h), kib, HN * PACK, BF16).rearrange("p (n t) -> p n t", t=PACK)
 
         def product(c, h, parts=1):
-            new_ker(c, h, (76, 80, 84)[2 * (c - 1) + h - 1])
+            new_ker(c, h, (64, 68, 72)[2 * (c - 1) + h - 1])
             for cols in split(HN, parts):
                 multiply(nc.vector, c, h, cols, 2)
 
@@ -278,53 +280,56 @@ def tile_kid_bootstrap_witness_s13_kernel(tc, gen_bytes, gen_scale, real, imp, m
                                         rhs=codes[:, cols].bitcast(FP8X4), rhs_scale=scales[:, cols],
                                         start=(c == 0), stop=(c == C - 1))
 
-        def emit(part, b, copy):
+        def emit(part, b, copy, parts=1):
             h, cols, tag = part
             tile = placed("result%d%d%d" % (h, b, cols.start), (32, 40)[h] + 2 * b + cols.start * 4 // KIB, cols.stop - cols.start, F32)
-            copy(out=tile, in_=sums[h, cols.start, b][:])
-            nc.sync.dma_start(out=out[b * P : (b + 1) * P, h * HN : (h + 1) * HN][:, cols], in_=tile)
+            for some in split(cols.stop - cols.start, parts):
+                copy(out=tile[:, some], in_=sums[h, cols.start, b][:, some])
+                nc.sync.dma_start(out=out[b * P : (b + 1) * P, h * HN : (h + 1) * HN][:, cols][:, some], in_=tile[:, some])
 
         load_gen(0, 2)
         load_gen(1)
         nc.sync.dma_start(out=scale_cols[:], in_=gen_scale.rearrange("o (g p t) -> p (o g) t", p=P, t=PACK))
-        for k in range(2, 5):
-            load_gen(k)
-        load_real(0)
-        load_real(1)
-        load_gen(5)
-        load_real(2)
+        load_gen(2)
+        load_gen(3)
+        load_gen_pair(2)
+        for j in range(3):
+            load_real(j)
+        load_gen(6)
         load_real(3)
         for k in range(PACK):
             wide_run(k, 1, 64 + 4 * k)
         widen(0, on_vector, on_scalar, on_vector, on_scalar)
-        widen(1, on_scalar, on_scalar)
-        load_gen(6)
+        widen(1, on_vector, on_scalar)
         load_real(4)
         load_real(5)
         load_gen(7)
         load_real(6)
         load_real(7)
+        widen(2, on_scalar, on_scalar)
+        widen(3, on_scalar, on_scalar)
+        wide_run(4, 1, 80)
+        wide_run(5, 1, 84)
+        widen(4, on_scalar)
+        widen(5, on_gpsimd)
         load_gen_pair(4)
         nc.sync.dma_start(out=imp_raw[:], in_=imp.rearrange("(c p t) -> p c t", p=P, t=PACK))
         load_gen_pair(5)
         load_mult()
-        widen(2, on_scalar, on_scalar)
-        widen(3, on_scalar, on_scalar)
         for k in range(PACK):
             turn_gen(k)
-        wide_run(4, 2, 80)
-        widen(4, on_gpsimd)
-        widen(5, on_gpsimd)
-        for k in range(PACK):
+        for k in range(3):
             scale_gen(k, (0, 1))
             turn_real(k)
             empty_real(k)
         first_run = wide_run(6, 3, 64)
-        widen_part(6, on_gpsimd, slice(0, 1024))
-        widen_part(6, on_scalar, slice(1024, D))
-        turn_gen(4)
-        turn_real(4)
-        empty_real(4)
+        widen(6, on_gpsimd)
+        turn_gen_by_product(4, 0)
+        scale_gen(3, (0, 1))
+        for j in (3, 4):
+            turn_real(j)
+            empty_real(j)
+        turn_gen_by_product(4, 1)
         widen(7, on_scalar)
         turn_real(5)
         empty_real(5)
@@ -338,35 +343,35 @@ def tile_kid_bootstrap_witness_s13_kernel(tc, gen_bytes, gen_scale, real, imp, m
         widen(8, on_scalar)
         sort_aside(first_run, 6, 2, 40)
         sort_aside(first_run[:, 2 * D :], 8, 1, 36)
+        wide_run(9, 1, 76)
         quant_gen(1)
         scale_gen(4, (0, 1))
         scale_gen(5, (0, 1))
         nc.scalar.activation(out=imp32[:], in_=imp_raw[:].rearrange("p c t -> p (c t)"), func=IDENTITY)
         turn_real(7)
         empty_real(7)
-        for t in range(PACK):
+        for t in range(3):
             inner(t, [0])
+        turn_gen(6)
+        inner(3, [0])
         quant_real(1, 0)
         quant_real(1, 1)
         quant_gen(2)
-        wide_run(9, 3, 76)
+        wide_run(10, 2, 80)
         product_aside(0, 0, 88, 416)
-        turn_gen(6)
         turn_gen(7)
         widen(9, on_scalar)
-        inner(0, [1])
-        sort_on(on_scalar, 9, 64)
         scale_gen(6)
         scale_gen(7)
-        for k, h in ((1, 1), (2, 1), (3, 1), (4, 0)):
+        for k, h in ((0, 1), (1, 1), (2, 1), (3, 1), (4, 0)):
             inner(k, [h])
         multiply(nc.vector, 0, 0, slice(416, HN), 2)
         quant_gen(3)
         product_aside(0, 1, 96, SHARE)
         turn_gen(8)
-        turn_gen(9)
         widen(10, on_scalar)
         inner(5, [0])
+        turn_gen(9)
         widen(11, on_scalar)
         scale_gen(8)
         scale_gen(9)
@@ -386,26 +391,21 @@ def tile_kid_bootstrap_witness_s13_kernel(tc, gen_bytes, gen_scale, real, imp, m
         quant_gen(5)
         last = C - 1
         first, second = (0, slice(0, HN), "held"), (1, slice(0, HN), "passing")
-        halves = [(1, cols, "held") for cols in split(HN, 2)]
         product(1, 1)
-        for c, h in ((0, 0), (1, 0), (0, 1)):
+        for c, h in ((0, 0), (1, 0), (0, 1), (1, 1)):
             quant_ker(c, h)
         for k, h in ((10, 0), (11, 0), (9, 1), (10, 1), (11, 1)):
             inner(k, [h])
-        product(last, 0)
-        quant_ker(1, 1)
+        product(last, 0, 2)
         witness(first, range(3), range(last))
-        quant_ker(last, 0)
+        quant_ker(last, 0, 2)
         witness(first, range(3), [last])
         witness(first, range(3, B), range(C))
         product(last, 1, 2)
         for b in range(B):
             emit(first, b, on_scalar)
-        witness(second, range(2), range(last))
+        witness(second, range(B - 1), range(last))
         quant_ker(last, 1, 2)
-        for b in range(B - 1):
-            witness(second, [b], [last] if b < 2 else range(C))
-            emit(second, b, on_vector if b % 2 else on_scalar)
-        for i, part in enumerate(halves):
-            witness(part, [B - 1], range(C))
-            emit(part, B - 1, on_vector if i else on_scalar)
+        for b in range(B):
+            witness(second, [b], [last] if b < B - 1 else range(C))
+            emit(second, b, on_vector if b % 2 else on_scalar, 2 if b in (0, B - 1) else 1)

@@ -35,6 +35,8 @@ BY_PRODUCT = (4, 5)
 CAST_ASIDE = D - P * PACK
 SORTED = (6, 7, 8)
 SHARE = 432
+WARM_REAL = (2, 1, 1, 0, 1, 0, 0, 0)
+WARM_GEN = {}
 
 
 def tile_kid_bootstrap_witness_s13_kernel(tc, gen_bytes, gen_scale, real, imp, mult_words, mult_scales, out):
@@ -136,17 +138,17 @@ def tile_kid_bootstrap_witness_s13_kernel(tc, gen_bytes, gen_scale, real, imp, m
             copy(out=tile.rearrange("p (u w) -> p u w", u=2), in_=wide[k].bitcast(F32).rearrange("p (w u) -> p u w", u=2))
             wide[k] = tile.bitcast(BF16)
 
-        def turn(rows, tag, is_sorted):
+        def turn(rows, tag, is_sorted, warm_up=0):
             words = rows.bitcast(F32)
             by_u = words.rearrange("p (u g q) -> p u g q" if is_sorted else "p (g q u) -> p u g q", u=2, g=G)
-            banks = []
-            for x in range(2):
-                bank = new_bank(tag)
+            banks = [new_bank(tag) for x in range(2)]
+            for i in range(warm_up):
+                nc.tensor.matmul(out=banks[1][:], lhsT=ident16[:], rhs=real_tiles[0][:, :BANK], start=True, stop=True)
+            for x, bank in enumerate(banks):
                 for i in range(2):
                     for u in range(2):
                         col = (2 * u + i) * P
                         nc.tensor.transpose(bank[:, col : col + P], by_u[:, u, 2 * x + i], ident[:])
-                banks.append(bank)
             return banks
 
         turned = {}
@@ -155,7 +157,7 @@ def tile_kid_bootstrap_witness_s13_kernel(tc, gen_bytes, gen_scale, real, imp, m
         real_banks = {}
 
         def turn_gen(k):
-            turned[k] = turn(wide[k], "passing" if k < 2 else "held", k in SORTED)
+            turned[k] = turn(wide[k], "passing" if k < 2 else "held", k in SORTED, WARM_GEN.get(k, 0))
 
         def turn_gen_by_product(k, x):
             bank = new_bank("held")
@@ -165,6 +167,23 @@ def tile_kid_bootstrap_witness_s13_kernel(tc, gen_bytes, gen_scale, real, imp, m
                 for t in range(PACK):
                     nc.tensor.matmul(out=planes[:, i, t], lhsT=by_t[:, 2 * x + i, t], rhs=ident16[:], start=True, stop=True)
             turned[k] = turned.get(k, []) + [bank]
+
+        def turn_both(j, k, x):
+            by_u = real_tiles[j].bitcast(F32).rearrange("p (g q u) -> p u g q", u=2, g=G)
+            held = new_bank("held")
+            planes = held[:].bitcast(BF16).rearrange("p (g t r) -> p g t r", g=2, t=PACK)
+            by_t = wide[k].rearrange("p (g q t) -> p g t q", g=G, t=PACK)
+            real_banks[j] = []
+            for y in range(2):
+                bank = new_bank("passing")
+                for i in range(2):
+                    for u in range(2):
+                        col = (2 * u + i) * P
+                        nc.tensor.transpose(bank[:, col : col + P], by_u[:, u, 2 * y + i], ident[:])
+                real_banks[j].append(bank)
+                for t in range(PACK):
+                    nc.tensor.matmul(out=planes[:, y, t], lhsT=by_t[:, 2 * x + y, t], rhs=ident16[:], start=True, stop=True)
+            turned[k] = turned.get(k, []) + [held]
 
         def scale_gen(k, order=(1, 0)):
             pair = k // 2
@@ -179,7 +198,7 @@ def tile_kid_bootstrap_witness_s13_kernel(tc, gen_bytes, gen_scale, real, imp, m
                 nc.vector.tensor_tensor(out=rows[:, g0 : g0 + 2], in0=values, in1=by_d, op=MULT)
 
         def turn_real(j):
-            real_banks[j] = turn(real_tiles[j], "passing", False)
+            real_banks[j] = turn(real_tiles[j], "passing", False, WARM_REAL[j])
 
         def empty_real(j, which=(0, 1)):
             h = j // JT
@@ -218,6 +237,20 @@ def tile_kid_bootstrap_witness_s13_kernel(tc, gen_bytes, gen_scale, real, imp, m
                     nc.tensor.matmul_mx(out=dot_banks[k, h][:], lhsT=codes[:, m].bitcast(FP8X4), lhsT_scale=scales[:, m],
                                         rhs=rcodes[:, h, g].bitcast(FP8X4), rhs_scale=rscales[:, h, g],
                                         start=(g == 0), stop=(g == G - 1))
+
+        def dots_by_halves(tiles, h):
+            for k in tiles:
+                dot_banks[k, h] = new_bank("passing")
+            for x in range(2):
+                for k in tiles:
+                    codes, scales = gcodes[k]
+                    for g in (2 * x, 2 * x + 1):
+                        m = slice(g * P, (g + 1) * P)
+                        nc.tensor.matmul_mx(out=dot_banks[k, h][:], lhsT=codes[:, m].bitcast(FP8X4), lhsT_scale=scales[:, m],
+                                            rhs=rcodes[:, h, g].bitcast(FP8X4), rhs_scale=rscales[:, h, g],
+                                            start=(g == 0), stop=(g == G - 1))
+            for k in tiles:
+                factor(k, [h])
 
         def factor(k, halves=range(H)):
             c, t = k // PACK, k % PACK

from contextlib import ExitStack

import concourse.mybir as mybir
from concourse.masks import make_identity

M, N, D, R = 1536, 1024, 2048, 512
FLOPS = 2 * M * N * D + 2 * M * R * N

F32 = mybir.dt.float32
BF16 = mybir.dt.bfloat16
I32 = mybir.dt.int32
U32 = mybir.dt.uint32
U8 = mybir.dt.uint8
FP8 = mybir.dt.float8_e4m3fn
FP8X4 = mybir.dt.float8_e4m3fn_x4
FP4X4 = mybir.dt.float4_e2m1fn_x4
MULT = mybir.AluOpType.mult
SQUARE = mybir.ActivationFunctionType.Square
IDENTITY = mybir.ActivationFunctionType.Identity

P = 128
PACK = 4
G = D // (P * PACK)
C = M // (P * PACK)
H = 2
HN = N // H
JT = HN // P
KT = C * PACK
PAIRS = KT // 2
B = R // P
BANK = 512
MX_ALIGN = 256
KIB = 1024
BY_PRODUCT = (4, 5)
CAST_ASIDE = D - P * PACK
SORTED = (6, 7, 8)
SHARE = 432
WARM_REAL = (2, 1, 1, 0, 1, 0, 0, 0)
WARM_GEN = {}


def tile_kid_bootstrap_witness_s13_kernel(tc, gen_bytes, gen_scale, real, imp, mult_words, mult_scales, out):
    nc = tc.nc
    with ExitStack() as ctx:
        keep = ctx.enter_context(tc.tile_pool(name="keep", bufs=1))
        work = ctx.enter_context(tc.tile_pool(name="work", bufs=1))
        arena = ctx.enter_context(tc.tile_pool(name="arena", bufs=1))
        psum = ctx.enter_context(tc.psum_pool(name="psum", bufs=1))
        ctx.enter_context(tc.manual_schedule())

        def placed(name, kib, width, dtype):
            return arena.tile([P, width], dtype, name=name, offset=kib * KIB, align_bytes=64)[:]

        taken = {"passing": 0, "held": 0}

        def new_bank(role, width=BANK):
            number = taken[role] % 4
            taken[role] = taken[role] + 1
            return psum.tile([P, width], F32, name="bank", tag="%s%d" % (role, number))

        ident = keep.tile([P, P], F32, name="ident")
        make_identity(nc, ident[:])
        ident16 = keep.tile([P, P], BF16, name="ident16")
        scale_cols = keep.tile([P, G, PACK], F32, name="scale_cols")
        wwords = keep.tile([P, C, 2 * R], U8, name="wwords", align_bytes=MX_ALIGN)
        wscales = keep.tile([P, C, R], U8, name="wscales", align_bytes=MX_ALIGN)
        imp_raw = keep.tile([P, C, PACK], BF16, name="imp_raw")
        zero = keep.tile([P, 1], F32, name="zero")
        one = keep.tile([P, 1], F32, name="one")
        imp32 = keep.tile([P, KT], F32, name="imp32")
        rcodes = keep.tile([P, H, G, HN], U32, name="rcodes", align_bytes=MX_ALIGN)
        rscales = keep.tile([P, H, G, HN], U8, name="rscales", align_bytes=MX_ALIGN)

        nc.vector.memset(wscales[:].rearrange("p c n -> p (c n)").bitcast(I32), 0)
        nc.vector.memset(zero[:], 0.0)
        nc.scalar.activation(out=one[:], in_=zero[:], func=IDENTITY, bias=1.0)
        nc.vector.tensor_copy(out=ident16[:], in_=ident[:])

        on_vector, on_scalar, on_gpsimd = nc.vector.tensor_copy, nc.scalar.copy, nc.gpsimd.tensor_copy

        def split(width, parts):
            return [slice(i * width // parts, (i + 1) * width // parts) for i in range(parts)]

        gen_rows = gen_bytes.rearrange("(c p t) k -> c p t k", p=P, t=PACK)
        gen_tiles = {}
        real_tiles = {}
        gen_pairs = {}

        def load_gen(k, parts=1):
            tile = work.tile([P, D], U8, name="gen_in", bufs=5)
            for cols in split(D, parts):
                nc.sync.dma_start(out=tile[:, cols], in_=gen_rows[k // PACK][:, k % PACK, cols])
            gen_tiles[k] = tile[:]

        def load_gen_pair(pair):
            tile = work.tile([P, 2, D], U8, name="gen_pair_in", bufs=2)
            t = 2 * pair % PACK
            nc.sync.dma_start(out=tile[:], in_=gen_rows[2 * pair // PACK][:, t : t + 2])
            gen_pairs[pair] = tile[:].rearrange("p i k -> p (i k)")
            for i in range(2):
                gen_tiles[2 * pair + i] = tile[:, i]

        def load_real(j):
            real_tiles[j] = placed("real_in%d" % j, 4 * j, D, BF16)
            nc.sync.dma_start(out=real_tiles[j], in_=real[j * P : (j + 1) * P, :])

        def load_mult():
            nc.sync.dma_start(out=wwords[:].rearrange("p c n -> p (c n)").bitcast(I32).rearrange("p (c n) -> p c n", c=C),
                              in_=mult_words.rearrange("c p n -> p c n").bitcast(I32))
            for q in range(4):
                nc.sync.dma_start(out=wscales[32 * q : 32 * q + 4].bitcast(I32),
                                  in_=mult_scales[:, 4 * q : 4 * q + 4, :].rearrange("c q n -> q c n").bitcast(I32))

        wide = {}

        def wide_run(first, count, kib):
            run = placed("wide%d" % first, kib, count * D, BF16)
            for i in range(count):
                wide[first + i] = run[:, i * D : (i + 1) * D]
            return run

        def widen(k, *copies):
            for copy, cols in zip(copies, split(D, len(copies))):
                copy(out=wide[k][:, cols], in_=gen_tiles[k][:, cols].bitcast(FP8))

        def widen_part(k, copy, cols):
            copy(out=wide[k][:, cols], in_=gen_tiles[k][:, cols].bitcast(FP8))

        def sort_aside(run, first, count, kib):
            tile = placed("sorted%d" % first, kib, count * D // 2, F32)
            on_gpsimd(out=tile.rearrange("p (i u w) -> p i u w", i=count, u=2),
                      in_=run[:, : count * D].bitcast(F32).rearrange("p (i w u) -> p i u w", i=count, u=2))
            for i in range(count):
                wide[first + i] = tile[:, i * D // 2 : (i + 1) * D // 2].bitcast(BF16)

        def sort_on(copy, k, kib):
            tile = placed("sorted%d" % k, kib, D // 2, F32)
            copy(out=tile.rearrange("p (u w) -> p u w", u=2), in_=wide[k].bitcast(F32).rearrange("p (w u) -> p u w", u=2))
            wide[k] = tile.bitcast(BF16)

        def turn(rows, tag, is_sorted, warm_up=0):
            words = rows.bitcast(F32)
            by_u = words.rearrange("p (u g q) -> p u g q" if is_sorted else "p (g q u) -> p u g q", u=2, g=G)
            banks = [new_bank(tag) for x in range(2)]
            for i in range(warm_up):
                nc.tensor.matmul(out=banks[1][:], lhsT=ident16[:], rhs=real_tiles[0][:, :BANK], start=True, stop=True)
            for x, bank in enumerate(banks):
                for i in range(2):
                    for u in range(2):
                        col = (2 * u + i) * P
                        nc.tensor.transpose(bank[:, col : col + P], by_u[:, u, 2 * x + i], ident[:])
            return banks

        turned = {}
        gen_grouped = {}
        real_grouped = {}
        real_banks = {}

        def turn_gen(k):
            turned[k] = turn(wide[k], "passing" if k < 2 else "held", k in SORTED, WARM_GEN.get(k, 0))

        def turn_gen_by_product(k, x):
            bank = new_bank("held")
            planes = bank[:].bitcast(BF16).rearrange("p (g t r) -> p g t r", g=2, t=PACK)
            by_t = wide[k].rearrange("p (g q t) -> p g t q", g=G, t=PACK)
            for i in range(2):
                for t in range(PACK):
                    nc.tensor.matmul(out=planes[:, i, t], lhsT=by_t[:, 2 * x + i, t], rhs=ident16[:], start=True, stop=True)
            turned[k] = turned.get(k, []) + [bank]

        def turn_both(j, k, x):
            by_u = real_tiles[j].bitcast(F32).rearrange("p (g q u) -> p u g q", u=2, g=G)
            held = new_bank("held")
            planes = held[:].bitcast(BF16).rearrange("p (g t r) -> p g t r", g=2, t=PACK)
            by_t = wide[k].rearrange("p (g q t) -> p g t q", g=G, t=PACK)
            real_banks[j] = []
            for y in range(2):
                bank = new_bank("passing")
                for i in range(2):
                    for u in range(2):
                        col = (2 * u + i) * P
                        nc.tensor.transpose(bank[:, col : col + P], by_u[:, u, 2 * y + i], ident[:])
                real_banks[j].append(bank)
                for t in range(PACK):
                    nc.tensor.matmul(out=planes[:, y, t], lhsT=by_t[:, 2 * x + y, t], rhs=ident16[:], start=True, stop=True)
            turned[k] = turned.get(k, []) + [held]

        def scale_gen(k, order=(1, 0)):
            pair = k // 2
            if pair not in gen_grouped:
                gen_grouped[pair] = placed("gen_grouped%d" % pair, (88, 96, 88, 96, 48, 56)[pair], 2 * D, BF16)
            rows = gen_grouped[pair].rearrange("p (g r u e) -> p g r u e", r=P, u=2, e=2)
            for x in order:
                g0 = G * (k % 2) + 2 * x
                held = "p (g u e r) -> p g r u e" if k in BY_PRODUCT else "p (u g r e) -> p g r u e"
                values = turned[k][x][:].bitcast(BF16).rearrange(held, g=2, u=2, e=2)
                by_d = scale_cols[:, 2 * x : 2 * x + 2].rearrange("p g (u e) -> p g u e", u=2).unsqueeze(2).to_broadcast([P, 2, P, 2, 2])
                nc.vector.tensor_tensor(out=rows[:, g0 : g0 + 2], in0=values, in1=by_d, op=MULT)

        def turn_real(j):
            real_banks[j] = turn(real_tiles[j], "passing", False, WARM_REAL[j])

        def empty_real(j, which=(0, 1)):
            h = j // JT
            for x in which:
                if (h, x) not in real_grouped:
                    real_grouped[h, x] = placed("real_grouped%d%d" % (h, x), 32 + 16 * h + 8 * x, 2 * HN * PACK, BF16)
                words = real_grouped[h, x].bitcast(F32).rearrange("p (g r u) -> p g r u", g=2, u=2)
                on_scalar(out=words[:, :, j % JT * P : (j % JT + 1) * P], in_=real_banks[j][x][:].rearrange("p (u g r) -> p g r u", g=2, u=2))

        gcodes = {}

        def quant_gen(pair, parts=1):
            codes = work.tile([P, 2, G * P], U32, name="gcodes", bufs=4, align_bytes=MX_ALIGN)
            scales = work.tile([P, 2, G * P], U8, name="gscales", bufs=4, align_bytes=MX_ALIGN)
            for cols, values in zip(split(2 * G * P, parts), split(2 * D, parts)):
                nc.vector.quantize_mx(out=codes[:].rearrange("p i n -> p (i n)")[:, cols].bitcast(FP8X4),
                                      scales=scales[:].rearrange("p i n -> p (i n)")[:, cols], in_=gen_grouped[pair][:, values])
            for i in range(2):
                gcodes[2 * pair + i] = (codes[:, i], scales[:, i])

        def quant_real(h, x):
            passes = slice(2 * x, 2 * x + 2)
            nc.vector.quantize_mx(out=rcodes[:, h, passes].rearrange("p g n -> p (g n)").bitcast(FP8X4),
                                  scales=rscales[:, h, passes].rearrange("p g n -> p (g n)"), in_=real_grouped[h, x])

        factors = {}
        dot_banks = {}

        def dots(k, halves=range(H)):
            codes, scales = gcodes[k]
            for h in halves:
                dot_banks[k, h] = new_bank("passing")
            for g in range(G):
                m = slice(g * P, (g + 1) * P)
                for h in halves:
                    nc.tensor.matmul_mx(out=dot_banks[k, h][:], lhsT=codes[:, m].bitcast(FP8X4), lhsT_scale=scales[:, m],
                                        rhs=rcodes[:, h, g].bitcast(FP8X4), rhs_scale=rscales[:, h, g],
                                        start=(g == 0), stop=(g == G - 1))

        def dots_by_halves(tiles, h):
            for k in tiles:
                dot_banks[k, h] = new_bank("passing")
            for x in range(2):
                for k in tiles:
                    codes, scales = gcodes[k]
                    for g in (2 * x, 2 * x + 1):
                        m = slice(g * P, (g + 1) * P)
                        nc.tensor.matmul_mx(out=dot_banks[k, h][:], lhsT=codes[:, m].bitcast(FP8X4), lhsT_scale=scales[:, m],
                                            rhs=rcodes[:, h, g].bitcast(FP8X4), rhs_scale=rscales[:, h, g],
                                            start=(g == 0), stop=(g == G - 1))
            for k in tiles:
                factor(k, [h])

        def factor(k, halves=range(H)):
            c, t = k // PACK, k % PACK
            weight = imp32[:, k : k + 1]
            for h in halves:
                if (c, h) not in factors:
                    kib = ((104, 120), (136, 0), (16, 104))[c][h]
                    factors[c, h] = placed("factors%d%d" % (c, h), kib, 2 * PACK * HN, F32).rearrange("p (f t n) -> p f t n", f=2, t=PACK)
                nc.scalar.activation(out=factors[c, h][:, 0, t], in_=dot_banks[k, h][:], func=SQUARE, bias=one[:])
                nc.scalar.activation(out=factors[c, h][:, 1, t], in_=dot_banks[k, h][:], func=IDENTITY, scale=weight, bias=weight)

        def inner(k, halves=range(H)):
            dots(k, halves)
            factor(k, halves)

        ker = {}
        kcodes = {}

        def multiply(engine, c, h, cols, run):
            both = factors[c, h]
            engine.tensor_tensor(out=ker[c, h][:, cols].rearrange("p (n i) t -> p n t i", i=run),
                                 in0=both[:, 0, :, cols].rearrange("p t (n i) -> p n t i", i=run),
                                 in1=both[:, 1, :, cols].rearrange("p t (n i) -> p n t i", i=run), op=MULT)

        def new_ker(c, h, kib):
            ker[c, h] = placed("ker%d%d" % (c, h), kib, HN * PACK, BF16).rearrange("p (n t) -> p n t", t=PACK)

        def product(c, h, parts=1):
            new_ker(c, h, (64, 68, 72)[2 * (c - 1) + h - 1])
            for cols in split(HN, parts):
                multiply(nc.vector, c, h, cols, 2)

        def product_aside(c, h, kib, share):
            new_ker(c, h, kib)
            multiply(nc.gpsimd, c, h, slice(0, share), 4)

        def quant_ker(c, h, parts=1):
            codes = work.tile([P, HN], U32, name="kcodes", bufs=C * H, align_bytes=MX_ALIGN)
            scales = work.tile([P, HN], U8, name="kscales", bufs=C * H, align_bytes=MX_ALIGN)
            for cols in split(HN, parts):
                nc.vector.quantize_mx(out=codes[:, cols].bitcast(FP8X4), scales=scales[:, cols],
                                      in_=ker[c, h][:, cols].rearrange("p n t -> p (n t)"))
            kcodes[c, h] = (codes, scales)

        def quant_cols(c, h, cols):
            codes, scales = kcodes[c, h]
            nc.vector.quantize_mx(out=codes[:, cols].bitcast(FP8X4), scales=scales[:, cols], in_=ker[c, h][:, cols].rearrange("p n t -> p (n t)"))

        sums = {}

        def witness(part, blocks, chunks):
            h, cols, tag = part
            for b in blocks:
                if (h, cols.start, b) not in sums:
                    sums[h, cols.start, b] = new_bank(tag, cols.stop - cols.start)
                for c in chunks:
                    codes, scales = kcodes[c, h]
                    nc.tensor.matmul_mx(out=sums[h, cols.start, b][:], lhsT=wwords[:, c, 2 * P * b : 2 * P * (b + 1)].bitcast(FP4X4),
                                        lhsT_scale=wscales[:, c, P * b : P * (b + 1)],
                                        rhs=codes[:, cols].bitcast(FP8X4), rhs_scale=scales[:, cols],
                                        start=(c == 0), stop=(c == C - 1))

        def emit(part, b, copy, parts=1):
            h, cols, tag = part
            tile = placed("result%d%d%d" % (h, b, cols.start), (32, 40)[h] + 2 * b + cols.start * 4 // KIB, cols.stop - cols.start, F32)
            for some in split(cols.stop - cols.start, parts):
                copy(out=tile[:, some], in_=sums[h, cols.start, b][:, some])
                nc.sync.dma_start(out=out[b * P : (b + 1) * P, h * HN : (h + 1) * HN][:, cols][:, some], in_=tile[:, some])

        load_gen(0, 2)
        load_gen(1)
        nc.sync.dma_start(out=scale_cols[:], in_=gen_scale.rearrange("o (g p t) -> p (o g) t", p=P, t=PACK))
        load_gen(2)
        load_gen(3)
        load_gen_pair(2)
        for j in range(3):
            load_real(j)
        load_gen(6)
        load_real(3)
        for k in range(PACK):
            wide_run(k, 1, 64 + 4 * k)
        widen(0, on_vector, on_scalar, on_vector, on_scalar)
        widen(1, on_vector, on_scalar)
        load_real(4)
        load_real(5)
        load_gen(7)
        load_real(6)
        load_real(7)
        widen(2, on_scalar, on_scalar)
        widen(3, on_scalar, on_scalar)
        wide_run(4, 1, 80)
        wide_run(5, 1, 84)
        widen(4, on_scalar)
        widen(5, on_gpsimd)
        load_gen_pair(4)
        nc.sync.dma_start(out=imp_raw[:], in_=imp.rearrange("(c p t) -> p c t", p=P, t=PACK))
        load_gen_pair(5)
        load_mult()
        for k in range(PACK):
            turn_gen(k)
        for k in range(3):
            scale_gen(k, (0, 1))
            turn_real(k)
            empty_real(k)
        first_run = wide_run(6, 3, 64)
        widen(6, on_gpsimd)
        turn_gen_by_product(4, 0)
        scale_gen(3, (0, 1))
        for j in (3, 4):
            turn_real(j)
            empty_real(j)
        turn_gen_by_product(4, 1)
        widen(7, on_scalar)
        turn_real(5)
        empty_real(5)
        turn_gen_by_product(5, 0)
        quant_gen(0)
        quant_real(0, 0)
        quant_real(0, 1)
        turn_real(6)
        empty_real(6)
        turn_gen_by_product(5, 1)
        widen(8, on_scalar)
        sort_aside(first_run, 6, 2, 40)
        sort_aside(first_run[:, 2 * D :], 8, 1, 36)
        wide_run(9, 1, 76)
        quant_gen(1)
        scale_gen(4, (0, 1))
        scale_gen(5, (0, 1))
        nc.scalar.activation(out=imp32[:], in_=imp_raw[:].rearrange("p c t -> p (c t)"), func=IDENTITY)
        turn_real(7)
        empty_real(7)
        for t in range(3):
            inner(t, [0])
        turn_gen(6)
        inner(3, [0])
        quant_real(1, 0)
        quant_real(1, 1)
        quant_gen(2)
        wide_run(10, 2, 80)
        product_aside(0, 0, 88, 416)
        turn_gen(7)
        widen(9, on_scalar)
        scale_gen(6)
        scale_gen(7)
        for k, h in ((0, 1), (1, 1), (2, 1), (3, 1), (4, 0)):
            inner(k, [h])
        multiply(nc.vector, 0, 0, slice(416, HN), 2)
        quant_gen(3)
        product_aside(0, 1, 96, SHARE)
        turn_gen(8)
        widen(10, on_scalar)
        inner(5, [0])
        turn_gen(9)
        widen(11, on_scalar)
        scale_gen(8)
        scale_gen(9)
        for k, h in ((6, 0), (7, 0), (4, 1)):
            inner(k, [h])
        multiply(nc.vector, 0, 1, slice(SHARE, HN), 2)
        quant_gen(4)
        product_aside(1, 0, 48, SHARE)
        turn_gen(10)
        inner(5, [1])
        turn_gen(11)
        scale_gen(10)
        scale_gen(11)
        for k, h in ((6, 1), (7, 1), (8, 0), (9, 0), (8, 1)):
            inner(k, [h])
        multiply(nc.vector, 1, 0, slice(SHARE, HN), 2)
        quant_gen(5)
        last = C - 1
        first, second = (0, slice(0, HN), "held"), (1, slice(0, HN), "passing")
        product(1, 1)
        for c, h in ((0, 0), (1, 0), (0, 1), (1, 1)):
            quant_ker(c, h)
        for k, h in ((10, 0), (11, 0), (9, 1), (10, 1), (11, 1)):
            inner(k, [h])
        product(last, 0, 2)
        witness(first, range(3), range(last))
        quant_ker(last, 0, 2)
        witness(first, range(3), [last])
        witness(first, range(3, B), range(C))
        product(last, 1, 2)
        for b in range(B):
            emit(first, b, on_scalar)
        witness(second, range(B - 1), range(last))
        quant_ker(last, 1, 2)
        for b in range(B):
            witness(second, [b], [last] if b < B - 1 else range(C))
            emit(second, b, on_vector if b % 2 else on_scalar, 2 if b in (0, B - 1) else 1)
